import numpy as np
import ml_dtypes


def mxq(x, axis, fmt="e4m3"):
    dtype, down = {"e4m3": (ml_dtypes.float8_e4m3fn, 7), "e5m2": (ml_dtypes.float8_e5m2, 14)}[fmt]
    v = np.moveaxis(np.asarray(x, np.float32).astype(ml_dtypes.bfloat16).astype(np.float64), axis, -1)
    blocks = v.reshape(v.shape[:-1] + (-1, 32))
    amax = np.abs(blocks).max(-1, keepdims=True)
    byte = np.maximum(np.where(amax > 0, np.frexp(amax)[1] - 1 + 127, 0) - down, 1)
    scale = np.exp2(byte - 127.0)
    codes = (blocks / scale).astype(np.float32).astype(dtype).astype(np.float64)
    return np.moveaxis((codes * scale).reshape(v.shape), -1, axis)


WIDE = False


def mx_kscale(k):
    if not WIDE:
        return np.ones(k)
    levels = np.array([18, -18])
    if k % 512:
        return np.exp2(np.random.permutation(np.resize(levels, k // 32))).repeat(32)
    a = np.empty((k // 512, 16))
    for p in range(k // 512):
        a[p, :8] = np.random.permutation(np.resize(levels, 8))
        for g in range(8):
            far = levels[np.abs(levels - a[p, g]) >= 10]
            a[p, g + 8] = far[np.random.randint(len(far))]
    return np.exp2(a.ravel()).repeat(32)


def f64(x):
    return np.asarray(x).astype(np.float64)


def striped(idx):
    return np.tile(np.asarray(idx).reshape(-1, 16).T, (8, 1)).astype(np.uint16)


def unstriped(offs):
    return offs[:16].T.reshape(-1).astype(np.int64)


def eight(idx):
    return np.concatenate([idx[h].reshape(-1, 16).T for h in range(8)]).astype(np.uint16)


def uneight(offs):
    return np.stack([offs[16 * h:16 * h + 16].T.reshape(-1) for h in range(8)]).astype(np.int64)


def setup_inputs():
    n = np.random.standard_normal
    uni = np.random.uniform
    place = np.stack([np.random.permutation(512) for _ in range(8)])
    f_d = mx_kscale(512)
    f_e = mx_kscale(512)
    return {
        "wo": (n((512, 512)) / np.sqrt(512) * f_e[:, None] * f_d[None, :]).astype(np.float32),
        "dyT": (n((512, 512)) / f_e[:, None]).astype(np.float32),
        "W": (n((512, 512)) / np.sqrt(512) / f_d[:, None]).astype(np.float32),
        "h": (1.0 / (1.0 + np.exp(-3.0 * n((512, 512))))).astype(np.float32),
        "offs": eight(place),
    }


def reference(wo, dyT, W, h, offs):
    place = uneight(offs)
    u = mxq(f64(wo), 0, "e4m3").T @ mxq(f64(dyT), 0, "e5m2")
    ui = np.concatenate([u[64 * run:64 * run + 64][:, place[run % 8]] for run in range(8)])
    dz = ui * f64(h) * (1.0 - f64(h))
    out = mxq(f64(W), 0, "e4m3").T @ mxq(dz, 0, "e5m2")
    return out

@@ -1,0 +1,159 @@
+from contextlib import ExitStack
+
+import concourse.mybir as mybir
+
+S = 512
+P = 128
+PACK = 4
+FLOPS = 2 * 2 * S * S * S
+
+F32 = mybir.dt.float32
+BF16 = mybir.dt.bfloat16
+U32 = mybir.dt.uint32
+U16 = mybir.dt.uint16
+U8 = mybir.dt.uint8
+E4 = mybir.dt.float8_e4m3fn_x4
+E5 = mybir.dt.float8_e5m2_x4
+ALU = mybir.AluOpType
+COPY = mybir.ActivationFunctionType.Copy
+
+WO_CHUNKS = ((0, 256), (256, 512))
+DY_CHUNKS = ((0, 256), (256, 384), (384, 512))
+TOKEN_CHUNKS = ((0, 256), (256, 384), (384, 512))
+
+
+def weave(copy, dst, src):
+    copy(dst.rearrange("p (c i) j -> p c j i", i=4), src.rearrange("p j (c i) -> p c j i", i=4))
+
+
+def tile_attend_ghsort_sig_kernel(tc, wo, dyT, W, h, offs, out):
+    nc = tc.nc
+    with ExitStack() as ctx:
+        keep = ctx.enter_context(tc.tile_pool(name="keep", bufs=1))
+        psum = ctx.enter_context(tc.psum_pool(name="psum", bufs=1))
+
+        wo_rows = wo.rearrange("(p j) c -> p j c", j=PACK)
+        dy_rows = dyT.rearrange("(p j) c -> p j c", j=PACK)
+        w_rows = W.rearrange("(p j) c -> p j c", j=PACK)
+        h_rows = h.rearrange("(p j) c -> p j c", j=PACK)
+
+        wo_raw = []
+        for n, (a, b) in enumerate(WO_CHUNKS):
+            t = keep.tile([P, PACK, b - a], F32, name="wo_raw%d" % n)
+            nc.sync.dma_start(out=t[:], in_=wo_rows[:, :, a:b])
+            wo_raw.append(t)
+        dy_raw = []
+        for n, (a, b) in enumerate(DY_CHUNKS):
+            t = keep.tile([P, PACK, b - a], F32, name="dy_raw%d" % n)
+            nc.sync.dma_start(out=t[:], in_=dy_rows[:, :, a:b])
+            dy_raw.append(t)
+        offsets = keep.tile([P, S // 16], U16, name="offsets")
+        nc.sync.dma_start(offsets[:], offs)
+        h_raw = []
+        for n in range(2):
+            t = keep.tile([P, 2, S], F32, name="h_raw%d" % n)
+            nc.sync.dma_start(out=t[:], in_=h_rows[:, 2 * n : 2 * n + 2, :])
+            h_raw.append(t)
+        w_raw = keep.tile([P, PACK, S], F32, name="w_raw")
+        nc.sync.dma_start(out=w_raw[:], in_=w_rows)
+
+        def vcopy(o, i):
+            nc.vector.tensor_copy(out=o, in_=i)
+
+        def scopy(o, i):
+            nc.scalar.copy(out=o, in_=i)
+
+        wo_bf = keep.tile([P, PACK, P, PACK], BF16, name="wo_bf", align_bytes=64)
+        for n, (a, b) in enumerate(WO_CHUNKS):
+            copy = scopy if n == 0 else vcopy
+            copy(
+                wo_bf[:, :, a // 4 : b // 4, :].rearrange("p t m j -> p m t j"),
+                wo_raw[n][:].rearrange("p j (m t) -> p m t j", t=PACK),
+            )
+        wo_codes = keep.tile([P, S], U32, name="wo_codes", align_bytes=64)
+        wo_scales = keep.tile([P, S], U8, name="wo_scales", align_bytes=64)
+        nc.vector.quantize_mx(
+            out=wo_codes[:].bitcast(E4), scales=wo_scales[:], in_=wo_bf[:].rearrange("p t m j -> p (t m j)")
+        )
+
+        dy_codes = keep.tile([P, S], U32, name="dy_codes", align_bytes=64)
+        dy_scales = keep.tile([P, S], U8, name="dy_scales", align_bytes=64)
+        dy_bf = [keep.tile([P, b - a, PACK], BF16, name="dy_bf%d" % n, align_bytes=64) for n, (a, b) in enumerate(DY_CHUNKS)]
+        weave(scopy, dy_bf[0][:, 0:128, :], dy_raw[0][:, :, 0:128])
+        weave(vcopy, dy_bf[0][:, 128:256, :], dy_raw[0][:, :, 128:256])
+        weave(scopy, dy_bf[1][:], dy_raw[1][:])
+        nc.vector.quantize_mx(
+            out=dy_codes[:, 0:256].bitcast(E5), scales=dy_scales[:, 0:256], in_=dy_bf[0][:].rearrange("p c j -> p (c j)")
+        )
+        weave(vcopy, dy_bf[2][:], dy_raw[2][:])
+        for n in (1, 2):
+            a, b = DY_CHUNKS[n]
+            nc.vector.quantize_mx(
+                out=dy_codes[:, a:b].bitcast(E5), scales=dy_scales[:, a:b], in_=dy_bf[n][:].rearrange("p c j -> p (c j)")
+            )
+
+        u = []
+        for t in range(PACK):
+            acc = psum.tile([P, S], F32, name="u_acc%d" % t)
+            nc.tensor.matmul_mx(
+                out=acc[:],
+                lhsT=wo_codes[:, P * t : P * (t + 1)].bitcast(E4),
+                lhsT_scale=wo_scales[:, P * t : P * (t + 1)],
+                rhs=dy_codes[:].bitcast(E5),
+                rhs_scale=dy_scales[:],
+                start=True,
+                stop=True,
+            )
+            ut = keep.tile([P, S], F32, name="u%d" % t)
+            nc.scalar.copy(out=ut[:], in_=acc[:])
+            u.append(ut)
+
+        slope = []
+        for t in range(PACK):
+            g = keep.tile([P, S], F32, name="slope%d" % t)
+            hv = h_raw[t // 2][:, t % 2, :]
+            nc.vector.scalar_tensor_tensor(out=g[:], in0=hv, scalar=1.0, in1=hv, op0=ALU.subtract, op1=ALU.mult)
+            slope.append(g)
+
+        dz_codes = keep.tile([P, S], U32, name="dz_codes", align_bytes=64)
+        dz_scales = keep.tile([P, S], U8, name="dz_scales", align_bytes=64)
+        dz_bf = []
+        for n, (a, b) in enumerate(TOKEN_CHUNKS):
+            prod = keep.tile([P, PACK, b - a], F32, name="prod%d" % n)
+            for t in range(PACK):
+                nc.vector.tensor_tensor(
+                    out=prod[:, t, :],
+                    in0=u[t][:].indirect(offsets[:, a // 16 : b // 16]),
+                    in1=slope[t][:, a:b],
+                    op=ALU.mult,
+                )
+            z = keep.tile([P, b - a, PACK], BF16, name="dz_bf%d" % n, align_bytes=64)
+            weave(lambda o, i: nc.scalar.activation(out=o, in_=i, func=COPY, scale=-1.0), z[:], prod[:])
+            dz_bf.append(z)
+            if n == 0:
+                w_bf = keep.tile([P, S, PACK], BF16, name="w_bf", align_bytes=64)
+                for q in range(2):
+                    weave(scopy, w_bf[:, 256 * q : 256 * (q + 1), :], w_raw[:, :, 256 * q : 256 * (q + 1)])
+
+        w_codes = keep.tile([P, S], U32, name="w_codes", align_bytes=64)
+        w_scales = keep.tile([P, S], U8, name="w_scales", align_bytes=64)
+        nc.vector.quantize_mx(out=w_codes[:].bitcast(E4), scales=w_scales[:], in_=w_bf[:].rearrange("p c j -> p (c j)"))
+        for n, (a, b) in enumerate(TOKEN_CHUNKS):
+            nc.vector.quantize_mx(
+                out=dz_codes[:, a:b].bitcast(E5), scales=dz_scales[:, a:b], in_=dz_bf[n][:].rearrange("p c j -> p (c j)")
+            )
+
+        for q in range(S // P):
+            acc = psum.tile([P, S], F32, name="out_acc%d" % q)
+            nc.tensor.matmul_mx(
+                out=acc[:],
+                lhsT=w_codes[:, P * q : P * (q + 1)].bitcast(E4),
+                lhsT_scale=w_scales[:, P * q : P * (q + 1)],
+                rhs=dz_codes[:].bitcast(E5),
+                rhs_scale=dz_scales[:],
+                start=True,
+                stop=True,
+            )
+            res = keep.tile([P, S], F32, name="res%d" % q)
+            (vcopy if q % 2 == 0 else scopy)(res[:], acc[:])
+            nc.sync.dma_start(out=out[P * q : P * (q + 1), :], in_=res[:])

@@ -17,8 +17,8 @@ E5 = mybir.dt.float8_e5m2_x4
 ALU = mybir.AluOpType
 COPY = mybir.ActivationFunctionType.Copy
 
-WO_CHUNKS = ((0, 256), (256, 512))
-DY_CHUNKS = ((0, 256), (256, 384), (384, 512))
+DY_SPLIT = 336
+H_LOADS = ((0, 1), (1, 2), (2, 4))
 TOKEN_CHUNKS = ((0, 256), (256, 384), (384, 512))
 
 
@@ -37,23 +37,18 @@ def tile_attend_ghsort_sig_kernel(tc, wo, dyT, W, h, offs, out):
         w_rows = W.rearrange("(p j) c -> p j c", j=PACK)
         h_rows = h.rearrange("(p j) c -> p j c", j=PACK)
 
-        wo_raw = []
-        for n, (a, b) in enumerate(WO_CHUNKS):
-            t = keep.tile([P, PACK, b - a], F32, name="wo_raw%d" % n)
-            nc.sync.dma_start(out=t[:], in_=wo_rows[:, :, a:b])
-            wo_raw.append(t)
-        dy_raw = []
-        for n, (a, b) in enumerate(DY_CHUNKS):
-            t = keep.tile([P, PACK, b - a], F32, name="dy_raw%d" % n)
-            nc.sync.dma_start(out=t[:], in_=dy_rows[:, :, a:b])
-            dy_raw.append(t)
+        dy_raw = keep.tile([P, PACK, S], F32, name="dy_raw")
+        nc.sync.dma_start(out=dy_raw[:], in_=dy_rows)
+        wo_raw = keep.tile([P, PACK, S], F32, name="wo_raw")
+        nc.sync.dma_start(out=wo_raw[:], in_=wo_rows)
         offsets = keep.tile([P, S // 16], U16, name="offsets")
-        nc.sync.dma_start(offsets[:], offs)
-        h_raw = []
-        for n in range(2):
-            t = keep.tile([P, 2, S], F32, name="h_raw%d" % n)
-            nc.sync.dma_start(out=t[:], in_=h_rows[:, 2 * n : 2 * n + 2, :])
-            h_raw.append(t)
+        h_plane = []
+        for n, (a, b) in enumerate(H_LOADS):
+            t = keep.tile([P, b - a, S], F32, name="h_raw%d" % n)
+            nc.sync.dma_start(out=t[:], in_=h_rows[:, a:b, :])
+            h_plane.extend(t[:, j, :] for j in range(b - a))
+            if n == 0:
+                nc.sync.dma_start(offsets[:], offs)
         w_raw = keep.tile([P, PACK, S], F32, name="w_raw")
         nc.sync.dma_start(out=w_raw[:], in_=w_rows)
 
@@ -63,33 +58,33 @@ def tile_attend_ghsort_sig_kernel(tc, wo, dyT, W, h, offs, out):
         def scopy(o, i):
             nc.scalar.copy(out=o, in_=i)
 
-        wo_bf = keep.tile([P, PACK, P, PACK], BF16, name="wo_bf", align_bytes=64)
-        for n, (a, b) in enumerate(WO_CHUNKS):
-            copy = scopy if n == 0 else vcopy
-            copy(
-                wo_bf[:, :, a // 4 : b // 4, :].rearrange("p t m j -> p m t j"),
-                wo_raw[n][:].rearrange("p j (m t) -> p m t j", t=PACK),
-            )
-        wo_codes = keep.tile([P, S], U32, name="wo_codes", align_bytes=64)
-        wo_scales = keep.tile([P, S], U8, name="wo_scales", align_bytes=64)
-        nc.vector.quantize_mx(
-            out=wo_codes[:].bitcast(E4), scales=wo_scales[:], in_=wo_bf[:].rearrange("p t m j -> p (t m j)")
-        )
-
         dy_codes = keep.tile([P, S], U32, name="dy_codes", align_bytes=64)
         dy_scales = keep.tile([P, S], U8, name="dy_scales", align_bytes=64)
-        dy_bf = [keep.tile([P, b - a, PACK], BF16, name="dy_bf%d" % n, align_bytes=64) for n, (a, b) in enumerate(DY_CHUNKS)]
-        weave(scopy, dy_bf[0][:, 0:128, :], dy_raw[0][:, :, 0:128])
-        weave(vcopy, dy_bf[0][:, 128:256, :], dy_raw[0][:, :, 128:256])
-        weave(scopy, dy_bf[1][:], dy_raw[1][:])
-        nc.vector.quantize_mx(
-            out=dy_codes[:, 0:256].bitcast(E5), scales=dy_scales[:, 0:256], in_=dy_bf[0][:].rearrange("p c j -> p (c j)")
-        )
-        weave(vcopy, dy_bf[2][:], dy_raw[2][:])
-        for n in (1, 2):
-            a, b = DY_CHUNKS[n]
+        dy_bf = keep.tile([P, S, PACK], BF16, name="dy_bf", align_bytes=64)
+        weave(vcopy, dy_bf[:, 0:DY_SPLIT, :], dy_raw[:, :, 0:DY_SPLIT])
+        weave(scopy, dy_bf[:, DY_SPLIT:S, :], dy_raw[:, :, DY_SPLIT:S])
+        nc.vector.quantize_mx(out=dy_codes[:].bitcast(E5), scales=dy_scales[:], in_=dy_bf[:].rearrange("p c j -> p (c j)"))
+
+        slope = []
+
+        def make_slope(t):
+            g = keep.tile([P, S], F32, name="slope%d" % t)
+            nc.vector.scalar_tensor_tensor(
+                out=g[:], in0=h_plane[t], scalar=1.0, in1=h_plane[t], op0=ALU.subtract, op1=ALU.mult
+            )
+            slope.append(g)
+
+        wo_codes = keep.tile([P, S], U32, name="wo_codes", align_bytes=64)
+        wo_scales = keep.tile([P, S], U8, name="wo_scales", align_bytes=64)
+        wo_view = wo_raw[:].rearrange("p j (m t) -> p m t j", t=PACK)
+        for n, copy in enumerate((vcopy, scopy)):
+            wo_bf = keep.tile([P, 2, P, PACK], BF16, name="wo_bf%d" % n, align_bytes=64)
+            copy(wo_bf[:].rearrange("p t m j -> p m t j"), wo_view[:, :, 2 * n : 2 * n + 2, :])
+            make_slope(n)
             nc.vector.quantize_mx(
-                out=dy_codes[:, a:b].bitcast(E5), scales=dy_scales[:, a:b], in_=dy_bf[n][:].rearrange("p c j -> p (c j)")
+                out=wo_codes[:, 256 * n : 256 * (n + 1)].bitcast(E4),
+                scales=wo_scales[:, 256 * n : 256 * (n + 1)],
+                in_=wo_bf[:].rearrange("p t m j -> p (t m j)"),
             )
 
         u = []
@@ -108,12 +103,8 @@ def tile_attend_ghsort_sig_kernel(tc, wo, dyT, W, h, offs, out):
             nc.scalar.copy(out=ut[:], in_=acc[:])
             u.append(ut)
 
-        slope = []
-        for t in range(PACK):
-            g = keep.tile([P, S], F32, name="slope%d" % t)
-            hv = h_raw[t // 2][:, t % 2, :]
-            nc.vector.scalar_tensor_tensor(out=g[:], in0=hv, scalar=1.0, in1=hv, op0=ALU.subtract, op1=ALU.mult)
-            slope.append(g)
+        make_slope(2)
+        make_slope(3)
 
         dz_codes = keep.tile([P, S], U32, name="dz_codes", align_bytes=64)
         dz_scales = keep.tile([P, S], U8, name="dz_scales", align_bytes=64)

@@ -49,8 +49,11 @@ def tile_attend_ghsort_sig_kernel(tc, wo, dyT, W, h, offs, out):
             h_plane.extend(t[:, j, :] for j in range(b - a))
             if n == 0:
                 nc.sync.dma_start(offsets[:], offs)
-        w_raw = keep.tile([P, PACK, S], F32, name="w_raw")
-        nc.sync.dma_start(out=w_raw[:], in_=w_rows)
+        w_raw = []
+        for q in range(2):
+            t = keep.tile([P, PACK, S // 2], F32, name="w_raw%d" % q, tag="w_raw%d" % q, align_bytes=64)
+            nc.sync.dma_start(out=t[:], in_=w_rows[:, :, 256 * q : 256 * (q + 1)])
+            w_raw.append(t)
 
         def vcopy(o, i):
             nc.vector.tensor_copy(out=o, in_=i)
@@ -68,7 +71,7 @@ def tile_attend_ghsort_sig_kernel(tc, wo, dyT, W, h, offs, out):
         slope = []
 
         def make_slope(t):
-            g = keep.tile([P, S], F32, name="slope%d" % t)
+            g = keep.tile([P, S], F32, name="slope%d" % t, tag="slope%d" % t, align_bytes=64)
             nc.vector.scalar_tensor_tensor(
                 out=g[:], in0=h_plane[t], scalar=1.0, in1=h_plane[t], op0=ALU.subtract, op1=ALU.mult
             )
@@ -106,6 +109,10 @@ def tile_attend_ghsort_sig_kernel(tc, wo, dyT, W, h, offs, out):
         make_slope(2)
         make_slope(3)
 
+        w_bf = keep.tile([P, S, PACK], BF16, name="w_bf", align_bytes=64)
+        for q in range(2):
+            weave(scopy, w_bf[:, 256 * q : 256 * (q + 1), :], w_raw[q][:])
+
         dz_codes = keep.tile([P, S], U32, name="dz_codes", align_bytes=64)
         dz_scales = keep.tile([P, S], U8, name="dz_scales", align_bytes=64)
         dz_bf = []
@@ -118,17 +125,22 @@ def tile_attend_ghsort_sig_kernel(tc, wo, dyT, W, h, offs, out):
                     in1=slope[t][:, a:b],
                     op=ALU.mult,
                 )
-            z = keep.tile([P, b - a, PACK], BF16, name="dz_bf%d" % n, align_bytes=64)
-            weave(lambda o, i: nc.scalar.activation(out=o, in_=i, func=COPY, scale=-1.0), z[:], prod[:])
+            z = keep.tile([P, b - a, PACK], BF16, name="dz_bf%d" % n, tag="w_raw1" if n == 0 else "dz_bf%d" % n, align_bytes=64)
+            if n < 2:
+                weave(lambda o, i: nc.scalar.activation(out=o, in_=i, func=COPY, scale=-1.0), z[:], prod[:])
+            else:
+                w_codes = keep.tile([P, S], U32, name="w_codes", tag="slope2", align_bytes=64)
+                w_scales = keep.tile([P, S], U8, name="w_scales", align_bytes=64)
+                nc.vector.quantize_mx(
+                    out=w_codes[:].bitcast(E4), scales=w_scales[:], in_=w_bf[:].rearrange("p c j -> p (c j)")
+                )
+                weave(
+                    lambda o, i: nc.vector.tensor_scalar(out=o, in0=i, scalar1=-1.0, scalar2=None, op0=ALU.mult),
+                    z[:],
+                    prod[:],
+                )
             dz_bf.append(z)
-            if n == 0:
-                w_bf = keep.tile([P, S, PACK], BF16, name="w_bf", align_bytes=64)
-                for q in range(2):
-                    weave(scopy, w_bf[:, 256 * q : 256 * (q + 1), :], w_raw[:, :, 256 * q : 256 * (q + 1)])
 
-        w_codes = keep.tile([P, S], U32, name="w_codes", align_bytes=64)
-        w_scales = keep.tile([P, S], U8, name="w_scales", align_bytes=64)
-        nc.vector.quantize_mx(out=w_codes[:].bitcast(E4), scales=w_scales[:], in_=w_bf[:].rearrange("p c j -> p (c j)"))
         for n, (a, b) in enumerate(TOKEN_CHUNKS):
             nc.vector.quantize_mx(
                 out=dz_codes[:, a:b].bitcast(E5), scales=dz_scales[:, a:b], in_=dz_bf[n][:].rearrange("p c j -> p (c j)")

@@ -37,16 +37,16 @@ def tile_attend_ghsort_sig_kernel(tc, wo, dyT, W, h, offs, out):
         w_rows = W.rearrange("(p j) c -> p j c", j=PACK)
         h_rows = h.rearrange("(p j) c -> p j c", j=PACK)
 
-        dy_raw = keep.tile([P, PACK, S], F32, name="dy_raw")
+        dy_raw = keep.tile([P, PACK, S], F32, name="dy_raw", tag="dy_raw", align_bytes=64)
         nc.sync.dma_start(out=dy_raw[:], in_=dy_rows)
-        wo_raw = keep.tile([P, PACK, S], F32, name="wo_raw")
+        wo_raw = keep.tile([P, PACK, S], F32, name="wo_raw", tag="wo_raw", align_bytes=64)
         nc.sync.dma_start(out=wo_raw[:], in_=wo_rows)
         offsets = keep.tile([P, S // 16], U16, name="offsets")
         h_plane = []
         for n, (a, b) in enumerate(H_LOADS):
             t = keep.tile([P, b - a, S], F32, name="h_raw%d" % n)
             nc.sync.dma_start(out=t[:], in_=h_rows[:, a:b, :])
-            h_plane.extend(t[:, j, :] for j in range(b - a))
+            h_plane.append(t)
             if n == 0:
                 nc.sync.dma_start(offsets[:], offs)
         w_raw = []
@@ -61,27 +61,28 @@ def tile_attend_ghsort_sig_kernel(tc, wo, dyT, W, h, offs, out):
         def scopy(o, i):
             nc.scalar.copy(out=o, in_=i)
 
-        dy_codes = keep.tile([P, S], U32, name="dy_codes", align_bytes=64)
+        dy_codes = keep.tile([P, S], U32, name="dy_codes", tag="dy_codes", align_bytes=64)
         dy_scales = keep.tile([P, S], U8, name="dy_scales", align_bytes=64)
-        dy_bf = keep.tile([P, S, PACK], BF16, name="dy_bf", align_bytes=64)
+        dy_bf = keep.tile([P, S, PACK], BF16, name="dy_bf", tag="dy_bf", align_bytes=64)
         weave(vcopy, dy_bf[:, 0:DY_SPLIT, :], dy_raw[:, :, 0:DY_SPLIT])
         weave(scopy, dy_bf[:, DY_SPLIT:S, :], dy_raw[:, :, DY_SPLIT:S])
         nc.vector.quantize_mx(out=dy_codes[:].bitcast(E5), scales=dy_scales[:], in_=dy_bf[:].rearrange("p c j -> p (c j)"))
 
         slope = []
 
-        def make_slope(t):
-            g = keep.tile([P, S], F32, name="slope%d" % t, tag="slope%d" % t, align_bytes=64)
+        def make_slope(n):
+            planes = H_LOADS[n][1] - H_LOADS[n][0]
+            g = keep.tile([P, planes, S], F32, name="slope%d" % n, tag=("dy_bf", "wo_raw", "dy_raw")[n], align_bytes=64)
             nc.vector.scalar_tensor_tensor(
-                out=g[:], in0=h_plane[t], scalar=1.0, in1=h_plane[t], op0=ALU.subtract, op1=ALU.mult
+                out=g[:], in0=h_plane[n][:], scalar=1.0, in1=h_plane[n][:], op0=ALU.subtract, op1=ALU.mult
             )
-            slope.append(g)
+            slope.extend(g[:, j, :] for j in range(planes))
 
         wo_codes = keep.tile([P, S], U32, name="wo_codes", align_bytes=64)
         wo_scales = keep.tile([P, S], U8, name="wo_scales", align_bytes=64)
         wo_view = wo_raw[:].rearrange("p j (m t) -> p m t j", t=PACK)
         for n, copy in enumerate((vcopy, scopy)):
-            wo_bf = keep.tile([P, 2, P, PACK], BF16, name="wo_bf%d" % n, align_bytes=64)
+            wo_bf = keep.tile([P, 2, P, PACK], BF16, name="wo_bf%d" % n, tag=("dy_raw", "wo_bf1")[n], align_bytes=64)
             copy(wo_bf[:].rearrange("p t m j -> p m t j"), wo_view[:, :, 2 * n : 2 * n + 2, :])
             make_slope(n)
             nc.vector.quantize_mx(
@@ -102,14 +103,13 @@ def tile_attend_ghsort_sig_kernel(tc, wo, dyT, W, h, offs, out):
                 start=True,
                 stop=True,
             )
-            ut = keep.tile([P, S], F32, name="u%d" % t)
+            ut = keep.tile([P, S], F32, name="u%d" % t, tag="u%d" % t, align_bytes=64)
             nc.scalar.copy(out=ut[:], in_=acc[:])
             u.append(ut)
 
         make_slope(2)
-        make_slope(3)
 
-        w_bf = keep.tile([P, S, PACK], BF16, name="w_bf", align_bytes=64)
+        w_bf = keep.tile([P, S, PACK], BF16, name="w_bf", tag="dy_codes", align_bytes=64)
         for q in range(2):
             weave(scopy, w_bf[:, 256 * q : 256 * (q + 1), :], w_raw[q][:])
 
@@ -126,21 +126,12 @@ def tile_attend_ghsort_sig_kernel(tc, wo, dyT, W, h, offs, out):
                     op=ALU.mult,
                 )
             z = keep.tile([P, b - a, PACK], BF16, name="dz_bf%d" % n, tag="w_raw1" if n == 0 else "dz_bf%d" % n, align_bytes=64)
-            if n < 2:
-                weave(lambda o, i: nc.scalar.activation(out=o, in_=i, func=COPY, scale=-1.0), z[:], prod[:])
-            else:
-                w_codes = keep.tile([P, S], U32, name="w_codes", tag="slope2", align_bytes=64)
-                w_scales = keep.tile([P, S], U8, name="w_scales", align_bytes=64)
-                nc.vector.quantize_mx(
-                    out=w_codes[:].bitcast(E4), scales=w_scales[:], in_=w_bf[:].rearrange("p c j -> p (c j)")
-                )
-                weave(
-                    lambda o, i: nc.vector.tensor_scalar(out=o, in0=i, scalar1=-1.0, scalar2=None, op0=ALU.mult),
-                    z[:],
-                    prod[:],
-                )
+            weave(lambda o, i: nc.scalar.activation(out=o, in_=i, func=COPY, scale=-1.0), z[:], prod[:])
             dz_bf.append(z)
 
+        w_codes = keep.tile([P, S], U32, name="w_codes", tag="u2", align_bytes=64)
+        w_scales = keep.tile([P, S], U8, name="w_scales", align_bytes=64)
+        nc.vector.quantize_mx(out=w_codes[:].bitcast(E4), scales=w_scales[:], in_=w_bf[:].rearrange("p c j -> p (c j)"))
         for n, (a, b) in enumerate(TOKEN_CHUNKS):
             nc.vector.quantize_mx(
                 out=dz_codes[:, a:b].bitcast(E5), scales=dz_scales[:, a:b], in_=dz_bf[n][:].rearrange("p c j -> p (c j)")

@@ -5,6 +5,7 @@ import concourse.mybir as mybir
 S = 512
 P = 128
 PACK = 4
+LIST_ROWS = 16
 FLOPS = 2 * 2 * S * S * S
 
 F32 = mybir.dt.float32
@@ -12,18 +13,20 @@ BF16 = mybir.dt.bfloat16
 U32 = mybir.dt.uint32
 U16 = mybir.dt.uint16
 U8 = mybir.dt.uint8
-E4 = mybir.dt.float8_e4m3fn_x4
-E5 = mybir.dt.float8_e5m2_x4
+E4M3 = mybir.dt.float8_e4m3fn_x4
+E5M2 = mybir.dt.float8_e5m2_x4
 ALU = mybir.AluOpType
 COPY = mybir.ActivationFunctionType.Copy
 
-DY_SPLIT = 336
+DY_ON_VECTOR = 336
 H_LOADS = ((0, 1), (1, 2), (2, 4))
-TOKEN_CHUNKS = ((0, 256), (256, 384), (384, 512))
+GATHER_RUNS = ((0, 384), (384, 512))
+TOKEN_PIECES = ((0, 256), (256, 384), (384, 512))
+LAST_RUN_ON_VECTOR = 96
 
 
-def weave(copy, dst, src):
-    copy(dst.rearrange("p (c i) j -> p c j i", i=4), src.rearrange("p j (c i) -> p c j i", i=4))
+def weave_views(dst, src):
+    return dst.rearrange("p (c n) j -> p c j n", n=4), src.rearrange("p j (c n) -> p c j n", n=4)
 
 
 def tile_attend_ghsort_sig_kernel(tc, wo, dyT, W, h, offs, out):
@@ -32,122 +35,123 @@ def tile_attend_ghsort_sig_kernel(tc, wo, dyT, W, h, offs, out):
         keep = ctx.enter_context(tc.tile_pool(name="keep", bufs=1))
         psum = ctx.enter_context(tc.psum_pool(name="psum", bufs=1))
 
-        wo_rows = wo.rearrange("(p j) c -> p j c", j=PACK)
-        dy_rows = dyT.rearrange("(p j) c -> p j c", j=PACK)
-        w_rows = W.rearrange("(p j) c -> p j c", j=PACK)
-        h_rows = h.rearrange("(p j) c -> p j c", j=PACK)
+        def sbuf(shape, dtype, name, reuse=None):
+            return keep.tile(shape, dtype, name=name, tag=reuse or name, align_bytes=64)
 
-        dy_raw = keep.tile([P, PACK, S], F32, name="dy_raw", tag="dy_raw", align_bytes=64)
-        nc.sync.dma_start(out=dy_raw[:], in_=dy_rows)
-        wo_raw = keep.tile([P, PACK, S], F32, name="wo_raw", tag="wo_raw", align_bytes=64)
-        nc.sync.dma_start(out=wo_raw[:], in_=wo_rows)
-        offsets = keep.tile([P, S // 16], U16, name="offsets")
-        h_plane = []
-        for n, (a, b) in enumerate(H_LOADS):
-            t = keep.tile([P, b - a, S], F32, name="h_raw%d" % n)
-            nc.sync.dma_start(out=t[:], in_=h_rows[:, a:b, :])
-            h_plane.append(t)
+        def quantise(codes, scales, woven, fmt):
+            nc.vector.quantize_mx(out=codes.bitcast(fmt), scales=scales, in_=woven)
+
+        def multiply(acc, e4m3_codes, e4m3_scales, e5m2_codes, e5m2_scales):
+            nc.tensor.matmul_mx(
+                out=acc,
+                lhsT=e4m3_codes.bitcast(E4M3),
+                lhsT_scale=e4m3_scales,
+                rhs=e5m2_codes.bitcast(E5M2),
+                rhs_scale=e5m2_scales,
+                start=True,
+                stop=True,
+            )
+
+        def rows(matrix):
+            return matrix.rearrange("(p j) c -> p j c", j=PACK)
+
+        dy_raw = sbuf([P, PACK, S], F32, "dy_raw")
+        nc.sync.dma_start(out=dy_raw[:], in_=rows(dyT))
+        wo_raw = sbuf([P, PACK, S], F32, "wo_raw")
+        nc.sync.dma_start(out=wo_raw[:], in_=rows(wo))
+        offsets = keep.tile([P, S // LIST_ROWS], U16, name="offsets")
+        h_raw = []
+        for n, (first, end) in enumerate(H_LOADS):
+            h_part = keep.tile([P, end - first, S], F32, name="h_raw%d" % n)
+            nc.sync.dma_start(out=h_part[:], in_=rows(h)[:, first:end, :])
+            h_raw.append(h_part)
             if n == 0:
                 nc.sync.dma_start(offsets[:], offs)
+        half = S // 2
         w_raw = []
-        for q in range(2):
-            t = keep.tile([P, PACK, S // 2], F32, name="w_raw%d" % q, tag="w_raw%d" % q, align_bytes=64)
-            nc.sync.dma_start(out=t[:], in_=w_rows[:, :, 256 * q : 256 * (q + 1)])
-            w_raw.append(t)
+        for n in range(2):
+            w_part = sbuf([P, PACK, half], F32, "w_raw%d" % n)
+            nc.sync.dma_start(out=w_part[:], in_=rows(W)[:, :, half * n : half * (n + 1)])
+            w_raw.append(w_part)
 
-        def vcopy(o, i):
-            nc.vector.tensor_copy(out=o, in_=i)
+        dy_codes = sbuf([P, S], U32, "dy_codes")
+        dy_scales = sbuf([P, S], U8, "dy_scales")
+        dy_bf = sbuf([P, S, PACK], BF16, "dy_bf")
+        nc.vector.tensor_copy(*weave_views(dy_bf[:, 0:DY_ON_VECTOR, :], dy_raw[:, :, 0:DY_ON_VECTOR]))
+        nc.scalar.copy(*weave_views(dy_bf[:, DY_ON_VECTOR:S, :], dy_raw[:, :, DY_ON_VECTOR:S]))
+        quantise(dy_codes[:], dy_scales[:], dy_bf[:].rearrange("p c j -> p (c j)"), E5M2)
 
-        def scopy(o, i):
-            nc.scalar.copy(out=o, in_=i)
+        neg_slope = []
 
-        dy_codes = keep.tile([P, S], U32, name="dy_codes", tag="dy_codes", align_bytes=64)
-        dy_scales = keep.tile([P, S], U8, name="dy_scales", align_bytes=64)
-        dy_bf = keep.tile([P, S, PACK], BF16, name="dy_bf", tag="dy_bf", align_bytes=64)
-        weave(vcopy, dy_bf[:, 0:DY_SPLIT, :], dy_raw[:, :, 0:DY_SPLIT])
-        weave(scopy, dy_bf[:, DY_SPLIT:S, :], dy_raw[:, :, DY_SPLIT:S])
-        nc.vector.quantize_mx(out=dy_codes[:].bitcast(E5), scales=dy_scales[:], in_=dy_bf[:].rearrange("p c j -> p (c j)"))
-
-        slope = []
-
-        def make_slope(n):
+        def make_neg_slope(n, reuse):
             planes = H_LOADS[n][1] - H_LOADS[n][0]
-            g = keep.tile([P, planes, S], F32, name="slope%d" % n, tag=("dy_bf", "wo_raw", "dy_raw")[n], align_bytes=64)
+            part = sbuf([P, planes, S], F32, "neg_slope%d" % n, reuse)
             nc.vector.scalar_tensor_tensor(
-                out=g[:], in0=h_plane[n][:], scalar=1.0, in1=h_plane[n][:], op0=ALU.subtract, op1=ALU.mult
+                out=part[:], in0=h_raw[n][:], scalar=1.0, in1=h_raw[n][:], op0=ALU.subtract, op1=ALU.mult
             )
-            slope.extend(g[:, j, :] for j in range(planes))
+            neg_slope.extend(part[:, t, :] for t in range(planes))
 
-        wo_codes = keep.tile([P, S], U32, name="wo_codes", align_bytes=64)
-        wo_scales = keep.tile([P, S], U8, name="wo_scales", align_bytes=64)
-        wo_view = wo_raw[:].rearrange("p j (m t) -> p m t j", t=PACK)
-        for n, copy in enumerate((vcopy, scopy)):
-            wo_bf = keep.tile([P, 2, P, PACK], BF16, name="wo_bf%d" % n, tag=("dy_raw", "wo_bf1")[n], align_bytes=64)
-            copy(wo_bf[:].rearrange("p t m j -> p m t j"), wo_view[:, :, 2 * n : 2 * n + 2, :])
-            make_slope(n)
-            nc.vector.quantize_mx(
-                out=wo_codes[:, 256 * n : 256 * (n + 1)].bitcast(E4),
-                scales=wo_scales[:, 256 * n : 256 * (n + 1)],
-                in_=wo_bf[:].rearrange("p t m j -> p (t m j)"),
-            )
+        wo_codes = sbuf([P, S], U32, "wo_codes")
+        wo_scales = sbuf([P, S], U8, "wo_scales")
+        wo_dealt = wo_raw[:].rearrange("p j (m t) -> p m t j", t=PACK)
+        wo_steps = ((nc.vector.tensor_copy, "dy_raw", "dy_bf"), (nc.scalar.copy, None, "wo_raw"))
+        for n, (copy, bf_reuse, slope_reuse) in enumerate(wo_steps):
+            wo_bf = sbuf([P, 2, P, PACK], BF16, "wo_bf%d" % n, bf_reuse)
+            copy(wo_bf[:].rearrange("p t m j -> p m t j"), wo_dealt[:, :, 2 * n : 2 * n + 2, :])
+            make_neg_slope(n, slope_reuse)
+            words = slice(half * n, half * (n + 1))
+            quantise(wo_codes[:, words], wo_scales[:, words], wo_bf[:].rearrange("p t m j -> p (t m j)"), E4M3)
 
         u = []
         for t in range(PACK):
-            acc = psum.tile([P, S], F32, name="u_acc%d" % t)
-            nc.tensor.matmul_mx(
-                out=acc[:],
-                lhsT=wo_codes[:, P * t : P * (t + 1)].bitcast(E4),
-                lhsT_scale=wo_scales[:, P * t : P * (t + 1)],
-                rhs=dy_codes[:].bitcast(E5),
-                rhs_scale=dy_scales[:],
-                start=True,
-                stop=True,
-            )
-            ut = keep.tile([P, S], F32, name="u%d" % t, tag="u%d" % t, align_bytes=64)
-            nc.scalar.copy(out=ut[:], in_=acc[:])
-            u.append(ut)
+            u_acc = psum.tile([P, S], F32, name="u_acc%d" % t)
+            words = slice(P * t, P * (t + 1))
+            multiply(u_acc[:], wo_codes[:, words], wo_scales[:, words], dy_codes[:], dy_scales[:])
+            u_plane = sbuf([P, S], F32, "u%d" % t)
+            nc.scalar.copy(out=u_plane[:], in_=u_acc[:])
+            u.append(u_plane)
 
-        make_slope(2)
+        make_neg_slope(2, "dy_raw")
 
-        w_bf = keep.tile([P, S, PACK], BF16, name="w_bf", tag="dy_codes", align_bytes=64)
-        for q in range(2):
-            weave(scopy, w_bf[:, 256 * q : 256 * (q + 1), :], w_raw[q][:])
+        w_bf = sbuf([P, S, PACK], BF16, "w_bf", "dy_codes")
+        for n in range(2):
+            nc.scalar.copy(*weave_views(w_bf[:, half * n : half * (n + 1), :], w_raw[n][:]))
 
-        dz_codes = keep.tile([P, S], U32, name="dz_codes", align_bytes=64)
-        dz_scales = keep.tile([P, S], U8, name="dz_scales", align_bytes=64)
+        dz_codes = sbuf([P, S], U32, "dz_codes")
+        dz_scales = sbuf([P, S], U8, "dz_scales")
         dz_bf = []
-        for n, (a, b) in enumerate(TOKEN_CHUNKS):
-            prod = keep.tile([P, PACK, b - a], F32, name="prod%d" % n)
+        for n, (run_first, run_end) in enumerate(GATHER_RUNS):
+            neg_dz = keep.tile([P, PACK, run_end - run_first], F32, name="neg_dz%d" % n)
             for t in range(PACK):
                 nc.vector.tensor_tensor(
-                    out=prod[:, t, :],
-                    in0=u[t][:].indirect(offsets[:, a // 16 : b // 16]),
-                    in1=slope[t][:, a:b],
+                    out=neg_dz[:, t, :],
+                    in0=u[t][:].indirect(offsets[:, run_first // LIST_ROWS : run_end // LIST_ROWS]),
+                    in1=neg_slope[t][:, run_first:run_end],
                     op=ALU.mult,
                 )
-            z = keep.tile([P, b - a, PACK], BF16, name="dz_bf%d" % n, tag="w_raw1" if n == 0 else "dz_bf%d" % n, align_bytes=64)
-            weave(lambda o, i: nc.scalar.activation(out=o, in_=i, func=COPY, scale=-1.0), z[:], prod[:])
-            dz_bf.append(z)
+            for first, end in TOKEN_PIECES:
+                if run_first <= first < run_end:
+                    tokens = end - first
+                    woven = sbuf([P, tokens, PACK], BF16, "dz_bf%d" % first, "w_raw1" if first == 0 else None)
+                    on_scalar = tokens - LAST_RUN_ON_VECTOR if end == S else tokens
+                    columns = slice(first - run_first, first - run_first + on_scalar)
+                    dst, src = weave_views(woven[:, 0:on_scalar, :], neg_dz[:, :, columns])
+                    nc.scalar.activation(out=dst, in_=src, func=COPY, scale=-1.0)
+                    dz_bf.append(woven)
 
-        w_codes = keep.tile([P, S], U32, name="w_codes", tag="u2", align_bytes=64)
-        w_scales = keep.tile([P, S], U8, name="w_scales", align_bytes=64)
-        nc.vector.quantize_mx(out=w_codes[:].bitcast(E4), scales=w_scales[:], in_=w_bf[:].rearrange("p c j -> p (c j)"))
-        for n, (a, b) in enumerate(TOKEN_CHUNKS):
-            nc.vector.quantize_mx(
-                out=dz_codes[:, a:b].bitcast(E5), scales=dz_scales[:, a:b], in_=dz_bf[n][:].rearrange("p c j -> p (c j)")
-            )
+        w_codes = sbuf([P, S], U32, "w_codes", "u2")
+        w_scales = sbuf([P, S], U8, "w_scales")
+        quantise(w_codes[:], w_scales[:], w_bf[:].rearrange("p c j -> p (c j)"), E4M3)
+        dst, src = weave_views(woven[:, on_scalar:tokens, :], neg_dz[:, :, on_scalar:tokens])
+        nc.vector.tensor_scalar(out=dst, in0=src, scalar1=-1.0, scalar2=None, op0=ALU.mult)
+
+        for n, (first, end) in enumerate(TOKEN_PIECES):
+            quantise(dz_codes[:, first:end], dz_scales[:, first:end], dz_bf[n][:].rearrange("p c j -> p (c j)"), E5M2)
 
         for q in range(S // P):
-            acc = psum.tile([P, S], F32, name="out_acc%d" % q)
-            nc.tensor.matmul_mx(
-                out=acc[:],
-                lhsT=w_codes[:, P * q : P * (q + 1)].bitcast(E4),
-                lhsT_scale=w_scales[:, P * q : P * (q + 1)],
-                rhs=dz_codes[:].bitcast(E5),
-                rhs_scale=dz_scales[:],
-                start=True,
-                stop=True,
-            )
-            res = keep.tile([P, S], F32, name="res%d" % q)
-            (vcopy if q % 2 == 0 else scopy)(res[:], acc[:])
-            nc.sync.dma_start(out=out[P * q : P * (q + 1), :], in_=res[:])
+            out_acc = psum.tile([P, S], F32, name="out_acc%d" % q)
+            words = slice(P * q, P * (q + 1))
+            multiply(out_acc[:], w_codes[:, words], w_scales[:, words], dz_codes[:], dz_scales[:])
+            result = keep.tile([P, S], F32, name="result%d" % q)
+            (nc.vector.tensor_copy if q % 2 == 0 else nc.scalar.copy)(result[:], out_acc[:])
+            nc.sync.dma_start(out=out[words, :], in_=result[:])

@@ -20,9 +20,6 @@ COPY = mybir.ActivationFunctionType.Copy
 
 DY_ON_VECTOR = 336
 H_LOADS = ((0, 1), (1, 2), (2, 4))
-GATHER_RUNS = ((0, 384), (384, 512))
-TOKEN_PIECES = ((0, 256), (256, 384), (384, 512))
-LAST_RUN_ON_VECTOR = 96
 
 
 def weave_views(dst, src):
@@ -69,17 +66,19 @@ def tile_attend_ghsort_sig_kernel(tc, wo, dyT, W, h, offs, out):
                 nc.sync.dma_start(offsets[:], offs)
         half = S // 2
         w_raw = []
-        for n in range(2):
-            w_part = sbuf([P, PACK, half], F32, "w_raw%d" % n)
-            nc.sync.dma_start(out=w_part[:], in_=rows(W)[:, :, half * n : half * (n + 1)])
+        stage = sbuf([P, 4 * S], F32, "stage")
+        w_second = sbuf([P, 2 * S], F32, "w_raw1")
+        for n, flat in enumerate((stage[:, 0 : 2 * S], w_second[:])):
+            w_part = flat.rearrange("p (j c) -> p j c", j=PACK)
+            nc.sync.dma_start(out=w_part, in_=rows(W)[:, :, half * n : half * (n + 1)])
             w_raw.append(w_part)
 
-        dy_codes = sbuf([P, S], U32, "dy_codes")
-        dy_scales = sbuf([P, S], U8, "dy_scales")
+        grad_codes = sbuf([P, 2 * S], U32, "grad_codes")
+        grad_scales = sbuf([P, 2 * S], U8, "grad_scales")
         dy_bf = sbuf([P, S, PACK], BF16, "dy_bf")
         nc.vector.tensor_copy(*weave_views(dy_bf[:, 0:DY_ON_VECTOR, :], dy_raw[:, :, 0:DY_ON_VECTOR]))
         nc.scalar.copy(*weave_views(dy_bf[:, DY_ON_VECTOR:S, :], dy_raw[:, :, DY_ON_VECTOR:S]))
-        quantise(dy_codes[:], dy_scales[:], dy_bf[:].rearrange("p c j -> p (c j)"), E5M2)
+        quantise(grad_codes[:, 0:S], grad_scales[:, 0:S], dy_bf[:].rearrange("p c j -> p (c j)"), E5M2)
 
         neg_slope = []
 
@@ -106,52 +105,80 @@ def tile_attend_ghsort_sig_kernel(tc, wo, dyT, W, h, offs, out):
         for t in range(PACK):
             u_acc = psum.tile([P, S], F32, name="u_acc%d" % t)
             words = slice(P * t, P * (t + 1))
-            multiply(u_acc[:], wo_codes[:, words], wo_scales[:, words], dy_codes[:], dy_scales[:])
+            multiply(u_acc[:], wo_codes[:, words], wo_scales[:, words], grad_codes[:, 0:S], grad_scales[:, 0:S])
             u_plane = sbuf([P, S], F32, "u%d" % t)
             nc.scalar.copy(out=u_plane[:], in_=u_acc[:])
             u.append(u_plane)
 
         make_neg_slope(2, "dy_raw")
 
-        w_bf = sbuf([P, S, PACK], BF16, "w_bf", "dy_codes")
-        for n in range(2):
-            nc.scalar.copy(*weave_views(w_bf[:, half * n : half * (n + 1), :], w_raw[n][:]))
+        w_bf = sbuf([P, S, PACK], BF16, "w_bf", "wo_codes")
 
-        dz_codes = sbuf([P, S], U32, "dz_codes")
-        dz_scales = sbuf([P, S], U8, "dz_scales")
-        dz_bf = []
-        for n, (run_first, run_end) in enumerate(GATHER_RUNS):
-            neg_dz = keep.tile([P, PACK, run_end - run_first], F32, name="neg_dz%d" % n)
-            for t in range(PACK):
-                nc.vector.tensor_tensor(
-                    out=neg_dz[:, t, :],
-                    in0=u[t][:].indirect(offsets[:, run_first // LIST_ROWS : run_end // LIST_ROWS]),
-                    in1=neg_slope[t][:, run_first:run_end],
-                    op=ALU.mult,
-                )
-            for first, end in TOKEN_PIECES:
-                if run_first <= first < run_end:
-                    tokens = end - first
-                    woven = sbuf([P, tokens, PACK], BF16, "dz_bf%d" % first, "w_raw1" if first == 0 else None)
-                    on_scalar = tokens - LAST_RUN_ON_VECTOR if end == S else tokens
-                    columns = slice(first - run_first, first - run_first + on_scalar)
-                    dst, src = weave_views(woven[:, 0:on_scalar, :], neg_dz[:, :, columns])
-                    nc.scalar.activation(out=dst, in_=src, func=COPY, scale=-1.0)
-                    dz_bf.append(woven)
+        def weave_w(n):
+            nc.scalar.copy(*weave_views(w_bf[:, half * n : half * (n + 1), :], w_raw[n]))
 
-        w_codes = sbuf([P, S], U32, "w_codes", "u2")
-        w_scales = sbuf([P, S], U8, "w_scales")
-        quantise(w_codes[:], w_scales[:], w_bf[:].rearrange("p c j -> p (c j)"), E4M3)
-        dst, src = weave_views(woven[:, on_scalar:tokens, :], neg_dz[:, :, on_scalar:tokens])
+        def quantise_w(first, end, reuse=None):
+            codes = sbuf([P, end - first], U32, "w_codes%d" % first, reuse)
+            scales = sbuf([P, end - first], U8, "w_scales%d" % first)
+            quantise(codes[:], scales[:], w_bf[:, first:end, :].rearrange("p c j -> p (c j)"), E4M3)
+            return [(codes[:, c : c + P], scales[:, c : c + P]) for c in range(0, end - first, P)]
+
+        def gather(dst, t, first, end):
+            nc.vector.tensor_tensor(
+                out=dst,
+                in0=u[t][:].indirect(offsets[:, first // LIST_ROWS : end // LIST_ROWS]),
+                in1=neg_slope[t][:, first:end],
+                op=ALU.mult,
+            )
+
+        def quantise_dz(first, end, woven):
+            words = slice(S + first, S + end)
+            quantise(grad_codes[:, words], grad_scales[:, words], woven[:].rearrange("p c j -> p (c j)"), E5M2)
+
+        def weave_dz_on_scalar(woven, planes):
+            dst, src = weave_views(woven[:], planes)
+            nc.scalar.activation(out=dst, in_=src, func=COPY, scale=-1.0)
+
+        weave_w(0)
+        early = stage[:, 2 * S : 4 * S].rearrange("p (j c) -> p j c", j=PACK)
+        late = stage[:, S : 3 * S].rearrange("p (j c) -> p j c", j=PACK)
+        for t in range(PACK):
+            gather(early[:, t, :], t, 0, half)
+        woven0 = sbuf([P, half, PACK], BF16, "dz_bf0")
+        weave_dz_on_scalar(woven0, early)
+        weave_w(1)
+        for t in range(2):
+            gather(late[:, t, :], t, half, S)
+        w_tiles = quantise_w(0, half)
+        quantise_dz(0, half, woven0)
+        gather(late[:, 2, :], 2, half, S)
+        gather(late[:, 3, 0:P], 3, half, half + P)
+        woven1 = sbuf([P, P, PACK], BF16, "dz_bf1")
+        weave_dz_on_scalar(woven1, late[:, :, 0:P])
+        gather(late[:, 3, P:half], 3, half + P, S)
+        w_tiles = w_tiles + quantise_w(half, half + P)
+        woven2 = sbuf([P, P, PACK], BF16, "dz_bf2", "w_raw1")
+        dst, src = weave_views(woven2[:], late[:, :, P:half])
         nc.vector.tensor_scalar(out=dst, in0=src, scalar1=-1.0, scalar2=None, op0=ALU.mult)
+        quantise_dz(half, half + P, woven1)
+        quantise_dz(half + P, S, woven2)
+        w_tiles = w_tiles + quantise_w(half + P, S, "dz_bf1")
 
-        for n, (first, end) in enumerate(TOKEN_PIECES):
-            quantise(dz_codes[:, first:end], dz_scales[:, first:end], dz_bf[n][:].rearrange("p c j -> p (c j)"), E5M2)
+        def product(q, tag, first_word, pieces, copy, staged=None):
+            acc = psum.tile([P, S], F32, name="acc_" + tag, tag=tag)
+            words = slice(first_word, first_word + S)
+            multiply(acc[:], w_tiles[q][0], w_tiles[q][1], grad_codes[:, words], grad_scales[:, words])
+            for first, end in pieces:
+                result = staged
+                if staged is None:
+                    result = keep.tile([P, end - first], F32, name="result%d_%d" % (q, first))
+                column = S + first - first_word
+                copy(result[:], acc[:, column : column + end - first])
+                nc.sync.dma_start(out=out[P * q : P * (q + 1), first:end], in_=result[:])
 
-        for q in range(S // P):
-            out_acc = psum.tile([P, S], F32, name="out_acc%d" % q)
-            words = slice(P * q, P * (q + 1))
-            multiply(out_acc[:], w_codes[:, words], w_scales[:, words], dz_codes[:], dz_scales[:])
-            result = keep.tile([P, S], F32, name="result%d" % q)
-            (nc.vector.tensor_copy if q % 2 == 0 else nc.scalar.copy)(result[:], out_acc[:])
-            nc.sync.dma_start(out=out[words, :], in_=result[:])
+        product(0, "out0", half, ((0, half),), nc.scalar.copy, stage[:, S - P : S + P])
+        product(1, "out1", half, ((0, half),), nc.scalar.copy, stage[:, S + P : S + 3 * P])
+        product(2, "out2", S, ((0, half), (half, S)), nc.vector.tensor_copy)
+        product(3, "out3", S, ((0, S),), nc.scalar.copy)
+        product(0, "u_acc0", S, ((half, S),), nc.vector.tensor_copy)
+        product(1, "u_acc1", S, ((half, S),), nc.scalar.copy)

@@ -141,17 +141,16 @@ def tile_attend_ghsort_sig_kernel(tc, wo, dyT, W, h, offs, out):
 
         weave_w(0)
         early = stage[:, 2 * S : 4 * S].rearrange("p (j c) -> p j c", j=PACK)
-        late = stage[:, S : 3 * S].rearrange("p (j c) -> p j c", j=PACK)
+        late = stage[:, half : half + 2 * S].rearrange("p (j c) -> p j c", j=PACK)
         for t in range(PACK):
             gather(early[:, t, :], t, 0, half)
         woven0 = sbuf([P, half, PACK], BF16, "dz_bf0")
         weave_dz_on_scalar(woven0, early)
         weave_w(1)
-        for t in range(2):
+        for t in range(PACK - 1):
             gather(late[:, t, :], t, half, S)
         w_tiles = quantise_w(0, half)
         quantise_dz(0, half, woven0)
-        gather(late[:, 2, :], 2, half, S)
         gather(late[:, 3, 0:P], 3, half, half + P)
         woven1 = sbuf([P, P, PACK], BF16, "dz_bf1")
         weave_dz_on_scalar(woven1, late[:, :, 0:P])
@@ -176,8 +175,8 @@ def tile_attend_ghsort_sig_kernel(tc, wo, dyT, W, h, offs, out):
                 copy(result[:], acc[:, column : column + end - first])
                 nc.sync.dma_start(out=out[P * q : P * (q + 1), first:end], in_=result[:])
 
-        product(0, "out0", half, ((0, half),), nc.scalar.copy, stage[:, S - P : S + P])
-        product(1, "out1", half, ((0, half),), nc.scalar.copy, stage[:, S + P : S + 3 * P])
+        product(0, "out0", half, ((0, half),), nc.scalar.copy, stage[:, half - P : half + P])
+        product(1, "out1", half, ((0, half),), nc.scalar.copy, stage[:, half + P : half + 3 * P])
         product(2, "out2", S, ((0, half), (half, S)), nc.vector.tensor_copy)
         product(3, "out3", S, ((0, S),), nc.scalar.copy)
         product(0, "u_acc0", S, ((half, S),), nc.vector.tensor_copy)

@@ -92,11 +92,11 @@ def tile_attend_ghsort_sig_kernel(tc, wo, dyT, W, h, offs, out):
 
         wo_codes = sbuf([P, S], U32, "wo_codes")
         wo_scales = sbuf([P, S], U8, "wo_scales")
-        wo_dealt = wo_raw[:].rearrange("p j (m t) -> p m t j", t=PACK)
+        wo_dealt = wo_raw[:].rearrange("p j (m t) -> p m j t", t=PACK)
         wo_steps = ((nc.vector.tensor_copy, "dy_raw", "dy_bf"), (nc.scalar.copy, None, "wo_raw"))
         for n, (copy, bf_reuse, slope_reuse) in enumerate(wo_steps):
             wo_bf = sbuf([P, 2, P, PACK], BF16, "wo_bf%d" % n, bf_reuse)
-            copy(wo_bf[:].rearrange("p t m j -> p m t j"), wo_dealt[:, :, 2 * n : 2 * n + 2, :])
+            copy(wo_bf[:].rearrange("p t m j -> p m j t"), wo_dealt[:, :, :, 2 * n : 2 * n + 2])
             make_neg_slope(n, slope_reuse)
             words = slice(half * n, half * (n + 1))
             quantise(wo_codes[:, words], wo_scales[:, words], wo_bf[:].rearrange("p t m j -> p (t m j)"), E4M3)
@@ -141,20 +141,21 @@ def tile_attend_ghsort_sig_kernel(tc, wo, dyT, W, h, offs, out):
 
         weave_w(0)
         early = stage[:, 2 * S : 4 * S].rearrange("p (j c) -> p j c", j=PACK)
-        late = stage[:, half : half + 2 * S].rearrange("p (j c) -> p j c", j=PACK)
+        late = stage[:, 3 * P : 3 * P + 2 * S].rearrange("p (j c) -> p j c", j=PACK)
         for t in range(PACK):
             gather(early[:, t, :], t, 0, half)
         woven0 = sbuf([P, half, PACK], BF16, "dz_bf0")
         weave_dz_on_scalar(woven0, early)
         weave_w(1)
-        for t in range(PACK - 1):
+        for t in range(2):
             gather(late[:, t, :], t, half, S)
+        gather(late[:, 2, 0:P], 2, half, half + P)
         w_tiles = quantise_w(0, half)
         quantise_dz(0, half, woven0)
-        gather(late[:, 3, 0:P], 3, half, half + P)
+        gather(late[:, 3, :], 3, half, S)
         woven1 = sbuf([P, P, PACK], BF16, "dz_bf1")
         weave_dz_on_scalar(woven1, late[:, :, 0:P])
-        gather(late[:, 3, P:half], 3, half + P, S)
+        gather(late[:, 2, P:half], 2, half + P, S)
         w_tiles = w_tiles + quantise_w(half, half + P)
         woven2 = sbuf([P, P, PACK], BF16, "dz_bf2", "w_raw1")
         dst, src = weave_views(woven2[:], late[:, :, P:half])
@@ -163,20 +164,18 @@ def tile_attend_ghsort_sig_kernel(tc, wo, dyT, W, h, offs, out):
         quantise_dz(half + P, S, woven2)
         w_tiles = w_tiles + quantise_w(half + P, S, "dz_bf1")
 
-        def product(q, tag, first_word, pieces, copy, staged=None):
+        def product(q, tag, first_word, pieces, copy):
             acc = psum.tile([P, S], F32, name="acc_" + tag, tag=tag)
             words = slice(first_word, first_word + S)
             multiply(acc[:], w_tiles[q][0], w_tiles[q][1], grad_codes[:, words], grad_scales[:, words])
             for first, end in pieces:
-                result = staged
-                if staged is None:
-                    result = keep.tile([P, end - first], F32, name="result%d_%d" % (q, first))
+                result = keep.tile([P, end - first], F32, name="result%d_%d" % (q, first))
                 column = S + first - first_word
                 copy(result[:], acc[:, column : column + end - first])
                 nc.sync.dma_start(out=out[P * q : P * (q + 1), first:end], in_=result[:])
 
-        product(0, "out0", half, ((0, half),), nc.scalar.copy, stage[:, half - P : half + P])
-        product(1, "out1", half, ((0, half),), nc.scalar.copy, stage[:, half + P : half + 3 * P])
+        product(0, "out0", half, ((0, half),), nc.scalar.copy)
+        product(1, "out1", half, ((0, half),), nc.scalar.copy)
         product(2, "out2", S, ((0, half), (half, S)), nc.vector.tensor_copy)
         product(3, "out3", S, ((0, S),), nc.scalar.copy)
         product(0, "u_acc0", S, ((half, S),), nc.vector.tensor_copy)

@@ -57,18 +57,20 @@ def tile_attend_ghsort_sig_kernel(tc, wo, dyT, W, h, offs, out):
         wo_raw = sbuf([P, PACK, S], F32, "wo_raw")
         nc.sync.dma_start(out=wo_raw[:], in_=rows(wo))
         offsets = keep.tile([P, S // LIST_ROWS], U16, name="offsets")
-        h_raw = []
+        h_all = keep.tile([P, PACK, S], F32, name="h_all")
         for n, (first, end) in enumerate(H_LOADS):
-            h_part = keep.tile([P, end - first, S], F32, name="h_raw%d" % n)
-            nc.sync.dma_start(out=h_part[:], in_=rows(h)[:, first:end, :])
-            h_raw.append(h_part)
+            nc.sync.dma_start(out=h_all[:, first:end, :], in_=rows(h)[:, first:end, :])
             if n == 0:
                 nc.sync.dma_start(offsets[:], offs)
         half = S // 2
         w_raw = []
-        stage = sbuf([P, 4 * S], F32, "stage")
+        stage = sbuf([P, 17 * P], F32, "stage")
+
+        def blocks(first, count):
+            return stage[:, P * first : P * (first + count)]
+
         w_second = sbuf([P, 2 * S], F32, "w_raw1")
-        for n, flat in enumerate((stage[:, 0 : 2 * S], w_second[:])):
+        for n, flat in enumerate((blocks(9, 8), w_second[:])):
             w_part = flat.rearrange("p (j c) -> p j c", j=PACK)
             nc.sync.dma_start(out=w_part, in_=rows(W)[:, :, half * n : half * (n + 1)])
             w_raw.append(w_part)
@@ -80,26 +82,25 @@ def tile_attend_ghsort_sig_kernel(tc, wo, dyT, W, h, offs, out):
         nc.scalar.copy(*weave_views(dy_bf[:, DY_ON_VECTOR:S, :], dy_raw[:, :, DY_ON_VECTOR:S]))
         quantise(grad_codes[:, 0:S], grad_scales[:, 0:S], dy_bf[:].rearrange("p c j -> p (c j)"), E5M2)
 
-        neg_slope = []
-
-        def make_neg_slope(n, reuse):
-            planes = H_LOADS[n][1] - H_LOADS[n][0]
-            part = sbuf([P, planes, S], F32, "neg_slope%d" % n, reuse)
-            nc.vector.scalar_tensor_tensor(
-                out=part[:], in0=h_raw[n][:], scalar=1.0, in1=h_raw[n][:], op0=ALU.subtract, op1=ALU.mult
-            )
-            neg_slope.extend(part[:, t, :] for t in range(planes))
+        def make_neg_slope(dst, planes):
+            part = h_all[:, planes, 0 : half + P]
+            nc.vector.scalar_tensor_tensor(out=dst[:, :, 0 : half + P], in0=part, scalar=1.0, in1=part, op0=ALU.subtract, op1=ALU.mult)
 
         wo_codes = sbuf([P, S], U32, "wo_codes")
         wo_scales = sbuf([P, S], U8, "wo_scales")
         wo_dealt = wo_raw[:].rearrange("p j (m t) -> p m j t", t=PACK)
-        wo_steps = ((nc.vector.tensor_copy, "dy_raw", "dy_bf"), (nc.scalar.copy, None, "wo_raw"))
-        for n, (copy, bf_reuse, slope_reuse) in enumerate(wo_steps):
-            wo_bf = sbuf([P, 2, P, PACK], BF16, "wo_bf%d" % n, bf_reuse)
-            copy(wo_bf[:].rearrange("p t m j -> p m j t"), wo_dealt[:, :, :, 2 * n : 2 * n + 2])
-            make_neg_slope(n, slope_reuse)
+        wo_bf = (sbuf([P, 2 * S], BF16, "wo_bf0", "dy_raw")[:], sbuf([P, 2 * S], BF16, "wo_bf1")[:])
+        neg_slope = []
+        slope_parts = []
+        for n, (copy, slope_reuse) in enumerate(((nc.vector.tensor_copy, "dy_bf"), (nc.scalar.copy, "wo_raw"))):
+            dst = wo_bf[n].rearrange("p (t m j) -> p m j t", t=2, j=PACK)
+            copy(dst, wo_dealt[:, :, :, 2 * n : 2 * n + 2])
+            slope = sbuf([P, 1, S], F32, "neg_slope%d" % n, slope_reuse)
+            make_neg_slope(slope[:], slice(n, n + 1))
+            slope_parts.append((slope[:], slice(n, n + 1)))
+            neg_slope.append(slope[:, 0, :])
             words = slice(half * n, half * (n + 1))
-            quantise(wo_codes[:, words], wo_scales[:, words], wo_bf[:].rearrange("p t m j -> p (t m j)"), E4M3)
+            quantise(wo_codes[:, words], wo_scales[:, words], wo_bf[n], E4M3)
 
         u = []
         for t in range(PACK):
@@ -110,12 +111,20 @@ def tile_attend_ghsort_sig_kernel(tc, wo, dyT, W, h, offs, out):
             nc.scalar.copy(out=u_plane[:], in_=u_acc[:])
             u.append(u_plane)
 
-        make_neg_slope(2, "dy_raw")
+        slopes23 = sbuf([P, 2, S], F32, "neg_slope2", "dy_raw")[:]
+        make_neg_slope(slopes23, slice(2, 4))
+        slope_parts.append((slopes23, slice(2, 4)))
+        neg_slope.extend(slopes23[:, t, :] for t in range(2))
+        for part, planes in slope_parts:
+            nc.scalar.activation(
+                out=part[:, :, half + P : S], in_=h_all[:, planes, half + P : S], func=COPY, scale=-1.0, bias=1.0
+            )
 
         w_bf = sbuf([P, S, PACK], BF16, "w_bf", "wo_codes")
 
-        def weave_w(n):
-            nc.scalar.copy(*weave_views(w_bf[:, half * n : half * (n + 1), :], w_raw[n]))
+        def weave_w(first, end):
+            n = first // half
+            nc.scalar.copy(*weave_views(w_bf[:, first:end, :], w_raw[n][:, :, first - half * n : end - half * n]))
 
         def quantise_w(first, end, reuse=None):
             codes = sbuf([P, end - first], U32, "w_codes%d" % first, reuse)
@@ -123,11 +132,11 @@ def tile_attend_ghsort_sig_kernel(tc, wo, dyT, W, h, offs, out):
             quantise(codes[:], scales[:], w_bf[:, first:end, :].rearrange("p c j -> p (c j)"), E4M3)
             return [(codes[:, c : c + P], scales[:, c : c + P]) for c in range(0, end - first, P)]
 
-        def gather(dst, t, first, end):
+        def gather(dst, t, first, end, factor):
             nc.vector.tensor_tensor(
                 out=dst,
                 in0=u[t][:].indirect(offsets[:, first // LIST_ROWS : end // LIST_ROWS]),
-                in1=neg_slope[t][:, first:end],
+                in1=factor,
                 op=ALU.mult,
             )
 
@@ -139,27 +148,31 @@ def tile_attend_ghsort_sig_kernel(tc, wo, dyT, W, h, offs, out):
             dst, src = weave_views(woven[:], planes)
             nc.scalar.activation(out=dst, in_=src, func=COPY, scale=-1.0)
 
-        weave_w(0)
-        early = stage[:, 2 * S : 4 * S].rearrange("p (j c) -> p j c", j=PACK)
-        late = stage[:, 3 * P : 3 * P + 2 * S].rearrange("p (j c) -> p j c", j=PACK)
+        weave_w(0, P)
+        weave_w(P, half)
+        early = blocks(0, 8).rearrange("p (j c) -> p j c", j=PACK)
+        late = blocks(6, 8).rearrange("p (j c) -> p j c", j=PACK)
         for t in range(PACK):
-            gather(early[:, t, :], t, 0, half)
+            gather(early[:, t, :], t, 0, half, neg_slope[t][:, 0:half])
         woven0 = sbuf([P, half, PACK], BF16, "dz_bf0")
         weave_dz_on_scalar(woven0, early)
-        weave_w(1)
-        for t in range(2):
-            gather(late[:, t, :], t, half, S)
-        gather(late[:, 2, 0:P], 2, half, half + P)
+        weave_w(half, S)
+        for t in range(1, PACK):
+            gather(late[:, t, :], t, half, S, neg_slope[t][:, half:S])
         w_tiles = quantise_w(0, half)
         quantise_dz(0, half, woven0)
-        gather(late[:, 3, :], 3, half, S)
+        gather(late[:, 0, 0:P], 0, half, half + P, neg_slope[0][:, half : half + P])
         woven1 = sbuf([P, P, PACK], BF16, "dz_bf1")
         weave_dz_on_scalar(woven1, late[:, :, 0:P])
-        gather(late[:, 2, P:half], 2, half + P, S)
+        gather(late[:, 0, P:half], 0, half + P, S, neg_slope[0][:, half + P : S])
         w_tiles = w_tiles + quantise_w(half, half + P)
         woven2 = sbuf([P, P, PACK], BF16, "dz_bf2", "w_raw1")
-        dst, src = weave_views(woven2[:], late[:, :, P:half])
-        nc.vector.tensor_scalar(out=dst, in0=src, scalar1=-1.0, scalar2=None, op0=ALU.mult)
+        nc.vector.tensor_tensor(
+            out=woven2[:].rearrange("p (c n) j -> p c j n", n=2),
+            in0=late[:, :, P:half].rearrange("p j (c n) -> p c j n", n=2),
+            in1=h_all[:, :, half + P : S].rearrange("p j (c n) -> p c j n", n=2),
+            op=ALU.mult,
+        )
         quantise_dz(half, half + P, woven1)
         quantise_dz(half + P, S, woven2)
         w_tiles = w_tiles + quantise_w(half + P, S, "dz_bf1")

@@ -19,7 +19,8 @@ ALU = mybir.AluOpType
 COPY = mybir.ActivationFunctionType.Copy
 
 DY_ON_VECTOR = 336
-H_LOADS = ((0, 1), (1, 2), (2, 4))
+H_LOADS = ((0, 1), (1, 2), (2, 3), (3, 4))
+WO_ON_VECTOR = 96
 
 
 def weave_views(dst, src):
@@ -60,8 +61,7 @@ def tile_attend_ghsort_sig_kernel(tc, wo, dyT, W, h, offs, out):
         h_all = keep.tile([P, PACK, S], F32, name="h_all")
         for n, (first, end) in enumerate(H_LOADS):
             nc.sync.dma_start(out=h_all[:, first:end, :], in_=rows(h)[:, first:end, :])
-            if n == 0:
-                nc.sync.dma_start(offsets[:], offs)
+        nc.sync.dma_start(offsets[:], offs)
         half = S // 2
         w_raw = []
         stage = sbuf([P, 17 * P], F32, "stage")
@@ -69,8 +69,8 @@ def tile_attend_ghsort_sig_kernel(tc, wo, dyT, W, h, offs, out):
         def blocks(first, count):
             return stage[:, P * first : P * (first + count)]
 
-        w_second = sbuf([P, 2 * S], F32, "w_raw1")
-        for n, flat in enumerate((blocks(9, 8), w_second[:])):
+        w_second = sbuf([P, P + 2 * S], F32, "w_raw1")
+        for n, flat in enumerate((blocks(9, 8), w_second[:, P : P + 2 * S])):
             w_part = flat.rearrange("p (j c) -> p j c", j=PACK)
             nc.sync.dma_start(out=w_part, in_=rows(W)[:, :, half * n : half * (n + 1)])
             w_raw.append(w_part)
@@ -82,25 +82,40 @@ def tile_attend_ghsort_sig_kernel(tc, wo, dyT, W, h, offs, out):
         nc.scalar.copy(*weave_views(dy_bf[:, DY_ON_VECTOR:S, :], dy_raw[:, :, DY_ON_VECTOR:S]))
         quantise(grad_codes[:, 0:S], grad_scales[:, 0:S], dy_bf[:].rearrange("p c j -> p (c j)"), E5M2)
 
-        def make_neg_slope(dst, planes):
-            part = h_all[:, planes, 0 : half + P]
-            nc.vector.scalar_tensor_tensor(out=dst[:, :, 0 : half + P], in0=part, scalar=1.0, in1=part, op0=ALU.subtract, op1=ALU.mult)
+        def make_neg_slope(t):
+            part = h_all[:, t, 0 : half + P]
+            nc.vector.scalar_tensor_tensor(out=part, in0=part, scalar=1.0, in1=part, op0=ALU.subtract, op1=ALU.mult)
 
         wo_codes = sbuf([P, S], U32, "wo_codes")
         wo_scales = sbuf([P, S], U8, "wo_scales")
         wo_dealt = wo_raw[:].rearrange("p j (m t) -> p m j t", t=PACK)
-        wo_bf = (sbuf([P, 2 * S], BF16, "wo_bf0", "dy_raw")[:], sbuf([P, 2 * S], BF16, "wo_bf1")[:])
-        neg_slope = []
-        slope_parts = []
-        for n, (copy, slope_reuse) in enumerate(((nc.vector.tensor_copy, "dy_bf"), (nc.scalar.copy, "wo_raw"))):
-            dst = wo_bf[n].rearrange("p (t m j) -> p m j t", t=2, j=PACK)
-            copy(dst, wo_dealt[:, :, :, 2 * n : 2 * n + 2])
-            slope = sbuf([P, 1, S], F32, "neg_slope%d" % n, slope_reuse)
-            make_neg_slope(slope[:], slice(n, n + 1))
-            slope_parts.append((slope[:], slice(n, n + 1)))
-            neg_slope.append(slope[:, 0, :])
-            words = slice(half * n, half * (n + 1))
-            quantise(wo_codes[:, words], wo_scales[:, words], wo_bf[n], E4M3)
+        shared = sbuf([P, 3 * half], F32, "shared", "dy_bf")
+        rest = shared[:, 0:S].rearrange("p (t c) -> p t c", t=PACK)
+        wo_bf = (sbuf([P, 2 * S], BF16, "wo_bf0", "dy_raw")[:], shared[:, half : 3 * half].bitcast(BF16))
+
+        def deal_wo(copy, pair, first, end):
+            dst = wo_bf[pair].rearrange("p (t m j) -> p m j t", t=2, j=PACK)
+            copy(dst[:, first:end], wo_dealt[:, first:end, :, 2 * pair : 2 * pair + 2])
+
+        def quantise_wo(pair):
+            words = slice(half * pair, half * (pair + 1))
+            quantise(wo_codes[:, words], wo_scales[:, words], wo_bf[pair], E4M3)
+
+        def make_rest(first, end):
+            nc.scalar.activation(
+                out=rest[:, first:end, :], in_=h_all[:, first:end, half + P : S], func=COPY, scale=-1.0, bias=1.0
+            )
+
+        deal_wo(nc.vector.tensor_copy, 0, 0, WO_ON_VECTOR)
+        deal_wo(nc.scalar.copy, 0, WO_ON_VECTOR, P)
+        deal_wo(nc.scalar.copy, 1, 0, P)
+        make_neg_slope(0)
+        quantise_wo(0)
+        make_neg_slope(1)
+        quantise_wo(1)
+        make_neg_slope(2)
+        make_neg_slope(3)
+        neg_slope = [h_all[:, t, :] for t in range(PACK)]
 
         u = []
         for t in range(PACK):
@@ -111,14 +126,7 @@ def tile_attend_ghsort_sig_kernel(tc, wo, dyT, W, h, offs, out):
             nc.scalar.copy(out=u_plane[:], in_=u_acc[:])
             u.append(u_plane)
 
-        slopes23 = sbuf([P, 2, S], F32, "neg_slope2", "dy_raw")[:]
-        make_neg_slope(slopes23, slice(2, 4))
-        slope_parts.append((slopes23, slice(2, 4)))
-        neg_slope.extend(slopes23[:, t, :] for t in range(2))
-        for part, planes in slope_parts:
-            nc.scalar.activation(
-                out=part[:, :, half + P : S], in_=h_all[:, planes, half + P : S], func=COPY, scale=-1.0, bias=1.0
-            )
+        make_rest(0, 2)
 
         w_bf = sbuf([P, S, PACK], BF16, "w_bf", "wo_codes")
 
@@ -142,7 +150,7 @@ def tile_attend_ghsort_sig_kernel(tc, wo, dyT, W, h, offs, out):
 
         def quantise_dz(first, end, woven):
             words = slice(S + first, S + end)
-            quantise(grad_codes[:, words], grad_scales[:, words], woven[:].rearrange("p c j -> p (c j)"), E5M2)
+            quantise(grad_codes[:, words], grad_scales[:, words], woven.rearrange("p c j -> p (c j)"), E5M2)
 
         def weave_dz_on_scalar(woven, planes):
             dst, src = weave_views(woven[:], planes)
@@ -154,26 +162,28 @@ def tile_attend_ghsort_sig_kernel(tc, wo, dyT, W, h, offs, out):
         late = blocks(6, 8).rearrange("p (j c) -> p j c", j=PACK)
         for t in range(PACK):
             gather(early[:, t, :], t, 0, half, neg_slope[t][:, 0:half])
+        make_rest(2, 4)
         woven0 = sbuf([P, half, PACK], BF16, "dz_bf0")
         weave_dz_on_scalar(woven0, early)
-        weave_w(half, S)
+        weave_w(half, half + P)
+        weave_w(half + P, S)
         for t in range(1, PACK):
             gather(late[:, t, :], t, half, S, neg_slope[t][:, half:S])
         w_tiles = quantise_w(0, half)
-        quantise_dz(0, half, woven0)
+        quantise_dz(0, half, woven0[:])
         gather(late[:, 0, 0:P], 0, half, half + P, neg_slope[0][:, half : half + P])
         woven1 = sbuf([P, P, PACK], BF16, "dz_bf1")
         weave_dz_on_scalar(woven1, late[:, :, 0:P])
         gather(late[:, 0, P:half], 0, half + P, S, neg_slope[0][:, half + P : S])
         w_tiles = w_tiles + quantise_w(half, half + P)
-        woven2 = sbuf([P, P, PACK], BF16, "dz_bf2", "w_raw1")
+        woven2 = w_second[:, 0:half].bitcast(BF16).rearrange("p (c j) -> p c j", j=PACK)
         nc.vector.tensor_tensor(
-            out=woven2[:].rearrange("p (c n) j -> p c j n", n=2),
+            out=woven2.rearrange("p (c n) j -> p c j n", n=2),
             in0=late[:, :, P:half].rearrange("p j (c n) -> p c j n", n=2),
-            in1=h_all[:, :, half + P : S].rearrange("p j (c n) -> p c j n", n=2),
+            in1=rest.rearrange("p j (c n) -> p c j n", n=2),
             op=ALU.mult,
         )
-        quantise_dz(half, half + P, woven1)
+        quantise_dz(half, half + P, woven1[:])
         quantise_dz(half + P, S, woven2)
         w_tiles = w_tiles + quantise_w(half + P, S, "dz_bf1")
 

@@ -169,8 +169,9 @@ def tile_attend_ghsort_sig_kernel(tc, wo, dyT, W, h, offs, out):
         weave_w(half + P, S)
         for t in range(1, PACK):
             gather(late[:, t, :], t, half, S, neg_slope[t][:, half:S])
-        w_tiles = quantise_w(0, half)
+        w_tiles = quantise_w(0, P)
         quantise_dz(0, half, woven0[:])
+        w_tiles = w_tiles + quantise_w(P, half, "dz_bf0")
         gather(late[:, 0, 0:P], 0, half, half + P, neg_slope[0][:, half : half + P])
         woven1 = sbuf([P, P, PACK], BF16, "dz_bf1")
         weave_dz_on_scalar(woven1, late[:, :, 0:P])

@@ -6,6 +6,9 @@ S = 512
 P = 128
 PACK = 4
 LIST_ROWS = 16
+HALF = S // 2
+MIDDLE = HALF
+LAST = HALF + P
 FLOPS = 2 * 2 * S * S * S
 
 F32 = mybir.dt.float32
@@ -19,12 +22,15 @@ ALU = mybir.AluOpType
 COPY = mybir.ActivationFunctionType.Copy
 
 DY_ON_VECTOR = 336
-H_LOADS = ((0, 1), (1, 2), (2, 3), (3, 4))
 WO_ON_VECTOR = 96
 
 
 def weave_views(dst, src):
     return dst.rearrange("p (c n) j -> p c j n", n=4), src.rearrange("p j (c n) -> p c j n", n=4)
+
+
+def as_planes(flat):
+    return flat.rearrange("p (j c) -> p j c", j=PACK)
 
 
 def tile_attend_ghsort_sig_kernel(tc, wo, dyT, W, h, offs, out):
@@ -58,22 +64,18 @@ def tile_attend_ghsort_sig_kernel(tc, wo, dyT, W, h, offs, out):
         wo_raw = sbuf([P, PACK, S], F32, "wo_raw")
         nc.sync.dma_start(out=wo_raw[:], in_=rows(wo))
         offsets = keep.tile([P, S // LIST_ROWS], U16, name="offsets")
-        h_all = keep.tile([P, PACK, S], F32, name="h_all")
-        for n, (first, end) in enumerate(H_LOADS):
-            nc.sync.dma_start(out=h_all[:, first:end, :], in_=rows(h)[:, first:end, :])
+        factor = keep.tile([P, PACK, S], F32, name="factor")
+        for t in range(PACK):
+            nc.sync.dma_start(out=factor[:, t : t + 1, :], in_=rows(h)[:, t : t + 1, :])
         nc.sync.dma_start(offsets[:], offs)
-        half = S // 2
-        w_raw = []
+
         stage = sbuf([P, 17 * P], F32, "stage")
-
-        def blocks(first, count):
-            return stage[:, P * first : P * (first + count)]
-
-        w_second = sbuf([P, P + 2 * S], F32, "w_raw1")
-        for n, flat in enumerate((blocks(9, 8), w_second[:, P : P + 2 * S])):
-            w_part = flat.rearrange("p (j c) -> p j c", j=PACK)
-            nc.sync.dma_start(out=w_part, in_=rows(W)[:, :, half * n : half * (n + 1)])
-            w_raw.append(w_part)
+        early = as_planes(stage[:, 0 : 8 * P])
+        later = as_planes(stage[:, 6 * P : 14 * P])
+        w_second = sbuf([P, P + 2 * S], F32, "w_second")
+        w_raw = (as_planes(stage[:, 9 * P : 17 * P]), as_planes(w_second[:, P : P + 2 * S]))
+        for n in range(2):
+            nc.sync.dma_start(out=w_raw[n], in_=rows(W)[:, :, HALF * n : HALF * (n + 1)])
 
         grad_codes = sbuf([P, 2 * S], U32, "grad_codes")
         grad_scales = sbuf([P, 2 * S], U8, "grad_scales")
@@ -83,39 +85,40 @@ def tile_attend_ghsort_sig_kernel(tc, wo, dyT, W, h, offs, out):
         quantise(grad_codes[:, 0:S], grad_scales[:, 0:S], dy_bf[:].rearrange("p c j -> p (c j)"), E5M2)
 
         def make_neg_slope(t):
-            part = h_all[:, t, 0 : half + P]
+            part = factor[:, t, 0:LAST]
             nc.vector.scalar_tensor_tensor(out=part, in0=part, scalar=1.0, in1=part, op0=ALU.subtract, op1=ALU.mult)
 
         wo_codes = sbuf([P, S], U32, "wo_codes")
         wo_scales = sbuf([P, S], U8, "wo_scales")
         wo_dealt = wo_raw[:].rearrange("p j (m t) -> p m j t", t=PACK)
-        shared = sbuf([P, 3 * half], F32, "shared", "dy_bf")
-        rest = shared[:, 0:S].rearrange("p (t c) -> p t c", t=PACK)
-        wo_bf = (sbuf([P, 2 * S], BF16, "wo_bf0", "dy_raw")[:], shared[:, half : 3 * half].bitcast(BF16))
+        shared = sbuf([P, 3 * HALF], F32, "shared", "dy_bf")
+        one_minus_h = as_planes(shared[:, 0:S])
+        wo_bf = (sbuf([P, 2 * S], BF16, "wo_bf0", "dy_raw")[:], shared[:, HALF : 3 * HALF].bitcast(BF16))
 
-        def deal_wo(copy, pair, first, end):
+        def weave_wo(copy, pair, first, end):
             dst = wo_bf[pair].rearrange("p (t m j) -> p m j t", t=2, j=PACK)
             copy(dst[:, first:end], wo_dealt[:, first:end, :, 2 * pair : 2 * pair + 2])
 
-        def quantise_wo(pair):
-            words = slice(half * pair, half * (pair + 1))
-            quantise(wo_codes[:, words], wo_scales[:, words], wo_bf[pair], E4M3)
+        def quantise_wo(first, end):
+            words = slice(P * first, P * end)
+            woven = wo_bf[first // 2][:, S * (first % 2) : S * (first % 2 + end - first)]
+            quantise(wo_codes[:, words], wo_scales[:, words], woven, E4M3)
 
-        def make_rest(first, end):
+        def make_one_minus_h(first, end):
             nc.scalar.activation(
-                out=rest[:, first:end, :], in_=h_all[:, first:end, half + P : S], func=COPY, scale=-1.0, bias=1.0
+                out=one_minus_h[:, first:end, :], in_=factor[:, first:end, LAST:S], func=COPY, scale=-1.0, bias=1.0
             )
 
-        deal_wo(nc.vector.tensor_copy, 0, 0, WO_ON_VECTOR)
-        deal_wo(nc.scalar.copy, 0, WO_ON_VECTOR, P)
-        deal_wo(nc.scalar.copy, 1, 0, P)
+        weave_wo(nc.vector.tensor_copy, 0, 0, WO_ON_VECTOR)
+        weave_wo(nc.scalar.copy, 0, WO_ON_VECTOR, P)
+        weave_wo(nc.scalar.copy, 1, 0, P)
         make_neg_slope(0)
-        quantise_wo(0)
+        quantise_wo(0, 1)
+        quantise_wo(1, 2)
         make_neg_slope(1)
-        quantise_wo(1)
+        quantise_wo(2, 4)
         make_neg_slope(2)
         make_neg_slope(3)
-        neg_slope = [h_all[:, t, :] for t in range(PACK)]
 
         u = []
         for t in range(PACK):
@@ -126,25 +129,25 @@ def tile_attend_ghsort_sig_kernel(tc, wo, dyT, W, h, offs, out):
             nc.scalar.copy(out=u_plane[:], in_=u_acc[:])
             u.append(u_plane)
 
-        make_rest(0, 2)
+        make_one_minus_h(0, 2)
 
         w_bf = sbuf([P, S, PACK], BF16, "w_bf", "wo_codes")
 
-        def weave_w(first, end):
-            n = first // half
-            nc.scalar.copy(*weave_views(w_bf[:, first:end, :], w_raw[n][:, :, first - half * n : end - half * n]))
+        def weave_w(q):
+            first = P * (q % 2)
+            nc.scalar.copy(*weave_views(w_bf[:, P * q : P * (q + 1), :], w_raw[q // 2][:, :, first : first + P]))
 
-        def quantise_w(first, end, reuse=None):
-            codes = sbuf([P, end - first], U32, "w_codes%d" % first, reuse)
-            scales = sbuf([P, end - first], U8, "w_scales%d" % first)
-            quantise(codes[:], scales[:], w_bf[:, first:end, :].rearrange("p c j -> p (c j)"), E4M3)
-            return [(codes[:, c : c + P], scales[:, c : c + P]) for c in range(0, end - first, P)]
+        def quantise_w(q, reuse=None):
+            codes = sbuf([P, P], U32, "w_codes%d" % q, reuse)
+            scales = sbuf([P, P], U8, "w_scales%d" % q)
+            quantise(codes[:], scales[:], w_bf[:, P * q : P * (q + 1), :].rearrange("p c j -> p (c j)"), E4M3)
+            return codes, scales
 
-        def gather(dst, t, first, end, factor):
+        def gather(dst, t, first, end):
             nc.vector.tensor_tensor(
                 out=dst,
                 in0=u[t][:].indirect(offsets[:, first // LIST_ROWS : end // LIST_ROWS]),
-                in1=factor,
+                in1=factor[:, t, first:end],
                 op=ALU.mult,
             )
 
@@ -153,54 +156,52 @@ def tile_attend_ghsort_sig_kernel(tc, wo, dyT, W, h, offs, out):
             quantise(grad_codes[:, words], grad_scales[:, words], woven.rearrange("p c j -> p (c j)"), E5M2)
 
         def weave_dz_on_scalar(woven, planes):
-            dst, src = weave_views(woven[:], planes)
+            dst, src = weave_views(woven, planes)
             nc.scalar.activation(out=dst, in_=src, func=COPY, scale=-1.0)
 
-        weave_w(0, P)
-        weave_w(P, half)
-        early = blocks(0, 8).rearrange("p (j c) -> p j c", j=PACK)
-        late = blocks(6, 8).rearrange("p (j c) -> p j c", j=PACK)
+        weave_w(0)
+        weave_w(1)
         for t in range(PACK):
-            gather(early[:, t, :], t, 0, half, neg_slope[t][:, 0:half])
-        make_rest(2, 4)
-        woven0 = sbuf([P, half, PACK], BF16, "dz_bf0")
-        weave_dz_on_scalar(woven0, early)
-        weave_w(half, half + P)
-        weave_w(half + P, S)
+            gather(early[:, t, :], t, 0, MIDDLE)
+        early_bf = sbuf([P, HALF, PACK], BF16, "early_bf")
+        weave_dz_on_scalar(early_bf[:], early)
+        weave_w(2)
+        make_one_minus_h(2, 4)
+        weave_w(3)
         for t in range(1, PACK):
-            gather(late[:, t, :], t, half, S, neg_slope[t][:, half:S])
-        w_tiles = quantise_w(0, P)
-        quantise_dz(0, half, woven0[:])
-        w_tiles = w_tiles + quantise_w(P, half, "dz_bf0")
-        gather(late[:, 0, 0:P], 0, half, half + P, neg_slope[0][:, half : half + P])
-        woven1 = sbuf([P, P, PACK], BF16, "dz_bf1")
-        weave_dz_on_scalar(woven1, late[:, :, 0:P])
-        gather(late[:, 0, P:half], 0, half + P, S, neg_slope[0][:, half + P : S])
-        w_tiles = w_tiles + quantise_w(half, half + P)
-        woven2 = w_second[:, 0:half].bitcast(BF16).rearrange("p (c j) -> p c j", j=PACK)
+            gather(later[:, t, :], t, MIDDLE, S)
+        w_tiles = [quantise_w(0)]
+        quantise_dz(0, MIDDLE, early_bf[:])
+        w_tiles.append(quantise_w(1, "early_bf"))
+        gather(later[:, 0, 0:P], 0, MIDDLE, LAST)
+        middle_bf = sbuf([P, P, PACK], BF16, "middle_bf")
+        weave_dz_on_scalar(middle_bf[:], later[:, :, 0:P])
+        gather(later[:, 0, P:HALF], 0, LAST, S)
+        w_tiles.append(quantise_w(2))
+        last_bf = w_second[:, 0:HALF].bitcast(BF16).rearrange("p (c j) -> p c j", j=PACK)
         nc.vector.tensor_tensor(
-            out=woven2.rearrange("p (c n) j -> p c j n", n=2),
-            in0=late[:, :, P:half].rearrange("p j (c n) -> p c j n", n=2),
-            in1=rest.rearrange("p j (c n) -> p c j n", n=2),
+            out=last_bf.rearrange("p (c n) j -> p c j n", n=2),
+            in0=later[:, :, P:HALF].rearrange("p j (c n) -> p c j n", n=2),
+            in1=one_minus_h.rearrange("p j (c n) -> p c j n", n=2),
             op=ALU.mult,
         )
-        quantise_dz(half, half + P, woven1[:])
-        quantise_dz(half + P, S, woven2)
-        w_tiles = w_tiles + quantise_w(half + P, S, "dz_bf1")
+        quantise_dz(MIDDLE, LAST, middle_bf[:])
+        quantise_dz(LAST, S, last_bf)
+        w_tiles.append(quantise_w(3, "middle_bf"))
 
-        def product(q, tag, first_word, pieces, copy):
-            acc = psum.tile([P, S], F32, name="acc_" + tag, tag=tag)
+        def product(q, bank, first_word, pieces, copy):
+            acc = psum.tile([P, S], F32, name="acc_" + bank, tag=bank)
             words = slice(first_word, first_word + S)
-            multiply(acc[:], w_tiles[q][0], w_tiles[q][1], grad_codes[:, words], grad_scales[:, words])
+            multiply(acc[:], w_tiles[q][0][:], w_tiles[q][1][:], grad_codes[:, words], grad_scales[:, words])
             for first, end in pieces:
                 result = keep.tile([P, end - first], F32, name="result%d_%d" % (q, first))
                 column = S + first - first_word
                 copy(result[:], acc[:, column : column + end - first])
                 nc.sync.dma_start(out=out[P * q : P * (q + 1), first:end], in_=result[:])
 
-        product(0, "out0", half, ((0, half),), nc.scalar.copy)
-        product(1, "out1", half, ((0, half),), nc.scalar.copy)
-        product(2, "out2", S, ((0, half), (half, S)), nc.vector.tensor_copy)
+        product(0, "out0", HALF, ((0, MIDDLE),), nc.scalar.copy)
+        product(1, "out1", HALF, ((0, MIDDLE),), nc.scalar.copy)
+        product(2, "out2", S, ((0, MIDDLE), (MIDDLE, S)), nc.vector.tensor_copy)
         product(3, "out3", S, ((0, S),), nc.scalar.copy)
-        product(0, "u_acc0", S, ((half, S),), nc.vector.tensor_copy)
-        product(1, "u_acc1", S, ((half, S),), nc.scalar.copy)
+        product(0, "u_acc0", S, ((MIDDLE, S),), nc.vector.tensor_copy)
+        product(1, "u_acc1", S, ((MIDDLE, S),), nc.scalar.copy)

@@ -22,7 +22,6 @@ ALU = mybir.AluOpType
 COPY = mybir.ActivationFunctionType.Copy
 
 DY_ON_VECTOR = 336
-WO_ON_VECTOR = 96
 
 
 def weave_views(dst, src):
@@ -61,12 +60,17 @@ def tile_attend_ghsort_sig_kernel(tc, wo, dyT, W, h, offs, out):
 
         dy_raw = sbuf([P, PACK, S], F32, "dy_raw")
         nc.sync.dma_start(out=dy_raw[:], in_=rows(dyT))
-        wo_raw = sbuf([P, PACK, S], F32, "wo_raw")
-        nc.sync.dma_start(out=wo_raw[:], in_=rows(wo))
+        wo_raw = []
+        for n in range(2):
+            wo_part = sbuf([P, 2, S], F32, "wo_raw%d" % n)
+            nc.sync.dma_start(out=wo_part[:], in_=rows(wo)[:, 2 * n : 2 * n + 2, :])
+            wo_raw.append(wo_part)
         offsets = keep.tile([P, S // LIST_ROWS], U16, name="offsets")
         factor = keep.tile([P, PACK, S], F32, name="factor")
-        for t in range(PACK):
-            nc.sync.dma_start(out=factor[:, t : t + 1, :], in_=rows(h)[:, t : t + 1, :])
+        factor_flat = factor[:].rearrange("p t c -> p (t c)")
+        h_flat = h.rearrange("(p j) c -> p (j c)", j=PACK)
+        for first, end in ((0, LAST), (LAST, 2 * S), (2 * S, 3 * S), (3 * S, 4 * S)):
+            nc.sync.dma_start(out=factor_flat[:, first:end], in_=h_flat[:, first:end])
         nc.sync.dma_start(offsets[:], offs)
 
         stage = sbuf([P, 17 * P], F32, "stage")
@@ -88,30 +92,30 @@ def tile_attend_ghsort_sig_kernel(tc, wo, dyT, W, h, offs, out):
             part = factor[:, t, 0:LAST]
             nc.vector.scalar_tensor_tensor(out=part, in0=part, scalar=1.0, in1=part, op0=ALU.subtract, op1=ALU.mult)
 
-        wo_codes = sbuf([P, S], U32, "wo_codes")
-        wo_scales = sbuf([P, S], U8, "wo_scales")
-        wo_dealt = wo_raw[:].rearrange("p j (m t) -> p m j t", t=PACK)
+        wo_codes = [sbuf([P, HALF], U32, "wo_codes0"), sbuf([P, HALF], U32, "wo_codes1", "wo_raw1")]
+        wo_scales = [sbuf([P, HALF], U8, "wo_scales%d" % pair) for pair in range(2)]
         shared = sbuf([P, 3 * HALF], F32, "shared", "dy_bf")
         one_minus_h = as_planes(shared[:, 0:S])
         wo_bf = (sbuf([P, 2 * S], BF16, "wo_bf0", "dy_raw")[:], shared[:, HALF : 3 * HALF].bitcast(BF16))
 
-        def weave_wo(copy, pair, first, end):
+        def weave_wo(copy, pair, n):
             dst = wo_bf[pair].rearrange("p (t m j) -> p m j t", t=2, j=PACK)
-            copy(dst[:, first:end], wo_dealt[:, first:end, :, 2 * pair : 2 * pair + 2])
+            src = wo_raw[n][:].rearrange("p j (m t) -> p m j t", t=PACK)
+            copy(dst[:, :, 2 * n : 2 * n + 2, :], src[:, :, :, 2 * pair : 2 * pair + 2])
 
         def quantise_wo(first, end):
-            words = slice(P * first, P * end)
+            words = slice(P * (first % 2), P * (first % 2 + end - first))
             woven = wo_bf[first // 2][:, S * (first % 2) : S * (first % 2 + end - first)]
-            quantise(wo_codes[:, words], wo_scales[:, words], woven, E4M3)
+            quantise(wo_codes[first // 2][:, words], wo_scales[first // 2][:, words], woven, E4M3)
 
         def make_one_minus_h(first, end):
             nc.scalar.activation(
                 out=one_minus_h[:, first:end, :], in_=factor[:, first:end, LAST:S], func=COPY, scale=-1.0, bias=1.0
             )
 
-        weave_wo(nc.vector.tensor_copy, 0, 0, WO_ON_VECTOR)
-        weave_wo(nc.scalar.copy, 0, WO_ON_VECTOR, P)
-        weave_wo(nc.scalar.copy, 1, 0, P)
+        for n in range(2):
+            weave_wo(nc.vector.tensor_copy, 0, n)
+            weave_wo(nc.scalar.copy, 1, n)
         make_neg_slope(0)
         quantise_wo(0, 1)
         quantise_wo(1, 2)
@@ -123,15 +127,15 @@ def tile_attend_ghsort_sig_kernel(tc, wo, dyT, W, h, offs, out):
         u = []
         for t in range(PACK):
             u_acc = psum.tile([P, S], F32, name="u_acc%d" % t)
-            words = slice(P * t, P * (t + 1))
-            multiply(u_acc[:], wo_codes[:, words], wo_scales[:, words], grad_codes[:, 0:S], grad_scales[:, 0:S])
+            words = slice(P * (t % 2), P * (t % 2 + 1))
+            multiply(u_acc[:], wo_codes[t // 2][:, words], wo_scales[t // 2][:, words], grad_codes[:, 0:S], grad_scales[:, 0:S])
             u_plane = sbuf([P, S], F32, "u%d" % t)
             nc.scalar.copy(out=u_plane[:], in_=u_acc[:])
             u.append(u_plane)
 
         make_one_minus_h(0, 2)
 
-        w_bf = sbuf([P, S, PACK], BF16, "w_bf", "wo_codes")
+        w_bf = sbuf([P, S, PACK], BF16, "w_bf", "wo_raw1")
 
         def weave_w(q):
             first = P * (q % 2)
@@ -189,19 +193,25 @@ def tile_attend_ghsort_sig_kernel(tc, wo, dyT, W, h, offs, out):
         quantise_dz(LAST, S, last_bf)
         w_tiles.append(quantise_w(3, "middle_bf"))
 
-        def product(q, bank, first_word, pieces, copy):
+        def product(q, bank, first_word):
             acc = psum.tile([P, S], F32, name="acc_" + bank, tag=bank)
             words = slice(first_word, first_word + S)
             multiply(acc[:], w_tiles[q][0][:], w_tiles[q][1][:], grad_codes[:, words], grad_scales[:, words])
+            return acc
+
+        early_result = keep.tile([P, 2, MIDDLE], F32, name="early_result")
+        for q in range(2):
+            nc.scalar.copy(early_result[:, q, :], product(q, "out%d" % q, HALF)[:, HALF:S])
+        nc.sync.dma_start(out=out[0:HALF, 0:MIDDLE].rearrange("(q p) c -> p q c", q=2), in_=early_result[:])
+
+        def close(q, bank, pieces, copy):
+            acc = product(q, bank, S)
             for first, end in pieces:
                 result = keep.tile([P, end - first], F32, name="result%d_%d" % (q, first))
-                column = S + first - first_word
-                copy(result[:], acc[:, column : column + end - first])
+                copy(result[:], acc[:, first:end])
                 nc.sync.dma_start(out=out[P * q : P * (q + 1), first:end], in_=result[:])
 
-        product(0, "out0", HALF, ((0, MIDDLE),), nc.scalar.copy)
-        product(1, "out1", HALF, ((0, MIDDLE),), nc.scalar.copy)
-        product(2, "out2", S, ((0, MIDDLE), (MIDDLE, S)), nc.vector.tensor_copy)
-        product(3, "out3", S, ((0, S),), nc.scalar.copy)
-        product(0, "u_acc0", S, ((MIDDLE, S),), nc.vector.tensor_copy)
-        product(1, "u_acc1", S, ((MIDDLE, S),), nc.scalar.copy)
+        close(2, "out2", ((0, MIDDLE), (MIDDLE, S)), nc.vector.tensor_copy)
+        close(3, "out3", ((0, S),), nc.scalar.copy)
+        close(0, "u_acc0", ((MIDDLE, S),), nc.vector.tensor_copy)
+        close(1, "u_acc1", ((MIDDLE, S),), nc.scalar.copy)

@@ -7,8 +7,6 @@ P = 128
 PACK = 4
 LIST_ROWS = 16
 HALF = S // 2
-MIDDLE = HALF
-LAST = HALF + P
 FLOPS = 2 * 2 * S * S * S
 
 F32 = mybir.dt.float32
@@ -21,7 +19,8 @@ E5M2 = mybir.dt.float8_e5m2_x4
 ALU = mybir.AluOpType
 COPY = mybir.ActivationFunctionType.Copy
 
-DY_ON_VECTOR = 336
+DY_ON_VECTOR = 168
+RUNS = ((0, 256), (256, 384), (384, 512))
 
 
 def weave_views(dst, src):
@@ -58,160 +57,173 @@ def tile_attend_ghsort_sig_kernel(tc, wo, dyT, W, h, offs, out):
         def rows(matrix):
             return matrix.rearrange("(p j) c -> p j c", j=PACK)
 
-        dy_raw = sbuf([P, PACK, S], F32, "dy_raw")
-        nc.sync.dma_start(out=dy_raw[:], in_=rows(dyT))
         wo_raw = []
         for n in range(2):
             wo_part = sbuf([P, 2, S], F32, "wo_raw%d" % n)
             nc.sync.dma_start(out=wo_part[:], in_=rows(wo)[:, 2 * n : 2 * n + 2, :])
             wo_raw.append(wo_part)
-        offsets = keep.tile([P, S // LIST_ROWS], U16, name="offsets")
-        factor = keep.tile([P, PACK, S], F32, name="factor")
-        factor_flat = factor[:].rearrange("p t c -> p (t c)")
-        h_flat = h.rearrange("(p j) c -> p (j c)", j=PACK)
-        for first, end in ((0, LAST), (LAST, 2 * S), (2 * S, 3 * S), (3 * S, 4 * S)):
-            nc.sync.dma_start(out=factor_flat[:, first:end], in_=h_flat[:, first:end])
-        nc.sync.dma_start(offsets[:], offs)
+        arena = sbuf([P, 3 * HALF + PACK * S], F32, "arena")
+        factor_halves = arena[:, 3 * HALF :].rearrange("p (n t c) -> p n t c", n=2, t=PACK)
 
-        stage = sbuf([P, 17 * P], F32, "stage")
-        early = as_planes(stage[:, 0 : 8 * P])
-        later = as_planes(stage[:, 6 * P : 14 * P])
-        w_second = sbuf([P, P + 2 * S], F32, "w_second")
-        w_raw = (as_planes(stage[:, 9 * P : 17 * P]), as_planes(w_second[:, P : P + 2 * S]))
+        def factor(planes, first, end):
+            if end - first == S:
+                return factor_halves[:, :, planes, :]
+            return factor_halves[:, first // HALF, planes, first % HALF : first % HALF + end - first]
+
+        def h_part(t, first, end):
+            if end - first == S:
+                return h_sb[:, t, :].rearrange("p (n c) -> p n c", n=2)
+            return h_sb[:, t, first:end]
+
+        dy_raw = (sbuf([P, PACK, HALF], F32, "dy_raw0")[:], as_planes(arena[:, 0 : 2 * S]))
         for n in range(2):
-            nc.sync.dma_start(out=w_raw[n], in_=rows(W)[:, :, HALF * n : HALF * (n + 1)])
+            nc.sync.dma_start(out=dy_raw[n], in_=rows(dyT)[:, :, HALF * n : HALF * (n + 1)])
+        offsets = keep.tile([P, S // LIST_ROWS], U16, name="offsets")
+        h_sb = keep.tile([P, PACK, S], F32, name="h_sb")
+        for t in (0, 2, 3, 1):
+            nc.sync.dma_start(out=h_sb[:, t, :], in_=rows(h)[:, t, :])
+        nc.sync.dma_start(offsets[:], offs)
+        w_raw = sbuf([P, PACK, S], F32, "w_raw")
+        nc.sync.dma_start(out=w_raw[:], in_=rows(W))
 
-        grad_codes = sbuf([P, 2 * S], U32, "grad_codes")
-        grad_scales = sbuf([P, 2 * S], U8, "grad_scales")
-        dy_bf = sbuf([P, S, PACK], BF16, "dy_bf")
-        nc.vector.tensor_copy(*weave_views(dy_bf[:, 0:DY_ON_VECTOR, :], dy_raw[:, :, 0:DY_ON_VECTOR]))
-        nc.scalar.copy(*weave_views(dy_bf[:, DY_ON_VECTOR:S, :], dy_raw[:, :, DY_ON_VECTOR:S]))
-        quantise(grad_codes[:, 0:S], grad_scales[:, 0:S], dy_bf[:].rearrange("p c j -> p (c j)"), E5M2)
+        def make_neg_slope(t, first, end):
+            part = h_part(t, first, end)
+            nc.vector.scalar_tensor_tensor(
+                out=factor(t, first, end), in0=part, scalar=1.0, in1=part, op0=ALU.subtract, op1=ALU.mult
+            )
 
-        def make_neg_slope(t):
-            part = factor[:, t, 0:LAST]
-            nc.vector.scalar_tensor_tensor(out=part, in0=part, scalar=1.0, in1=part, op0=ALU.subtract, op1=ALU.mult)
+        def make_one_minus_h(t, first, end):
+            nc.vector.tensor_scalar(
+                out=factor(t, first, end), in0=h_part(t, first, end), scalar1=-1.0, scalar2=1.0, op0=ALU.mult, op1=ALU.add
+            )
 
-        wo_codes = [sbuf([P, HALF], U32, "wo_codes0"), sbuf([P, HALF], U32, "wo_codes1", "wo_raw1")]
+        wo_codes = [sbuf([P, HALF], U32, "wo_codes0")[:], sbuf([P, HALF], U32, "wo_codes1", "wo_raw1")[:]]
         wo_scales = [sbuf([P, HALF], U8, "wo_scales%d" % pair) for pair in range(2)]
-        shared = sbuf([P, 3 * HALF], F32, "shared", "dy_bf")
-        one_minus_h = as_planes(shared[:, 0:S])
-        wo_bf = (sbuf([P, 2 * S], BF16, "wo_bf0", "dy_raw")[:], shared[:, HALF : 3 * HALF].bitcast(BF16))
+        woven = (sbuf([P, 2 * S], BF16, "woven0")[:], arena[:, 4 * HALF + P : 6 * HALF + P].bitcast(BF16))
 
         def weave_wo(copy, pair, n):
-            dst = wo_bf[pair].rearrange("p (t m j) -> p m j t", t=2, j=PACK)
+            dst = woven[pair].rearrange("p (t m j) -> p m j t", t=2, j=PACK)
             src = wo_raw[n][:].rearrange("p j (m t) -> p m j t", t=PACK)
             copy(dst[:, :, 2 * n : 2 * n + 2, :], src[:, :, :, 2 * pair : 2 * pair + 2])
 
-        def quantise_wo(first, end):
-            words = slice(P * (first % 2), P * (first % 2 + end - first))
-            woven = wo_bf[first // 2][:, S * (first % 2) : S * (first % 2 + end - first)]
-            quantise(wo_codes[first // 2][:, words], wo_scales[first // 2][:, words], woven, E4M3)
+        def quantise_wo(pair):
+            quantise(wo_codes[pair], wo_scales[pair][:], woven[pair], E4M3)
 
-        def make_one_minus_h(first, end):
-            nc.scalar.activation(
-                out=one_minus_h[:, first:end, :], in_=factor[:, first:end, LAST:S], func=COPY, scale=-1.0, bias=1.0
-            )
+        dy_codes = [sbuf([P, HALF], U32, "dy_codes%d" % n) for n in range(2)]
+        dy_scales = [sbuf([P, HALF], U8, "dy_scales%d" % n) for n in range(2)]
+
+        def weave_dy(n):
+            dy_bf = woven[n].rearrange("p (c j) -> p c j", j=PACK)
+            nc.vector.tensor_copy(*weave_views(dy_bf[:, 0:DY_ON_VECTOR, :], dy_raw[n][:, :, 0:DY_ON_VECTOR]))
+            nc.scalar.copy(*weave_views(dy_bf[:, DY_ON_VECTOR:HALF, :], dy_raw[n][:, :, DY_ON_VECTOR:HALF]))
+
+        def quantise_dy(n):
+            quantise(dy_codes[n][:], dy_scales[n][:], woven[n], E5M2)
+
+        u_acc = [psum.tile([P, S], F32, name="u_acc%d" % t) for t in range(PACK)]
+        u = [sbuf([P, S], F32, "u%d" % t) for t in range(PACK)]
+
+        def make_u(n):
+            cols = slice(HALF * n, HALF * (n + 1))
+            for t in range(PACK):
+                words = slice(P * (t % 2), P * (t % 2 + 1))
+                multiply(u_acc[t][:, cols], wo_codes[t // 2][:, words], wo_scales[t // 2][:, words], dy_codes[n][:], dy_scales[n][:])
+                nc.scalar.copy(out=u[t][:, cols], in_=u_acc[t][:, cols])
 
         for n in range(2):
             weave_wo(nc.vector.tensor_copy, 0, n)
             weave_wo(nc.scalar.copy, 1, n)
-        make_neg_slope(0)
-        quantise_wo(0, 1)
-        quantise_wo(1, 2)
-        make_neg_slope(1)
-        quantise_wo(2, 4)
-        make_neg_slope(2)
-        make_neg_slope(3)
-
-        u = []
-        for t in range(PACK):
-            u_acc = psum.tile([P, S], F32, name="u_acc%d" % t)
-            words = slice(P * (t % 2), P * (t % 2 + 1))
-            multiply(u_acc[:], wo_codes[t // 2][:, words], wo_scales[t // 2][:, words], grad_codes[:, 0:S], grad_scales[:, 0:S])
-            u_plane = sbuf([P, S], F32, "u%d" % t)
-            nc.scalar.copy(out=u_plane[:], in_=u_acc[:])
-            u.append(u_plane)
-
-        make_one_minus_h(0, 2)
+        quantise_wo(0)
+        weave_dy(0)
+        quantise_wo(1)
+        quantise_dy(0)
+        weave_dy(1)
+        make_u(0)
+        make_one_minus_h(0, 0, S)
+        quantise_dy(1)
+        make_u(1)
+        make_neg_slope(2, 0, S)
+        make_neg_slope(3, 0, S)
+        make_neg_slope(1, 0, S)
 
         w_bf = sbuf([P, S, PACK], BF16, "w_bf", "wo_raw1")
+        w_codes = sbuf([P, S], U32, "w_codes")
+        w_scales = sbuf([P, S], U8, "w_scales")
 
-        def weave_w(q):
-            first = P * (q % 2)
-            nc.scalar.copy(*weave_views(w_bf[:, P * q : P * (q + 1), :], w_raw[q // 2][:, :, first : first + P]))
+        def quantise_w(n):
+            cols = slice(HALF * n, HALF * (n + 1))
+            quantise(w_codes[:, cols], w_scales[:, cols], w_bf[:, cols, :].rearrange("p c j -> p (c j)"), E4M3)
 
-        def quantise_w(q, reuse=None):
-            codes = sbuf([P, P], U32, "w_codes%d" % q, reuse)
-            scales = sbuf([P, P], U8, "w_scales%d" % q)
-            quantise(codes[:], scales[:], w_bf[:, P * q : P * (q + 1), :].rearrange("p c j -> p (c j)"), E4M3)
-            return codes, scales
+        picked_tile = sbuf([P, PACK, S], F32, "picked")
 
-        def gather(dst, t, first, end):
+        def picked(planes, first, end):
+            return picked_tile[:, planes, first:end]
+
+        dz_tile = sbuf([P, S, PACK], BF16, "dz_bf", "w_raw")
+        dz_bf = [dz_tile[:, first:end, :] for first, end in RUNS]
+        dz_codes = [sbuf([P, end - first], U32, "dz_codes%d" % r) for r, (first, end) in enumerate(RUNS)]
+        dz_scales = [sbuf([P, end - first], U8, "dz_scales%d" % r) for r, (first, end) in enumerate(RUNS)]
+
+        def gather_on_scalar(r, planes):
+            first, end = RUNS[r]
+            for t in planes:
+                nc.scalar.activation(
+                    out=picked(t, first, end),
+                    in_=u[t][:].indirect(offsets[:, first // LIST_ROWS : end // LIST_ROWS]),
+                    func=COPY,
+                    scale=-1.0,
+                )
+
+        def gather_on_vector(first, end, planes):
+            for t in planes:
+                nc.vector.tensor_tensor(
+                    out=picked(t, first, end),
+                    in0=u[t][:].indirect(offsets[:, first // LIST_ROWS : end // LIST_ROWS]),
+                    in1=h_sb[:, t, first:end],
+                    op=ALU.mult,
+                )
+
+        def weave_dz(r):
+            first, end = RUNS[r]
             nc.vector.tensor_tensor(
-                out=dst,
-                in0=u[t][:].indirect(offsets[:, first // LIST_ROWS : end // LIST_ROWS]),
-                in1=factor[:, t, first:end],
+                out=dz_bf[r].rearrange("p (c n) j -> p c j n", n=2),
+                in0=picked(slice(0, PACK), first, end).rearrange("p j (c n) -> p c j n", n=2),
+                in1=factor(slice(0, PACK), first, end).rearrange("p j (c n) -> p c j n", n=2),
                 op=ALU.mult,
             )
 
-        def quantise_dz(first, end, woven):
-            words = slice(S + first, S + end)
-            quantise(grad_codes[:, words], grad_scales[:, words], woven.rearrange("p c j -> p (c j)"), E5M2)
+        def quantise_dz(r):
+            quantise(dz_codes[r][:], dz_scales[r][:], dz_bf[r].rearrange("p c j -> p (c j)"), E5M2)
 
-        def weave_dz_on_scalar(woven, planes):
-            dst, src = weave_views(woven, planes)
-            nc.scalar.activation(out=dst, in_=src, func=COPY, scale=-1.0)
+        def close(r, quarters, banks, copies):
+            first, end = RUNS[r]
+            width = end - first
+            per_bank = len(quarters) // len(banks)
+            result = keep.tile([P, len(quarters), width], F32, name="result%d_%d" % (r, quarters[0]))
+            for b, bank in enumerate(banks):
+                acc = psum.tile([P, per_bank, width], F32, name="acc%d_%d_%d" % (r, quarters[0], b), tag=bank)
+                for k in range(per_bank):
+                    q = quarters[b * per_bank + k]
+                    cols = slice(P * q, P * (q + 1))
+                    multiply(acc[:, k, :], w_codes[:, cols], w_scales[:, cols], dz_codes[r][:], dz_scales[r][:])
+                copies[b](result[:, b * per_bank : (b + 1) * per_bank, :], acc[:])
+            rows_out = out[P * quarters[0] : P * (quarters[-1] + 1), first:end]
+            nc.sync.dma_start(out=rows_out.rearrange("(q p) c -> p q c", p=P), in_=result[:])
 
-        weave_w(0)
-        weave_w(1)
-        for t in range(PACK):
-            gather(early[:, t, :], t, 0, MIDDLE)
-        early_bf = sbuf([P, HALF, PACK], BF16, "early_bf")
-        weave_dz_on_scalar(early_bf[:], early)
-        weave_w(2)
-        make_one_minus_h(2, 4)
-        weave_w(3)
-        for t in range(1, PACK):
-            gather(later[:, t, :], t, MIDDLE, S)
-        w_tiles = [quantise_w(0)]
-        quantise_dz(0, MIDDLE, early_bf[:])
-        w_tiles.append(quantise_w(1, "early_bf"))
-        gather(later[:, 0, 0:P], 0, MIDDLE, LAST)
-        middle_bf = sbuf([P, P, PACK], BF16, "middle_bf")
-        weave_dz_on_scalar(middle_bf[:], later[:, :, 0:P])
-        gather(later[:, 0, P:HALF], 0, LAST, S)
-        w_tiles.append(quantise_w(2))
-        last_bf = w_second[:, 0:HALF].bitcast(BF16).rearrange("p (c j) -> p c j", j=PACK)
-        nc.vector.tensor_tensor(
-            out=last_bf.rearrange("p (c n) j -> p c j n", n=2),
-            in0=later[:, :, P:HALF].rearrange("p j (c n) -> p c j n", n=2),
-            in1=one_minus_h.rearrange("p j (c n) -> p c j n", n=2),
-            op=ALU.mult,
-        )
-        quantise_dz(MIDDLE, LAST, middle_bf[:])
-        quantise_dz(LAST, S, last_bf)
-        w_tiles.append(quantise_w(3, "middle_bf"))
-
-        def product(q, bank, first_word):
-            acc = psum.tile([P, S], F32, name="acc_" + bank, tag=bank)
-            words = slice(first_word, first_word + S)
-            multiply(acc[:], w_tiles[q][0][:], w_tiles[q][1][:], grad_codes[:, words], grad_scales[:, words])
-            return acc
-
-        early_result = keep.tile([P, 2, MIDDLE], F32, name="early_result")
-        for q in range(2):
-            nc.scalar.copy(early_result[:, q, :], product(q, "out%d" % q, HALF)[:, HALF:S])
-        nc.sync.dma_start(out=out[0:HALF, 0:MIDDLE].rearrange("(q p) c -> p q c", q=2), in_=early_result[:])
-
-        def close(q, bank, pieces, copy):
-            acc = product(q, bank, S)
-            for first, end in pieces:
-                result = keep.tile([P, end - first], F32, name="result%d_%d" % (q, first))
-                copy(result[:], acc[:, first:end])
-                nc.sync.dma_start(out=out[P * q : P * (q + 1), first:end], in_=result[:])
-
-        close(2, "out2", ((0, MIDDLE), (MIDDLE, S)), nc.vector.tensor_copy)
-        close(3, "out3", ((0, S),), nc.scalar.copy)
-        close(0, "u_acc0", ((MIDDLE, S),), nc.vector.tensor_copy)
-        close(1, "u_acc1", ((MIDDLE, S),), nc.scalar.copy)
+        gather_on_vector(0, HALF, (0,))
+        gather_on_vector(HALF, S, (0,))
+        for r in range(3):
+            gather_on_scalar(r, (1, 2, 3))
+        nc.vector.tensor_copy(*weave_views(w_bf[:], w_raw[:]))
+        weave_dz(0)
+        quantise_w(0)
+        quantise_dz(0)
+        close(0, (0, 1), ("out0",), (nc.scalar.copy,))
+        weave_dz(1)
+        quantise_w(1)
+        close(0, (2, 3), ("out1",), (nc.scalar.copy,))
+        quantise_dz(1)
+        close(1, (0, 1, 2, 3), ("out2",), (nc.scalar.copy,))
+        weave_dz(2)
+        quantise_dz(2)
+        close(2, (0, 1, 2, 3), ("u_acc0", "u_acc1"), (nc.vector.tensor_copy, nc.scalar.copy))

@@ -20,6 +20,7 @@ ALU = mybir.AluOpType
 COPY = mybir.ActivationFunctionType.Copy
 
 DY_ON_VECTOR = 168
+H_PIECES = ((0, 256), (256, 832), (832, 1280), (1280, 2048))
 RUNS = ((0, 256), (256, 384), (384, 512))
 
 
@@ -63,43 +64,30 @@ def tile_attend_ghsort_sig_kernel(tc, wo, dyT, W, h, offs, out):
             nc.sync.dma_start(out=wo_part[:], in_=rows(wo)[:, 2 * n : 2 * n + 2, :])
             wo_raw.append(wo_part)
         arena = sbuf([P, 3 * HALF + PACK * S], F32, "arena")
-        factor_halves = arena[:, 3 * HALF :].rearrange("p (n t c) -> p n t c", n=2, t=PACK)
-
-        def factor(planes, first, end):
-            if end - first == S:
-                return factor_halves[:, :, planes, :]
-            return factor_halves[:, first // HALF, planes, first % HALF : first % HALF + end - first]
-
-        def h_part(t, first, end):
-            if end - first == S:
-                return h_sb[:, t, :].rearrange("p (n c) -> p n c", n=2)
-            return h_sb[:, t, first:end]
-
+        factor_flat = arena[:, 3 * HALF :]
+        factor = as_planes(factor_flat)
         dy_raw = (sbuf([P, PACK, HALF], F32, "dy_raw0")[:], as_planes(arena[:, 0 : 2 * S]))
         for n in range(2):
             nc.sync.dma_start(out=dy_raw[n], in_=rows(dyT)[:, :, HALF * n : HALF * (n + 1)])
         offsets = keep.tile([P, S // LIST_ROWS], U16, name="offsets")
-        h_sb = keep.tile([P, PACK, S], F32, name="h_sb")
-        for t in (0, 2, 3, 1):
-            nc.sync.dma_start(out=h_sb[:, t, :], in_=rows(h)[:, t, :])
+        h_flat = keep.tile([P, PACK * S], F32, name="h_flat")
+        h_sb = as_planes(h_flat[:])
+        for first, end in H_PIECES:
+            nc.sync.dma_start(out=h_flat[:, first:end], in_=h.rearrange("(p j) c -> p (j c)", j=PACK)[:, first:end])
         nc.sync.dma_start(offsets[:], offs)
-        w_raw = sbuf([P, PACK, S], F32, "w_raw")
-        nc.sync.dma_start(out=w_raw[:], in_=rows(W))
+        w_raw = [sbuf([P, PACK, HALF], F32, "w_raw%d" % n) for n in range(2)]
+        for n in range(2):
+            nc.sync.dma_start(out=w_raw[n][:], in_=rows(W)[:, :, HALF * n : HALF * (n + 1)])
 
-        def make_neg_slope(t, first, end):
-            part = h_part(t, first, end)
+        def make_neg_slope(first, end):
+            part = h_flat[:, first:end]
             nc.vector.scalar_tensor_tensor(
-                out=factor(t, first, end), in0=part, scalar=1.0, in1=part, op0=ALU.subtract, op1=ALU.mult
-            )
-
-        def make_one_minus_h(t, first, end):
-            nc.vector.tensor_scalar(
-                out=factor(t, first, end), in0=h_part(t, first, end), scalar1=-1.0, scalar2=1.0, op0=ALU.mult, op1=ALU.add
+                out=factor_flat[:, first:end], in0=part, scalar=1.0, in1=part, op0=ALU.subtract, op1=ALU.mult
             )
 
         wo_codes = [sbuf([P, HALF], U32, "wo_codes0")[:], sbuf([P, HALF], U32, "wo_codes1", "wo_raw1")[:]]
         wo_scales = [sbuf([P, HALF], U8, "wo_scales%d" % pair) for pair in range(2)]
-        woven = (sbuf([P, 2 * S], BF16, "woven0")[:], arena[:, 4 * HALF + P : 6 * HALF + P].bitcast(BF16))
+        woven = (sbuf([P, 2 * S], BF16, "woven0")[:], factor_flat[:, 800 : 800 + S].bitcast(BF16))
 
         def weave_wo(copy, pair, n):
             dst = woven[pair].rearrange("p (t m j) -> p m j t", t=2, j=PACK)
@@ -139,16 +127,21 @@ def tile_attend_ghsort_sig_kernel(tc, wo, dyT, W, h, offs, out):
         quantise_dy(0)
         weave_dy(1)
         make_u(0)
-        make_one_minus_h(0, 0, S)
+        nc.vector.tensor_scalar(
+            out=factor_flat[:, 0:HALF], in0=h_flat[:, 0:HALF], scalar1=-1.0, scalar2=1.0, op0=ALU.mult, op1=ALU.add
+        )
         quantise_dy(1)
         make_u(1)
-        make_neg_slope(2, 0, S)
-        make_neg_slope(3, 0, S)
-        make_neg_slope(1, 0, S)
+        for first, end in H_PIECES[1:]:
+            make_neg_slope(first, end)
 
         w_bf = sbuf([P, S, PACK], BF16, "w_bf", "wo_raw1")
         w_codes = sbuf([P, S], U32, "w_codes")
         w_scales = sbuf([P, S], U8, "w_scales")
+
+        def weave_w(n):
+            dst = w_bf[:].rearrange("p (e n c k) j -> p n e c j k", e=2, n=2, k=4)[:, n]
+            nc.vector.tensor_copy(dst, w_raw[n][:].rearrange("p j (e c k) -> p e c j k", e=2, k=4))
 
         def quantise_w(n):
             cols = slice(HALF * n, HALF * (n + 1))
@@ -159,7 +152,7 @@ def tile_attend_ghsort_sig_kernel(tc, wo, dyT, W, h, offs, out):
         def picked(planes, first, end):
             return picked_tile[:, planes, first:end]
 
-        dz_tile = sbuf([P, S, PACK], BF16, "dz_bf", "w_raw")
+        dz_tile = sbuf([P, S, PACK], BF16, "dz_bf", "w_raw1")
         dz_bf = [dz_tile[:, first:end, :] for first, end in RUNS]
         dz_codes = [sbuf([P, end - first], U32, "dz_codes%d" % r) for r, (first, end) in enumerate(RUNS)]
         dz_scales = [sbuf([P, end - first], U8, "dz_scales%d" % r) for r, (first, end) in enumerate(RUNS)]
@@ -188,42 +181,55 @@ def tile_attend_ghsort_sig_kernel(tc, wo, dyT, W, h, offs, out):
             nc.vector.tensor_tensor(
                 out=dz_bf[r].rearrange("p (c n) j -> p c j n", n=2),
                 in0=picked(slice(0, PACK), first, end).rearrange("p j (c n) -> p c j n", n=2),
-                in1=factor(slice(0, PACK), first, end).rearrange("p j (c n) -> p c j n", n=2),
+                in1=factor[:, :, first:end].rearrange("p j (c n) -> p c j n", n=2),
                 op=ALU.mult,
             )
 
         def quantise_dz(r):
             quantise(dz_codes[r][:], dz_scales[r][:], dz_bf[r].rearrange("p c j -> p (c j)"), E5M2)
 
-        def close(r, quarters, banks, copies):
+        def close(r, parities, bank, copy):
             first, end = RUNS[r]
             width = end - first
-            per_bank = len(quarters) // len(banks)
-            result = keep.tile([P, len(quarters), width], F32, name="result%d_%d" % (r, quarters[0]))
-            for b, bank in enumerate(banks):
-                acc = psum.tile([P, per_bank, width], F32, name="acc%d_%d_%d" % (r, quarters[0], b), tag=bank)
-                for k in range(per_bank):
-                    q = quarters[b * per_bank + k]
-                    cols = slice(P * q, P * (q + 1))
-                    multiply(acc[:, k, :], w_codes[:, cols], w_scales[:, cols], dz_codes[r][:], dz_scales[r][:])
-                copies[b](result[:, b * per_bank : (b + 1) * per_bank, :], acc[:])
-            rows_out = out[P * quarters[0] : P * (quarters[-1] + 1), first:end]
-            nc.sync.dma_start(out=rows_out.rearrange("(q p) c -> p q c", p=P), in_=result[:])
+            count = 2 * len(parities)
+            result = keep.tile([P, count, width], F32, name="result%d_%d" % (r, parities[0]))
+            acc = psum.tile([P, count, width], F32, name="acc%d_%d" % (r, parities[0]), tag=bank)
+            for k in range(count):
+                place = 2 * parities[0] + k if count == 2 else 2 * (k % 2) + k // 2
+                cols = slice(P * place, P * (place + 1))
+                multiply(acc[:, k, :], w_codes[:, cols], w_scales[:, cols], dz_codes[r][:], dz_scales[r][:])
+            copy(result[:], acc[:])
+            if count == 2:
+                rows_out = out[:, first:end].rearrange("(n e p) c -> p e n c", e=2, p=P)[:, parities[0]]
+            else:
+                rows_out = out[:, first:end].rearrange("(q p) c -> p q c", p=P)
+            nc.sync.dma_start(out=rows_out, in_=result[:])
 
         gather_on_vector(0, HALF, (0,))
-        gather_on_vector(HALF, S, (0,))
-        for r in range(3):
-            gather_on_scalar(r, (1, 2, 3))
-        nc.vector.tensor_copy(*weave_views(w_bf[:], w_raw[:]))
+        gather_on_scalar(0, (1, 2, 3))
+        gather_on_scalar(1, (0, 1, 2, 3))
+        gather_on_scalar(2, (0, 1, 2, 3))
+        weave_w(0)
+        weave_w(1)
         weave_dz(0)
         quantise_w(0)
         quantise_dz(0)
-        close(0, (0, 1), ("out0",), (nc.scalar.copy,))
+        close(0, (0,), "out0", nc.scalar.copy)
         weave_dz(1)
         quantise_w(1)
-        close(0, (2, 3), ("out1",), (nc.scalar.copy,))
+        close(0, (1,), "out1", nc.scalar.copy)
         quantise_dz(1)
-        close(1, (0, 1, 2, 3), ("out2",), (nc.scalar.copy,))
+        close(1, (0, 1), "out2", nc.scalar.copy)
         weave_dz(2)
         quantise_dz(2)
-        close(2, (0, 1, 2, 3), ("u_acc0", "u_acc1"), (nc.vector.tensor_copy, nc.scalar.copy))
+        first, end = RUNS[2]
+        for parity in range(2):
+            result = keep.tile([P, 2, P], F32, name="last%d" % parity)
+            for n in range(2):
+                place = 2 * parity + n
+                acc = psum.tile([P, P], F32, name="last_acc%d" % place, tag="u_acc%d" % place)
+                cols = slice(P * place, P * (place + 1))
+                multiply(acc[:], w_codes[:, cols], w_scales[:, cols], dz_codes[2][:], dz_scales[2][:])
+                (nc.vector.tensor_copy, nc.scalar.copy)[n](result[:, n, :], acc[:])
+            rows_out = out[:, first:end].rearrange("(n e p) c -> p e n c", e=2, p=P)[:, parity]
+            nc.sync.dma_start(out=rows_out, in_=result[:])

@@ -20,7 +20,8 @@ ALU = mybir.AluOpType
 COPY = mybir.ActivationFunctionType.Copy
 
 DY_ON_VECTOR = 168
-H_PIECES = ((0, 256), (256, 832), (832, 1280), (1280, 2048))
+OVERLAP = 64
+LATE_STEP = 2 * S + P
 RUNS = ((0, 256), (256, 384), (384, 512))
 
 
@@ -63,31 +64,43 @@ def tile_attend_ghsort_sig_kernel(tc, wo, dyT, W, h, offs, out):
             wo_part = sbuf([P, 2, S], F32, "wo_raw%d" % n)
             nc.sync.dma_start(out=wo_part[:], in_=rows(wo)[:, 2 * n : 2 * n + 2, :])
             wo_raw.append(wo_part)
-        arena = sbuf([P, 3 * HALF + PACK * S], F32, "arena")
-        factor_flat = arena[:, 3 * HALF :]
+        arena = sbuf([P, 2 * S - OVERLAP + PACK * S], F32, "arena")
+        factor_flat = arena[:, 2 * S - OVERLAP :]
         factor = as_planes(factor_flat)
-        dy_raw = (sbuf([P, PACK, HALF], F32, "dy_raw0")[:], as_planes(arena[:, 0 : 2 * S]))
+        dy_raw = (sbuf([P, PACK, HALF], F32, "dy_raw0")[:], as_planes(factor_flat[:, OVERLAP : OVERLAP + 2 * S]))
         for n in range(2):
             nc.sync.dma_start(out=dy_raw[n], in_=rows(dyT)[:, :, HALF * n : HALF * (n + 1)])
         offsets = keep.tile([P, S // LIST_ROWS], U16, name="offsets")
-        h_flat = keep.tile([P, PACK * S], F32, name="h_flat")
-        h_sb = as_planes(h_flat[:])
-        for first, end in H_PIECES:
-            nc.sync.dma_start(out=h_flat[:, first:end], in_=h.rearrange("(p j) c -> p (j c)", j=PACK)[:, first:end])
+        h_outer = keep.tile([P, 2, S], F32, name="h_outer")
+
+        def h_flat(first, end):
+            if first < S:
+                return h_outer[:, 0, first:end]
+            if first >= 3 * S:
+                return h_outer[:, 1, first - 3 * S : end - 3 * S]
+            return arena[:, first - S : end - S]
+
+        for first, end in ((S, S + HALF), (S + HALF, 3 * S), (3 * S, 4 * S), (0, S)):
+            nc.sync.dma_start(out=h_flat(first, end), in_=h.rearrange("(p j) c -> p (j c)", j=PACK)[:, first:end])
         nc.sync.dma_start(offsets[:], offs)
         w_raw = [sbuf([P, PACK, HALF], F32, "w_raw%d" % n) for n in range(2)]
         for n in range(2):
             nc.sync.dma_start(out=w_raw[n][:], in_=rows(W)[:, :, HALF * n : HALF * (n + 1)])
 
         def make_neg_slope(first, end):
-            part = h_flat[:, first:end]
+            part = h_flat(first, end)
             nc.vector.scalar_tensor_tensor(
                 out=factor_flat[:, first:end], in0=part, scalar=1.0, in1=part, op0=ALU.subtract, op1=ALU.mult
             )
 
+        def make_one_minus_h(first, end):
+            nc.vector.tensor_scalar(
+                out=factor_flat[:, first:end], in0=h_flat(first, end), scalar1=-1.0, scalar2=1.0, op0=ALU.mult, op1=ALU.add
+            )
+
         wo_codes = [sbuf([P, HALF], U32, "wo_codes0")[:], sbuf([P, HALF], U32, "wo_codes1", "wo_raw1")[:]]
         wo_scales = [sbuf([P, HALF], U8, "wo_scales%d" % pair) for pair in range(2)]
-        woven = (sbuf([P, 2 * S], BF16, "woven0")[:], factor_flat[:, 800 : 800 + S].bitcast(BF16))
+        woven = (sbuf([P, 2 * S], BF16, "woven0")[:], factor_flat[:, 1120 : 1120 + S].bitcast(BF16))
 
         def weave_wo(copy, pair, n):
             dst = woven[pair].rearrange("p (t m j) -> p m j t", t=2, j=PACK)
@@ -113,7 +126,7 @@ def tile_attend_ghsort_sig_kernel(tc, wo, dyT, W, h, offs, out):
 
         def make_u(n):
             cols = slice(HALF * n, HALF * (n + 1))
-            for t in range(PACK):
+            for t in (1, 2, 3, 0):
                 words = slice(P * (t % 2), P * (t % 2 + 1))
                 multiply(u_acc[t][:, cols], wo_codes[t // 2][:, words], wo_scales[t // 2][:, words], dy_codes[n][:], dy_scales[n][:])
                 nc.scalar.copy(out=u[t][:, cols], in_=u_acc[t][:, cols])
@@ -127,29 +140,33 @@ def tile_attend_ghsort_sig_kernel(tc, wo, dyT, W, h, offs, out):
         quantise_dy(0)
         weave_dy(1)
         make_u(0)
-        nc.vector.tensor_scalar(
-            out=factor_flat[:, 0:HALF], in0=h_flat[:, 0:HALF], scalar1=-1.0, scalar2=1.0, op0=ALU.mult, op1=ALU.add
-        )
+        make_one_minus_h(S, S + HALF)
         quantise_dy(1)
         make_u(1)
-        for first, end in H_PIECES[1:]:
-            make_neg_slope(first, end)
+        make_one_minus_h(S + HALF, 2 * S + P)
+        make_neg_slope(2 * S + P, 3 * S)
+        make_neg_slope(3 * S, 4 * S)
+        make_neg_slope(0, S)
 
-        w_bf = sbuf([P, S, PACK], BF16, "w_bf", "wo_raw1")
+        late = sbuf([P, PACK * LATE_STEP], F32, "late", "wo_raw1")
+        w_end = LATE_STEP + OVERLAP
+        w_bf = late[:, w_end - 2 * S : w_end].bitcast(BF16).rearrange("p (c j) -> p c j", j=PACK)
         w_codes = sbuf([P, S], U32, "w_codes")
         w_scales = sbuf([P, S], U8, "w_scales")
 
         def weave_w(n):
-            dst = w_bf[:].rearrange("p (e n c k) j -> p n e c j k", e=2, n=2, k=4)[:, n]
+            dst = w_bf.rearrange("p (e n c k) j -> p n e c j k", e=2, n=2, k=4)[:, n]
             nc.vector.tensor_copy(dst, w_raw[n][:].rearrange("p j (e c k) -> p e c j k", e=2, k=4))
 
         def quantise_w(n):
             cols = slice(HALF * n, HALF * (n + 1))
             quantise(w_codes[:, cols], w_scales[:, cols], w_bf[:, cols, :].rearrange("p c j -> p (c j)"), E4M3)
 
-        picked_tile = sbuf([P, PACK, S], F32, "picked")
+        picked_tile = sbuf([P, PACK, HALF + P], F32, "picked")
 
         def picked(planes, first, end):
+            if first >= HALF + P:
+                return as_planes(late[:])[:, planes, first - HALF - P : end - HALF - P]
             return picked_tile[:, planes, first:end]
 
         dz_tile = sbuf([P, S, PACK], BF16, "dz_bf", "w_raw1")
@@ -157,8 +174,7 @@ def tile_attend_ghsort_sig_kernel(tc, wo, dyT, W, h, offs, out):
         dz_codes = [sbuf([P, end - first], U32, "dz_codes%d" % r) for r, (first, end) in enumerate(RUNS)]
         dz_scales = [sbuf([P, end - first], U8, "dz_scales%d" % r) for r, (first, end) in enumerate(RUNS)]
 
-        def gather_on_scalar(r, planes):
-            first, end = RUNS[r]
+        def gather_on_scalar(first, end, planes):
             for t in planes:
                 nc.scalar.activation(
                     out=picked(t, first, end),
@@ -172,7 +188,7 @@ def tile_attend_ghsort_sig_kernel(tc, wo, dyT, W, h, offs, out):
                 nc.vector.tensor_tensor(
                     out=picked(t, first, end),
                     in0=u[t][:].indirect(offsets[:, first // LIST_ROWS : end // LIST_ROWS]),
-                    in1=h_sb[:, t, first:end],
+                    in1=h_flat(S * t + first, S * t + end),
                     op=ALU.mult,
                 )
 
@@ -205,19 +221,22 @@ def tile_attend_ghsort_sig_kernel(tc, wo, dyT, W, h, offs, out):
                 rows_out = out[:, first:end].rearrange("(q p) c -> p q c", p=P)
             nc.sync.dma_start(out=rows_out, in_=result[:])
 
-        gather_on_vector(0, HALF, (0,))
-        gather_on_scalar(0, (1, 2, 3))
-        gather_on_scalar(1, (0, 1, 2, 3))
-        gather_on_scalar(2, (0, 1, 2, 3))
+        gather_on_vector(0, HALF + P, (1,))
+        gather_on_vector(0, P, (2,))
+        gather_on_scalar(P, HALF, (2,))
+        gather_on_scalar(0, HALF, (3, 0))
+        for first, end in RUNS[1:]:
+            gather_on_scalar(first, end, (2, 3, 0))
         weave_w(0)
         weave_w(1)
         weave_dz(0)
         quantise_w(0)
         quantise_dz(0)
         close(0, (0,), "out0", nc.scalar.copy)
-        weave_dz(1)
         quantise_w(1)
         close(0, (1,), "out1", nc.scalar.copy)
+        weave_dz(1)
+        gather_on_vector(HALF + P, S, (1,))
         quantise_dz(1)
         close(1, (0, 1), "out2", nc.scalar.copy)
         weave_dz(2)

@@ -21,8 +21,8 @@ COPY = mybir.ActivationFunctionType.Copy
 
 DY_ON_VECTOR = 168
 OVERLAP = 64
-LATE_STEP = 2 * S + P
-RUNS = ((0, 256), (256, 384), (384, 512))
+MIDDLE = HALF
+LAST = HALF + P
 
 
 def weave_views(dst, src):
@@ -59,56 +59,42 @@ def tile_attend_ghsort_sig_kernel(tc, wo, dyT, W, h, offs, out):
         def rows(matrix):
             return matrix.rearrange("(p j) c -> p j c", j=PACK)
 
-        wo_raw = []
+        wo_raw = sbuf([P, PACK, S], F32, "wo_raw")
+        nc.sync.dma_start(out=wo_raw[:], in_=rows(wo))
+        dy_raw = [sbuf([P, PACK, HALF], F32, "dy_raw%d" % n) for n in range(2)]
         for n in range(2):
-            wo_part = sbuf([P, 2, S], F32, "wo_raw%d" % n)
-            nc.sync.dma_start(out=wo_part[:], in_=rows(wo)[:, 2 * n : 2 * n + 2, :])
-            wo_raw.append(wo_part)
+            nc.sync.dma_start(out=dy_raw[n][:], in_=rows(dyT)[:, :, HALF * n : HALF * (n + 1)])
+        offsets = keep.tile([P, S // LIST_ROWS], U16, name="offsets")
+        nc.sync.dma_start(offsets[:], offs)
         arena = sbuf([P, 2 * S - OVERLAP + PACK * S], F32, "arena")
         factor_flat = arena[:, 2 * S - OVERLAP :]
         factor = as_planes(factor_flat)
-        dy_raw = (sbuf([P, PACK, HALF], F32, "dy_raw0")[:], as_planes(factor_flat[:, OVERLAP : OVERLAP + 2 * S]))
-        for n in range(2):
-            nc.sync.dma_start(out=dy_raw[n], in_=rows(dyT)[:, :, HALF * n : HALF * (n + 1)])
-        offsets = keep.tile([P, S // LIST_ROWS], U16, name="offsets")
-        h_outer = keep.tile([P, 2, S], F32, name="h_outer")
+        h_low = keep.tile([P, 2 * S], F32, name="h_low")
 
         def h_flat(first, end):
-            if first < S:
-                return h_outer[:, 0, first:end]
-            if first >= 3 * S:
-                return h_outer[:, 1, first - 3 * S : end - 3 * S]
-            return arena[:, first - S : end - S]
+            return h_low[:, first:end] if first < 2 * S else arena[:, first - 2 * S : end - 2 * S]
 
-        for first, end in ((S, S + HALF), (S + HALF, 3 * S), (3 * S, 4 * S), (0, S)):
-            nc.sync.dma_start(out=h_flat(first, end), in_=h.rearrange("(p j) c -> p (j c)", j=PACK)[:, first:end])
-        nc.sync.dma_start(offsets[:], offs)
-        w_raw = [sbuf([P, PACK, HALF], F32, "w_raw%d" % n) for n in range(2)]
-        for n in range(2):
-            nc.sync.dma_start(out=w_raw[n][:], in_=rows(W)[:, :, HALF * n : HALF * (n + 1)])
+        for first in (2 * S, 0):
+            h_pair = h.rearrange("(p j) c -> p (j c)", j=PACK)[:, first : first + 2 * S]
+            nc.sync.dma_start(out=h_flat(first, first + 2 * S), in_=h_pair)
+        w_flat = sbuf([P, PACK * S], F32, "w_raw")
+        w_raw = as_planes(w_flat[:])
+        nc.sync.dma_start(out=w_raw, in_=rows(W))
 
-        def make_neg_slope(first, end):
-            part = h_flat(first, end)
-            nc.vector.scalar_tensor_tensor(
-                out=factor_flat[:, first:end], in0=part, scalar=1.0, in1=part, op0=ALU.subtract, op1=ALU.mult
-            )
+        def make_neg_slope(dst, part):
+            nc.vector.scalar_tensor_tensor(out=dst, in0=part, scalar=1.0, in1=part, op0=ALU.subtract, op1=ALU.mult)
 
-        def make_one_minus_h(first, end):
-            nc.vector.tensor_scalar(
-                out=factor_flat[:, first:end], in0=h_flat(first, end), scalar1=-1.0, scalar2=1.0, op0=ALU.mult, op1=ALU.add
-            )
-
-        wo_codes = [sbuf([P, HALF], U32, "wo_codes0")[:], sbuf([P, HALF], U32, "wo_codes1", "wo_raw1")[:]]
+        wo_codes = [sbuf([P, HALF], U32, "wo_codes0"), sbuf([P, HALF], U32, "wo_codes1", "wo_raw")]
         wo_scales = [sbuf([P, HALF], U8, "wo_scales%d" % pair) for pair in range(2)]
-        woven = (sbuf([P, 2 * S], BF16, "woven0")[:], factor_flat[:, 1120 : 1120 + S].bitcast(BF16))
+        woven = (sbuf([P, 2 * S], BF16, "woven0")[:], factor_flat[:, 2 * S + P : 3 * S + P].bitcast(BF16))
 
-        def weave_wo(copy, pair, n):
+        def weave_wo(copy, pair):
             dst = woven[pair].rearrange("p (t m j) -> p m j t", t=2, j=PACK)
-            src = wo_raw[n][:].rearrange("p j (m t) -> p m j t", t=PACK)
-            copy(dst[:, :, 2 * n : 2 * n + 2, :], src[:, :, :, 2 * pair : 2 * pair + 2])
+            src = wo_raw[:].rearrange("p j (m t) -> p m j t", t=PACK)
+            copy(dst, src[:, :, :, 2 * pair : 2 * pair + 2])
 
         def quantise_wo(pair):
-            quantise(wo_codes[pair], wo_scales[pair][:], woven[pair], E4M3)
+            quantise(wo_codes[pair][:], wo_scales[pair][:], woven[pair], E4M3)
 
         dy_codes = [sbuf([P, HALF], U32, "dy_codes%d" % n) for n in range(2)]
         dy_scales = [sbuf([P, HALF], U8, "dy_scales%d" % n) for n in range(2)]
@@ -126,129 +112,97 @@ def tile_attend_ghsort_sig_kernel(tc, wo, dyT, W, h, offs, out):
 
         def make_u(n):
             cols = slice(HALF * n, HALF * (n + 1))
-            for t in (1, 2, 3, 0):
+            for t in (2, 3, 0, 1):
                 words = slice(P * (t % 2), P * (t % 2 + 1))
                 multiply(u_acc[t][:, cols], wo_codes[t // 2][:, words], wo_scales[t // 2][:, words], dy_codes[n][:], dy_scales[n][:])
                 nc.scalar.copy(out=u[t][:, cols], in_=u_acc[t][:, cols])
 
-        for n in range(2):
-            weave_wo(nc.vector.tensor_copy, 0, n)
-            weave_wo(nc.scalar.copy, 1, n)
+        weave_wo(nc.vector.tensor_copy, 0)
+        weave_wo(nc.scalar.copy, 1)
         quantise_wo(0)
-        weave_dy(0)
         quantise_wo(1)
+        weave_dy(0)
         quantise_dy(0)
         weave_dy(1)
         make_u(0)
-        make_one_minus_h(S, S + HALF)
         quantise_dy(1)
         make_u(1)
-        make_one_minus_h(S + HALF, 2 * S + P)
-        make_neg_slope(2 * S + P, 3 * S)
-        make_neg_slope(3 * S, 4 * S)
-        make_neg_slope(0, S)
+        nc.vector.tensor_scalar(
+            out=factor[:, 2, 0:LAST], in0=arena[:, 0:LAST], scalar1=-1.0, scalar2=1.0, op0=ALU.mult, op1=ALU.add
+        )
+        make_neg_slope(factor_flat[:, 2 * S + LAST :], arena[:, LAST : 2 * S])
 
-        late = sbuf([P, PACK * LATE_STEP], F32, "late", "wo_raw1")
-        w_end = LATE_STEP + OVERLAP
-        w_bf = late[:, w_end - 2 * S : w_end].bitcast(BF16).rearrange("p (c j) -> p c j", j=PACK)
+        w_bf = sbuf([P, S, PACK], BF16, "w_bf", "wo_raw")
         w_codes = sbuf([P, S], U32, "w_codes")
         w_scales = sbuf([P, S], U8, "w_scales")
-
-        def weave_w(n):
-            dst = w_bf.rearrange("p (e n c k) j -> p n e c j k", e=2, n=2, k=4)[:, n]
-            nc.vector.tensor_copy(dst, w_raw[n][:].rearrange("p j (e c k) -> p e c j k", e=2, k=4))
 
         def quantise_w(n):
             cols = slice(HALF * n, HALF * (n + 1))
             quantise(w_codes[:, cols], w_scales[:, cols], w_bf[:, cols, :].rearrange("p c j -> p (c j)"), E4M3)
 
-        picked_tile = sbuf([P, PACK, HALF + P], F32, "picked")
-
-        def picked(planes, first, end):
-            if first >= HALF + P:
-                return as_planes(late[:])[:, planes, first - HALF - P : end - HALF - P]
-            return picked_tile[:, planes, first:end]
-
-        dz_tile = sbuf([P, S, PACK], BF16, "dz_bf", "w_raw1")
-        dz_bf = [dz_tile[:, first:end, :] for first, end in RUNS]
-        dz_codes = [sbuf([P, end - first], U32, "dz_codes%d" % r) for r, (first, end) in enumerate(RUNS)]
-        dz_scales = [sbuf([P, end - first], U8, "dz_scales%d" % r) for r, (first, end) in enumerate(RUNS)]
+        picked = sbuf([P, PACK, S], F32, "picked")
+        dz_bf = w_flat[:, 2 * S :].bitcast(BF16).rearrange("p (c j) -> p c j", j=PACK)
+        dz_codes = [sbuf([P, HALF], U32, "dz_codes%d" % n) for n in range(2)]
+        dz_scales = [sbuf([P, HALF], U8, "dz_scales%d" % n) for n in range(2)]
 
         def gather_on_scalar(first, end, planes):
             for t in planes:
                 nc.scalar.activation(
-                    out=picked(t, first, end),
+                    out=picked[:, t, first:end],
                     in_=u[t][:].indirect(offsets[:, first // LIST_ROWS : end // LIST_ROWS]),
                     func=COPY,
                     scale=-1.0,
                 )
 
-        def gather_on_vector(first, end, planes):
-            for t in planes:
-                nc.vector.tensor_tensor(
-                    out=picked(t, first, end),
-                    in0=u[t][:].indirect(offsets[:, first // LIST_ROWS : end // LIST_ROWS]),
-                    in1=h_flat(S * t + first, S * t + end),
-                    op=ALU.mult,
-                )
-
-        def weave_dz(r):
-            first, end = RUNS[r]
+        def gather_on_vector(first, end, t):
             nc.vector.tensor_tensor(
-                out=dz_bf[r].rearrange("p (c n) j -> p c j n", n=2),
-                in0=picked(slice(0, PACK), first, end).rearrange("p j (c n) -> p c j n", n=2),
+                out=picked[:, t, first:end],
+                in0=u[t][:].indirect(offsets[:, first // LIST_ROWS : end // LIST_ROWS]),
+                in1=h_flat(S * t + first, S * t + end),
+                op=ALU.mult,
+            )
+
+        def weave_dz(first, end):
+            nc.vector.tensor_tensor(
+                out=dz_bf[:, first:end, :].rearrange("p (c n) j -> p c j n", n=2),
+                in0=picked[:, :, first:end].rearrange("p j (c n) -> p c j n", n=2),
                 in1=factor[:, :, first:end].rearrange("p j (c n) -> p c j n", n=2),
                 op=ALU.mult,
             )
 
-        def quantise_dz(r):
-            quantise(dz_codes[r][:], dz_scales[r][:], dz_bf[r].rearrange("p c j -> p (c j)"), E5M2)
+        def quantise_dz(first, end):
+            words = slice(first % HALF, first % HALF + end - first)
+            woven_dz = dz_bf[:, first:end, :].rearrange("p c j -> p (c j)")
+            quantise(dz_codes[first // HALF][:, words], dz_scales[first // HALF][:, words], woven_dz, E5M2)
 
-        def close(r, parities, bank, copy):
-            first, end = RUNS[r]
-            width = end - first
-            count = 2 * len(parities)
-            result = keep.tile([P, count, width], F32, name="result%d_%d" % (r, parities[0]))
-            acc = psum.tile([P, count, width], F32, name="acc%d_%d" % (r, parities[0]), tag=bank)
-            for k in range(count):
-                place = 2 * parities[0] + k if count == 2 else 2 * (k % 2) + k // 2
-                cols = slice(P * place, P * (place + 1))
-                multiply(acc[:, k, :], w_codes[:, cols], w_scales[:, cols], dz_codes[r][:], dz_scales[r][:])
-            copy(result[:], acc[:])
-            if count == 2:
-                rows_out = out[:, first:end].rearrange("(n e p) c -> p e n c", e=2, p=P)[:, parities[0]]
-            else:
-                rows_out = out[:, first:end].rearrange("(q p) c -> p q c", p=P)
-            nc.sync.dma_start(out=rows_out, in_=result[:])
+        def close(n, pair, banks, copies):
+            result = keep.tile([P, 2, HALF], F32, name="result%d_%d" % (n, pair))
+            per_bank = 2 // len(banks)
+            for b, bank in enumerate(banks):
+                acc = psum.tile([P, per_bank, HALF], F32, name="acc%d_%d_%d" % (n, pair, b), tag=bank)
+                for k in range(per_bank):
+                    q = 2 * pair + b * per_bank + k
+                    cols = slice(P * q, P * (q + 1))
+                    multiply(acc[:, k, :], w_codes[:, cols], w_scales[:, cols], dz_codes[n][:], dz_scales[n][:])
+                copies[b](result[:, b * per_bank : (b + 1) * per_bank, :], acc[:])
+            block = out[HALF * pair : HALF * (pair + 1), HALF * n : HALF * (n + 1)]
+            nc.sync.dma_start(out=block.rearrange("(q p) c -> p q c", p=P), in_=result[:])
 
-        gather_on_vector(0, HALF + P, (1,))
-        gather_on_vector(0, P, (2,))
-        gather_on_scalar(P, HALF, (2,))
-        gather_on_scalar(0, HALF, (3, 0))
-        for first, end in RUNS[1:]:
-            gather_on_scalar(first, end, (2, 3, 0))
-        weave_w(0)
-        weave_w(1)
-        weave_dz(0)
+        gather_on_vector(0, LAST, 2)
+        make_neg_slope(factor_flat[:, 0 : 2 * S], h_low[:])
+        gather_on_scalar(0, MIDDLE, (3, 0, 1))
+        nc.vector.tensor_copy(*weave_views(w_bf[:], w_raw))
+        gather_on_scalar(MIDDLE, LAST, (3, 0, 1))
+        gather_on_scalar(LAST, S, range(PACK))
+        weave_dz(0, MIDDLE)
         quantise_w(0)
-        quantise_dz(0)
-        close(0, (0,), "out0", nc.scalar.copy)
+        quantise_dz(0, MIDDLE)
+        close(0, 0, ("out0",), (nc.scalar.copy,))
         quantise_w(1)
-        close(0, (1,), "out1", nc.scalar.copy)
-        weave_dz(1)
-        gather_on_vector(HALF + P, S, (1,))
-        quantise_dz(1)
-        close(1, (0, 1), "out2", nc.scalar.copy)
-        weave_dz(2)
-        quantise_dz(2)
-        first, end = RUNS[2]
-        for parity in range(2):
-            result = keep.tile([P, 2, P], F32, name="last%d" % parity)
-            for n in range(2):
-                place = 2 * parity + n
-                acc = psum.tile([P, P], F32, name="last_acc%d" % place, tag="u_acc%d" % place)
-                cols = slice(P * place, P * (place + 1))
-                multiply(acc[:], w_codes[:, cols], w_scales[:, cols], dz_codes[2][:], dz_scales[2][:])
-                (nc.vector.tensor_copy, nc.scalar.copy)[n](result[:, n, :], acc[:])
-            rows_out = out[:, first:end].rearrange("(n e p) c -> p e n c", e=2, p=P)[:, parity]
-            nc.sync.dma_start(out=rows_out, in_=result[:])
+        close(0, 1, ("out1",), (nc.scalar.copy,))
+        weave_dz(MIDDLE, LAST)
+        weave_dz(LAST, S)
+        quantise_dz(MIDDLE, LAST)
+        quantise_dz(LAST, S)
+        close(1, 0, ("u_acc0", "u_acc1"), (nc.vector.tensor_copy, nc.scalar.copy))
+        close(1, 1, ("u_acc2", "u_acc3"), (nc.vector.tensor_copy, nc.scalar.copy))

@@ -22,7 +22,9 @@ COPY = mybir.ActivationFunctionType.Copy
 DY_ON_VECTOR = 168
 OVERLAP = 64
 MIDDLE = HALF
+PLANE_ORDER = (1, 2, 3, 0)
 LAST = HALF + P
+RUNS = ((0, MIDDLE), (MIDDLE, LAST), (LAST, S))
 
 
 def weave_views(dst, src):
@@ -59,39 +61,38 @@ def tile_attend_ghsort_sig_kernel(tc, wo, dyT, W, h, offs, out):
         def rows(matrix):
             return matrix.rearrange("(p j) c -> p j c", j=PACK)
 
-        wo_raw = sbuf([P, PACK, S], F32, "wo_raw")
-        nc.sync.dma_start(out=wo_raw[:], in_=rows(wo))
-        dy_raw = [sbuf([P, PACK, HALF], F32, "dy_raw%d" % n) for n in range(2)]
+        wo_raw = [sbuf([P, 2, S], F32, "wo_raw%d" % n) for n in range(2)]
         for n in range(2):
-            nc.sync.dma_start(out=dy_raw[n][:], in_=rows(dyT)[:, :, HALF * n : HALF * (n + 1)])
-        offsets = keep.tile([P, S // LIST_ROWS], U16, name="offsets")
-        nc.sync.dma_start(offsets[:], offs)
+            nc.sync.dma_start(out=wo_raw[n][:], in_=rows(wo)[:, 2 * n : 2 * n + 2, :])
         arena = sbuf([P, 2 * S - OVERLAP + PACK * S], F32, "arena")
         factor_flat = arena[:, 2 * S - OVERLAP :]
         factor = as_planes(factor_flat)
-        h_low = keep.tile([P, 2 * S], F32, name="h_low")
-
-        def h_flat(first, end):
-            return h_low[:, first:end] if first < 2 * S else arena[:, first - 2 * S : end - 2 * S]
-
-        for first in (2 * S, 0):
-            h_pair = h.rearrange("(p j) c -> p (j c)", j=PACK)[:, first : first + 2 * S]
-            nc.sync.dma_start(out=h_flat(first, first + 2 * S), in_=h_pair)
-        w_flat = sbuf([P, PACK * S], F32, "w_raw")
-        w_raw = as_planes(w_flat[:])
-        nc.sync.dma_start(out=w_raw, in_=rows(W))
+        dy_raw = (sbuf([P, PACK, HALF], F32, "dy_raw0")[:], as_planes(factor_flat[:, OVERLAP : OVERLAP + 2 * S]))
+        for n in range(2):
+            nc.sync.dma_start(out=dy_raw[n], in_=rows(dyT)[:, :, HALF * n : HALF * (n + 1)])
+        h_outer = keep.tile([P, 2, S], F32, name="h_outer")
+        h_plane = (h_outer[:, 0, :], arena[:, 0:S], arena[:, S : 2 * S], h_outer[:, 1, :])
+        for t in PLANE_ORDER:
+            nc.sync.dma_start(out=h_plane[t], in_=rows(h)[:, t, :])
+        offsets = keep.tile([P, S // LIST_ROWS], U16, name="offsets")
+        nc.sync.dma_start(offsets[:], offs)
+        w_raw = sbuf([P, PACK, S], F32, "w_raw")
+        nc.sync.dma_start(out=w_raw[:], in_=rows(W))
 
         def make_neg_slope(dst, part):
             nc.vector.scalar_tensor_tensor(out=dst, in0=part, scalar=1.0, in1=part, op0=ALU.subtract, op1=ALU.mult)
 
-        wo_codes = [sbuf([P, HALF], U32, "wo_codes0"), sbuf([P, HALF], U32, "wo_codes1", "wo_raw")]
-        wo_scales = [sbuf([P, HALF], U8, "wo_scales%d" % pair) for pair in range(2)]
-        woven = (sbuf([P, 2 * S], BF16, "woven0")[:], factor_flat[:, 2 * S + P : 3 * S + P].bitcast(BF16))
+        def make_one_minus_h(dst, part):
+            nc.vector.tensor_scalar(out=dst, in0=part, scalar1=-1.0, scalar2=1.0, op0=ALU.mult, op1=ALU.add)
 
-        def weave_wo(copy, pair):
+        wo_codes = [sbuf([P, HALF], U32, "wo_codes0"), sbuf([P, HALF], U32, "wo_codes1", "wo_raw1")]
+        wo_scales = [sbuf([P, HALF], U8, "wo_scales%d" % pair) for pair in range(2)]
+        woven = (sbuf([P, 2 * S], BF16, "woven0")[:], factor_flat[:, 2 * S + P - 32 : 3 * S + P - 32].bitcast(BF16))
+
+        def weave_wo(copy, pair, n):
             dst = woven[pair].rearrange("p (t m j) -> p m j t", t=2, j=PACK)
-            src = wo_raw[:].rearrange("p j (m t) -> p m j t", t=PACK)
-            copy(dst, src[:, :, :, 2 * pair : 2 * pair + 2])
+            src = wo_raw[n][:].rearrange("p j (m t) -> p m j t", t=PACK)
+            copy(dst[:, :, 2 * n : 2 * n + 2, :], src[:, :, :, 2 * pair : 2 * pair + 2])
 
         def quantise_wo(pair):
             quantise(wo_codes[pair][:], wo_scales[pair][:], woven[pair], E4M3)
@@ -112,27 +113,29 @@ def tile_attend_ghsort_sig_kernel(tc, wo, dyT, W, h, offs, out):
 
         def make_u(n):
             cols = slice(HALF * n, HALF * (n + 1))
-            for t in (2, 3, 0, 1):
+            for t in PLANE_ORDER:
                 words = slice(P * (t % 2), P * (t % 2 + 1))
                 multiply(u_acc[t][:, cols], wo_codes[t // 2][:, words], wo_scales[t // 2][:, words], dy_codes[n][:], dy_scales[n][:])
                 nc.scalar.copy(out=u[t][:, cols], in_=u_acc[t][:, cols])
 
-        weave_wo(nc.vector.tensor_copy, 0)
-        weave_wo(nc.scalar.copy, 1)
+        for n in range(2):
+            weave_wo(nc.vector.tensor_copy, 0, n)
+            weave_wo(nc.scalar.copy, 1, n)
         quantise_wo(0)
-        quantise_wo(1)
         weave_dy(0)
+        quantise_wo(1)
         quantise_dy(0)
         weave_dy(1)
         make_u(0)
+        make_one_minus_h(factor[:, 1, :], h_plane[1])
         quantise_dy(1)
         make_u(1)
-        nc.vector.tensor_scalar(
-            out=factor[:, 2, 0:LAST], in0=arena[:, 0:LAST], scalar1=-1.0, scalar2=1.0, op0=ALU.mult, op1=ALU.add
-        )
-        make_neg_slope(factor_flat[:, 2 * S + LAST :], arena[:, LAST : 2 * S])
+        make_one_minus_h(factor[:, 2, 0:P], h_plane[2][:, 0:P])
+        make_neg_slope(factor[:, 2, P:S], h_plane[2][:, P:S])
+        make_neg_slope(factor[:, 3, :], h_plane[3])
+        make_neg_slope(factor[:, 0, :], h_plane[0])
 
-        w_bf = sbuf([P, S, PACK], BF16, "w_bf", "wo_raw")
+        w_bf = sbuf([P, S, PACK], BF16, "w_bf", "wo_raw1")
         w_codes = sbuf([P, S], U32, "w_codes")
         w_scales = sbuf([P, S], U8, "w_scales")
 
@@ -141,9 +144,10 @@ def tile_attend_ghsort_sig_kernel(tc, wo, dyT, W, h, offs, out):
             quantise(w_codes[:, cols], w_scales[:, cols], w_bf[:, cols, :].rearrange("p c j -> p (c j)"), E4M3)
 
         picked = sbuf([P, PACK, S], F32, "picked")
-        dz_bf = w_flat[:, 2 * S :].bitcast(BF16).rearrange("p (c j) -> p c j", j=PACK)
-        dz_codes = [sbuf([P, HALF], U32, "dz_codes%d" % n) for n in range(2)]
-        dz_scales = [sbuf([P, HALF], U8, "dz_scales%d" % n) for n in range(2)]
+        after_w = sbuf([P, 5 * HALF], F32, "after_w", "w_raw")
+        dz_bf = after_w[:, 0 : 2 * S].bitcast(BF16).rearrange("p (c j) -> p c j", j=PACK)
+        dz_codes = {first: sbuf([P, end - first], U32, "dz_codes%d" % first) for first, end in RUNS}
+        dz_scales = {first: sbuf([P, end - first], U8, "dz_scales%d" % first) for first, end in RUNS}
 
         def gather_on_scalar(first, end, planes):
             for t in planes:
@@ -158,7 +162,7 @@ def tile_attend_ghsort_sig_kernel(tc, wo, dyT, W, h, offs, out):
             nc.vector.tensor_tensor(
                 out=picked[:, t, first:end],
                 in0=u[t][:].indirect(offsets[:, first // LIST_ROWS : end // LIST_ROWS]),
-                in1=h_flat(S * t + first, S * t + end),
+                in1=h_plane[t][:, first:end],
                 op=ALU.mult,
             )
 
@@ -171,38 +175,42 @@ def tile_attend_ghsort_sig_kernel(tc, wo, dyT, W, h, offs, out):
             )
 
         def quantise_dz(first, end):
-            words = slice(first % HALF, first % HALF + end - first)
             woven_dz = dz_bf[:, first:end, :].rearrange("p c j -> p (c j)")
-            quantise(dz_codes[first // HALF][:, words], dz_scales[first // HALF][:, words], woven_dz, E5M2)
+            quantise(dz_codes[first][:], dz_scales[first][:], woven_dz, E5M2)
 
-        def close(n, pair, banks, copies):
-            result = keep.tile([P, 2, HALF], F32, name="result%d_%d" % (n, pair))
-            per_bank = 2 // len(banks)
+        def close(first, end, quarters, banks, copies):
+            if first == MIDDLE:
+                result = as_planes(after_w[:, 3 * HALF : 5 * HALF])
+            else:
+                result = keep.tile([P, len(quarters), end - first], F32, name="result%d_%d" % (first, quarters[0]))[:]
+            per_bank = len(quarters) // len(banks)
             for b, bank in enumerate(banks):
-                acc = psum.tile([P, per_bank, HALF], F32, name="acc%d_%d_%d" % (n, pair, b), tag=bank)
+                acc = psum.tile([P, per_bank, end - first], F32, name="acc%d_%d_%d" % (first, quarters[0], b), tag=bank)
                 for k in range(per_bank):
-                    q = 2 * pair + b * per_bank + k
+                    q = quarters[b * per_bank + k]
                     cols = slice(P * q, P * (q + 1))
-                    multiply(acc[:, k, :], w_codes[:, cols], w_scales[:, cols], dz_codes[n][:], dz_scales[n][:])
+                    multiply(acc[:, k, :], w_codes[:, cols], w_scales[:, cols], dz_codes[first][:], dz_scales[first][:])
                 copies[b](result[:, b * per_bank : (b + 1) * per_bank, :], acc[:])
-            block = out[HALF * pair : HALF * (pair + 1), HALF * n : HALF * (n + 1)]
-            nc.sync.dma_start(out=block.rearrange("(q p) c -> p q c", p=P), in_=result[:])
+            block = out[P * quarters[0] : P * (quarters[-1] + 1), first:end]
+            nc.sync.dma_start(out=block.rearrange("(q p) c -> p q c", p=P), in_=result)
 
-        gather_on_vector(0, LAST, 2)
-        make_neg_slope(factor_flat[:, 0 : 2 * S], h_low[:])
-        gather_on_scalar(0, MIDDLE, (3, 0, 1))
-        nc.vector.tensor_copy(*weave_views(w_bf[:], w_raw))
-        gather_on_scalar(MIDDLE, LAST, (3, 0, 1))
-        gather_on_scalar(LAST, S, range(PACK))
+        gather_on_vector(0, MIDDLE, 1)
+        gather_on_vector(0, P, 2)
+        gather_on_vector(MIDDLE, S, 1)
+        gather_on_scalar(P, MIDDLE, (2,))
+        for first, end in RUNS:
+            gather_on_scalar(first, end, (3, 0) if first == 0 else (2, 3, 0))
+        nc.vector.tensor_copy(*weave_views(w_bf[:], w_raw[:]))
         weave_dz(0, MIDDLE)
         quantise_w(0)
         quantise_dz(0, MIDDLE)
-        close(0, 0, ("out0",), (nc.scalar.copy,))
-        quantise_w(1)
-        close(0, 1, ("out1",), (nc.scalar.copy,))
+        close(0, MIDDLE, (0, 1), ("out0",), (nc.scalar.copy,))
         weave_dz(MIDDLE, LAST)
-        weave_dz(LAST, S)
+        quantise_w(1)
+        close(0, MIDDLE, (2, 3), ("out1",), (nc.scalar.copy,))
         quantise_dz(MIDDLE, LAST)
+        weave_dz(LAST, S)
         quantise_dz(LAST, S)
-        close(1, 0, ("u_acc0", "u_acc1"), (nc.vector.tensor_copy, nc.scalar.copy))
-        close(1, 1, ("u_acc2", "u_acc3"), (nc.vector.tensor_copy, nc.scalar.copy))
+        close(MIDDLE, LAST, (0, 1, 2, 3), ("out2", "out3"), (nc.vector.tensor_copy, nc.scalar.copy))
+        close(LAST, S, (0, 1), ("u_acc0",), (nc.vector.tensor_copy,))
+        close(LAST, S, (2, 3), ("u_acc1",), (nc.scalar.copy,))

@@ -19,12 +19,13 @@ E5M2 = mybir.dt.float8_e5m2_x4
 ALU = mybir.AluOpType
 COPY = mybir.ActivationFunctionType.Copy
 
-DY_ON_VECTOR = 168
-OVERLAP = 64
 MIDDLE = HALF
-PLANE_ORDER = (1, 2, 3, 0)
 LAST = HALF + P
 RUNS = ((0, MIDDLE), (MIDDLE, LAST), (LAST, S))
+PLANE_ORDER = (3, 2, 1, 0)
+DY_ON_VECTOR = 168
+W_ON_VECTOR = 416
+OVERLAP = 64
 
 
 def weave_views(dst, src):
@@ -64,20 +65,25 @@ def tile_attend_ghsort_sig_kernel(tc, wo, dyT, W, h, offs, out):
         wo_raw = [sbuf([P, 2, S], F32, "wo_raw%d" % n) for n in range(2)]
         for n in range(2):
             nc.sync.dma_start(out=wo_raw[n][:], in_=rows(wo)[:, 2 * n : 2 * n + 2, :])
-        arena = sbuf([P, 2 * S - OVERLAP + PACK * S], F32, "arena")
-        factor_flat = arena[:, 2 * S - OVERLAP :]
-        factor = as_planes(factor_flat)
-        dy_raw = (sbuf([P, PACK, HALF], F32, "dy_raw0")[:], as_planes(factor_flat[:, OVERLAP : OVERLAP + 2 * S]))
+
+        factor_start = S - OVERLAP
+        arena = sbuf([P, (PACK + 2) * S], F32, "arena")
+        factor = as_planes(arena[:, factor_start : factor_start + PACK * S])
+        second_woven_start = factor_start + 2 * S - OVERLAP
+        dy_raw = (sbuf([P, PACK, HALF], F32, "dy_raw0")[:], as_planes(arena[:, PACK * S :]))
         for n in range(2):
             nc.sync.dma_start(out=dy_raw[n], in_=rows(dyT)[:, :, HALF * n : HALF * (n + 1)])
-        h_outer = keep.tile([P, 2, S], F32, name="h_outer")
-        h_plane = (h_outer[:, 0, :], arena[:, 0:S], arena[:, S : 2 * S], h_outer[:, 1, :])
+        h_rest = keep.tile([P, 3, S], F32, name="h_rest")
+        h_plane = (h_rest[:, 0, :], h_rest[:, 1, :], arena[:, 0:S], h_rest[:, 2, :])
         for t in PLANE_ORDER:
             nc.sync.dma_start(out=h_plane[t], in_=rows(h)[:, t, :])
         offsets = keep.tile([P, S // LIST_ROWS], U16, name="offsets")
         nc.sync.dma_start(offsets[:], offs)
-        w_raw = sbuf([P, PACK, S], F32, "w_raw")
-        nc.sync.dma_start(out=w_raw[:], in_=rows(W))
+
+        w_start = S - OVERLAP
+        w_stage = sbuf([P, w_start + (PACK + 1) * S], F32, "w_stage")
+        w_raw = as_planes(w_stage[:, w_start : w_start + PACK * S])
+        nc.sync.dma_start(out=w_raw, in_=rows(W))
 
         def make_neg_slope(dst, part):
             nc.vector.scalar_tensor_tensor(out=dst, in0=part, scalar=1.0, in1=part, op0=ALU.subtract, op1=ALU.mult)
@@ -87,7 +93,8 @@ def tile_attend_ghsort_sig_kernel(tc, wo, dyT, W, h, offs, out):
 
         wo_codes = [sbuf([P, HALF], U32, "wo_codes0"), sbuf([P, HALF], U32, "wo_codes1", "wo_raw1")]
         wo_scales = [sbuf([P, HALF], U8, "wo_scales%d" % pair) for pair in range(2)]
-        woven = (sbuf([P, 2 * S], BF16, "woven0")[:], factor_flat[:, 2 * S + P - 32 : 3 * S + P - 32].bitcast(BF16))
+        first_woven = sbuf([P, 2 * S], BF16, "woven0")
+        woven = (first_woven[:], arena[:, second_woven_start : second_woven_start + S].bitcast(BF16))
 
         def weave_wo(copy, pair, n):
             dst = woven[pair].rearrange("p (t m j) -> p m j t", t=2, j=PACK)
@@ -115,7 +122,8 @@ def tile_attend_ghsort_sig_kernel(tc, wo, dyT, W, h, offs, out):
             cols = slice(HALF * n, HALF * (n + 1))
             for t in PLANE_ORDER:
                 words = slice(P * (t % 2), P * (t % 2 + 1))
-                multiply(u_acc[t][:, cols], wo_codes[t // 2][:, words], wo_scales[t // 2][:, words], dy_codes[n][:], dy_scales[n][:])
+                codes, scales = wo_codes[t // 2][:, words], wo_scales[t // 2][:, words]
+                multiply(u_acc[t][:, cols], codes, scales, dy_codes[n][:], dy_scales[n][:])
                 nc.scalar.copy(out=u[t][:, cols], in_=u_acc[t][:, cols])
 
         for n in range(2):
@@ -127,12 +135,12 @@ def tile_attend_ghsort_sig_kernel(tc, wo, dyT, W, h, offs, out):
         quantise_dy(0)
         weave_dy(1)
         make_u(0)
-        make_one_minus_h(factor[:, 1, :], h_plane[1])
+        make_one_minus_h(factor[:, 3, :], h_plane[3])
         quantise_dy(1)
         make_u(1)
         make_one_minus_h(factor[:, 2, 0:P], h_plane[2][:, 0:P])
         make_neg_slope(factor[:, 2, P:S], h_plane[2][:, P:S])
-        make_neg_slope(factor[:, 3, :], h_plane[3])
+        make_neg_slope(factor[:, 1, :], h_plane[1])
         make_neg_slope(factor[:, 0, :], h_plane[0])
 
         w_bf = sbuf([P, S, PACK], BF16, "w_bf", "wo_raw1")
@@ -143,16 +151,24 @@ def tile_attend_ghsort_sig_kernel(tc, wo, dyT, W, h, offs, out):
             cols = slice(HALF * n, HALF * (n + 1))
             quantise(w_codes[:, cols], w_scales[:, cols], w_bf[:, cols, :].rearrange("p c j -> p (c j)"), E4M3)
 
-        picked = sbuf([P, PACK, S], F32, "picked")
-        after_w = sbuf([P, 5 * HALF], F32, "after_w", "w_raw")
-        dz_bf = after_w[:, 0 : 2 * S].bitcast(BF16).rearrange("p (c j) -> p c j", j=PACK)
+        first_runs = sbuf([P, PACK, LAST], F32, "first_runs")
+        last_run = as_planes(w_stage[:, w_start + S :])
+
+        def picked(planes, first, end):
+            return last_run[:, planes, first:end] if first >= LAST else first_runs[:, planes, first:end]
+
+        dz_bf = {
+            0: w_stage[:, 0:S].bitcast(BF16),
+            MIDDLE: w_raw[:, 1, 0:HALF].bitcast(BF16),
+            LAST: w_raw[:, 2, 0:HALF].bitcast(BF16),
+        }
         dz_codes = {first: sbuf([P, end - first], U32, "dz_codes%d" % first) for first, end in RUNS}
         dz_scales = {first: sbuf([P, end - first], U8, "dz_scales%d" % first) for first, end in RUNS}
 
         def gather_on_scalar(first, end, planes):
             for t in planes:
                 nc.scalar.activation(
-                    out=picked[:, t, first:end],
+                    out=picked(t, first, end),
                     in_=u[t][:].indirect(offsets[:, first // LIST_ROWS : end // LIST_ROWS]),
                     func=COPY,
                     scale=-1.0,
@@ -160,7 +176,7 @@ def tile_attend_ghsort_sig_kernel(tc, wo, dyT, W, h, offs, out):
 
         def gather_on_vector(first, end, t):
             nc.vector.tensor_tensor(
-                out=picked[:, t, first:end],
+                out=picked(t, first, end),
                 in0=u[t][:].indirect(offsets[:, first // LIST_ROWS : end // LIST_ROWS]),
                 in1=h_plane[t][:, first:end],
                 op=ALU.mult,
@@ -168,19 +184,18 @@ def tile_attend_ghsort_sig_kernel(tc, wo, dyT, W, h, offs, out):
 
         def weave_dz(first, end):
             nc.vector.tensor_tensor(
-                out=dz_bf[:, first:end, :].rearrange("p (c n) j -> p c j n", n=2),
-                in0=picked[:, :, first:end].rearrange("p j (c n) -> p c j n", n=2),
+                out=dz_bf[first].rearrange("p (c n j) -> p c j n", n=2, j=PACK),
+                in0=picked(slice(0, PACK), first, end).rearrange("p j (c n) -> p c j n", n=2),
                 in1=factor[:, :, first:end].rearrange("p j (c n) -> p c j n", n=2),
                 op=ALU.mult,
             )
 
-        def quantise_dz(first, end):
-            woven_dz = dz_bf[:, first:end, :].rearrange("p c j -> p (c j)")
-            quantise(dz_codes[first][:], dz_scales[first][:], woven_dz, E5M2)
+        def quantise_dz(first):
+            quantise(dz_codes[first][:], dz_scales[first][:], dz_bf[first], E5M2)
 
         def close(first, end, quarters, banks, copies):
             if first == MIDDLE:
-                result = as_planes(after_w[:, 3 * HALF : 5 * HALF])
+                result = as_planes(w_stage[:, w_start + 3 * S + HALF : w_start + 4 * S + HALF])
             else:
                 result = keep.tile([P, len(quarters), end - first], F32, name="result%d_%d" % (first, quarters[0]))[:]
             per_bank = len(quarters) // len(banks)
@@ -194,23 +209,27 @@ def tile_attend_ghsort_sig_kernel(tc, wo, dyT, W, h, offs, out):
             block = out[P * quarters[0] : P * (quarters[-1] + 1), first:end]
             nc.sync.dma_start(out=block.rearrange("(q p) c -> p q c", p=P), in_=result)
 
-        gather_on_vector(0, MIDDLE, 1)
+        gather_on_vector(0, LAST, 3)
         gather_on_vector(0, P, 2)
-        gather_on_vector(MIDDLE, S, 1)
+        gather_on_vector(LAST, S, 3)
         gather_on_scalar(P, MIDDLE, (2,))
-        for first, end in RUNS:
-            gather_on_scalar(first, end, (3, 0) if first == 0 else (2, 3, 0))
-        nc.vector.tensor_copy(*weave_views(w_bf[:], w_raw[:]))
+        gather_on_scalar(0, MIDDLE, (1, 0))
+        gather_on_scalar(MIDDLE, LAST, (2, 1, 0))
+        nc.vector.tensor_copy(*weave_views(w_bf[:, 0:W_ON_VECTOR, :], w_raw[:, :, 0:W_ON_VECTOR]))
+        nc.scalar.copy(*weave_views(w_bf[:, W_ON_VECTOR:S, :], w_raw[:, :, W_ON_VECTOR:S]))
+        gather_on_scalar(LAST, S, (2, 1, 0))
+
         weave_dz(0, MIDDLE)
         quantise_w(0)
-        quantise_dz(0, MIDDLE)
+        quantise_dz(0)
         close(0, MIDDLE, (0, 1), ("out0",), (nc.scalar.copy,))
         weave_dz(MIDDLE, LAST)
         quantise_w(1)
-        close(0, MIDDLE, (2, 3), ("out1",), (nc.scalar.copy,))
-        quantise_dz(MIDDLE, LAST)
+        close(0, MIDDLE, (2,), ("out1",), (nc.scalar.copy,))
+        close(0, MIDDLE, (3,), ("u_acc2",), (nc.scalar.copy,))
+        quantise_dz(MIDDLE)
         weave_dz(LAST, S)
-        quantise_dz(LAST, S)
+        quantise_dz(LAST)
         close(MIDDLE, LAST, (0, 1, 2, 3), ("out2", "out3"), (nc.vector.tensor_copy, nc.scalar.copy))
-        close(LAST, S, (0, 1), ("u_acc0",), (nc.vector.tensor_copy,))
-        close(LAST, S, (2, 3), ("u_acc1",), (nc.scalar.copy,))
+        close(LAST, S, (0, 1), ("u_acc0", "u_acc1"), (nc.scalar.copy, nc.vector.tensor_copy))
+        close(LAST, S, (2, 3), ("u_acc3", "out0"), (nc.scalar.copy, nc.vector.tensor_copy))

@@ -22,7 +22,7 @@ COPY = mybir.ActivationFunctionType.Copy
 MIDDLE = HALF
 LAST = HALF + P
 RUNS = ((0, MIDDLE), (MIDDLE, LAST), (LAST, S))
-PLANE_ORDER = (3, 2, 1, 0)
+PLANE_ORDER = (3, 2, 0, 1)
 DY_ON_VECTOR = 168
 W_ON_VECTOR = 416
 OVERLAP = 64
@@ -66,18 +66,18 @@ def tile_attend_ghsort_sig_kernel(tc, wo, dyT, W, h, offs, out):
         for n in range(2):
             nc.sync.dma_start(out=wo_raw[n][:], in_=rows(wo)[:, 2 * n : 2 * n + 2, :])
 
-        factor_start = S - OVERLAP
-        arena = sbuf([P, (PACK + 2) * S], F32, "arena")
-        factor = as_planes(arena[:, factor_start : factor_start + PACK * S])
-        second_woven_start = factor_start + 2 * S - OVERLAP
-        dy_raw = (sbuf([P, PACK, HALF], F32, "dy_raw0")[:], as_planes(arena[:, PACK * S :]))
+        dy_raw = [sbuf([P, PACK, HALF], F32, "dy_raw%d" % n) for n in range(2)]
         for n in range(2):
-            nc.sync.dma_start(out=dy_raw[n], in_=rows(dyT)[:, :, HALF * n : HALF * (n + 1)])
+            nc.sync.dma_start(out=dy_raw[n][:], in_=rows(dyT)[:, :, HALF * n : HALF * (n + 1)])
+
+        arena = sbuf([P, PACK * S], F32, "arena")
+        factor = as_planes(arena[:])
+        h_first = 3 * S - OVERLAP
         h_rest = keep.tile([P, 3, S], F32, name="h_rest")
-        h_plane = (h_rest[:, 0, :], h_rest[:, 1, :], arena[:, 0:S], h_rest[:, 2, :])
-        for t in PLANE_ORDER:
-            nc.sync.dma_start(out=h_plane[t], in_=rows(h)[:, t, :])
+        h_plane = (arena[:, h_first : h_first + S], h_rest[:, 0, :], h_rest[:, 1, :], h_rest[:, 2, :])
         offsets = keep.tile([P, S // LIST_ROWS], U16, name="offsets")
+        for t in range(PACK):
+            nc.sync.dma_start(out=h_plane[t], in_=rows(h)[:, t, :])
         nc.sync.dma_start(offsets[:], offs)
 
         w_start = S - OVERLAP
@@ -94,7 +94,7 @@ def tile_attend_ghsort_sig_kernel(tc, wo, dyT, W, h, offs, out):
         wo_codes = [sbuf([P, HALF], U32, "wo_codes0"), sbuf([P, HALF], U32, "wo_codes1", "wo_raw1")]
         wo_scales = [sbuf([P, HALF], U8, "wo_scales%d" % pair) for pair in range(2)]
         first_woven = sbuf([P, 2 * S], BF16, "woven0")
-        woven = (first_woven[:], arena[:, second_woven_start : second_woven_start + S].bitcast(BF16))
+        woven = (first_woven[:], arena[:, HALF : HALF + S].bitcast(BF16))
 
         def weave_wo(copy, pair, n):
             dst = woven[pair].rearrange("p (t m j) -> p m j t", t=2, j=PACK)
@@ -107,13 +107,14 @@ def tile_attend_ghsort_sig_kernel(tc, wo, dyT, W, h, offs, out):
         dy_codes = [sbuf([P, HALF], U32, "dy_codes%d" % n) for n in range(2)]
         dy_scales = [sbuf([P, HALF], U8, "dy_scales%d" % n) for n in range(2)]
 
-        def weave_dy(n):
+        def weave_dy(copy, n, first, end):
             dy_bf = woven[n].rearrange("p (c j) -> p c j", j=PACK)
-            nc.vector.tensor_copy(*weave_views(dy_bf[:, 0:DY_ON_VECTOR, :], dy_raw[n][:, :, 0:DY_ON_VECTOR]))
-            nc.scalar.copy(*weave_views(dy_bf[:, DY_ON_VECTOR:HALF, :], dy_raw[n][:, :, DY_ON_VECTOR:HALF]))
+            copy(*weave_views(dy_bf[:, first:end, :], dy_raw[n][:, :, first:end]))
 
-        def quantise_dy(n):
-            quantise(dy_codes[n][:], dy_scales[n][:], woven[n], E5M2)
+        def quantise_dy(n, first, end):
+            quantise(
+                dy_codes[n][:, first:end], dy_scales[n][:, first:end], woven[n][:, PACK * first : PACK * end], E5M2
+            )
 
         u_acc = [psum.tile([P, S], F32, name="u_acc%d" % t) for t in range(PACK)]
         u = [sbuf([P, S], F32, "u%d" % t) for t in range(PACK)]
@@ -130,18 +131,22 @@ def tile_attend_ghsort_sig_kernel(tc, wo, dyT, W, h, offs, out):
             weave_wo(nc.vector.tensor_copy, 0, n)
             weave_wo(nc.scalar.copy, 1, n)
         quantise_wo(0)
-        weave_dy(0)
+        weave_dy(nc.vector.tensor_copy, 0, 0, DY_ON_VECTOR)
+        weave_dy(nc.scalar.copy, 0, DY_ON_VECTOR, HALF)
         quantise_wo(1)
-        quantise_dy(0)
-        weave_dy(1)
+        quantise_dy(0, 0, HALF)
+        weave_dy(nc.vector.tensor_copy, 1, 0, P)
+        weave_dy(nc.vector.tensor_copy, 1, P, DY_ON_VECTOR)
+        weave_dy(nc.scalar.copy, 1, DY_ON_VECTOR, HALF)
         make_u(0)
-        make_one_minus_h(factor[:, 3, :], h_plane[3])
-        quantise_dy(1)
+        quantise_dy(1, 0, P)
+        quantise_dy(1, P, HALF)
         make_u(1)
-        make_one_minus_h(factor[:, 2, 0:P], h_plane[2][:, 0:P])
-        make_neg_slope(factor[:, 2, P:S], h_plane[2][:, P:S])
-        make_neg_slope(factor[:, 1, :], h_plane[1])
         make_neg_slope(factor[:, 0, :], h_plane[0])
+        make_neg_slope(factor[:, 1, :], h_plane[1])
+        make_neg_slope(factor[:, 2, P:S], h_plane[2][:, P:S])
+        make_one_minus_h(factor[:, 2, 0:P], h_plane[2][:, 0:P])
+        make_one_minus_h(factor[:, 3, :], h_plane[3])
 
         w_bf = sbuf([P, S, PACK], BF16, "w_bf", "wo_raw1")
         w_codes = sbuf([P, S], U32, "w_codes")

@@ -66,13 +66,13 @@ def tile_attend_ghsort_sig_kernel(tc, wo, dyT, W, h, offs, out):
         for n in range(2):
             nc.sync.dma_start(out=wo_raw[n][:], in_=rows(wo)[:, 2 * n : 2 * n + 2, :])
 
-        dy_raw = [sbuf([P, PACK, HALF], F32, "dy_raw%d" % n) for n in range(2)]
+        factor_start = S - OVERLAP
+        arena = sbuf([P, (PACK + 3) * S], F32, "arena")
+        factor = as_planes(arena[:, factor_start : factor_start + PACK * S])
+        dy_raw = (sbuf([P, PACK, HALF], F32, "dy_raw0")[:], as_planes(arena[:, (PACK + 1) * S :]))
         for n in range(2):
-            nc.sync.dma_start(out=dy_raw[n][:], in_=rows(dyT)[:, :, HALF * n : HALF * (n + 1)])
-
-        arena = sbuf([P, PACK * S], F32, "arena")
-        factor = as_planes(arena[:])
-        h_first = 3 * S - OVERLAP
+            nc.sync.dma_start(out=dy_raw[n], in_=rows(dyT)[:, :, HALF * n : HALF * (n + 1)])
+        h_first = factor_start + 3 * S - OVERLAP
         h_rest = keep.tile([P, 3, S], F32, name="h_rest")
         h_plane = (arena[:, h_first : h_first + S], h_rest[:, 0, :], h_rest[:, 1, :], h_rest[:, 2, :])
         offsets = keep.tile([P, S // LIST_ROWS], U16, name="offsets")
@@ -94,7 +94,7 @@ def tile_attend_ghsort_sig_kernel(tc, wo, dyT, W, h, offs, out):
         wo_codes = [sbuf([P, HALF], U32, "wo_codes0"), sbuf([P, HALF], U32, "wo_codes1", "wo_raw1")]
         wo_scales = [sbuf([P, HALF], U8, "wo_scales%d" % pair) for pair in range(2)]
         first_woven = sbuf([P, 2 * S], BF16, "woven0")
-        woven = (first_woven[:], arena[:, HALF : HALF + S].bitcast(BF16))
+        woven = (first_woven[:], arena[:, factor_start + HALF : factor_start + HALF + S].bitcast(BF16))
 
         def weave_wo(copy, pair, n):
             dst = woven[pair].rearrange("p (t m j) -> p m j t", t=2, j=PACK)

@@ -1,3 +1,4 @@
+import math
 from contextlib import ExitStack
 
 import concourse.mybir as mybir
@@ -26,6 +27,8 @@ PLANE_ORDER = (3, 2, 0, 1)
 DY_ON_VECTOR = 168
 W_ON_VECTOR = 416
 OVERLAP = 64
+BURST = 256
+BYTES_OF = {F32: 4, U32: 4, BF16: 2, U8: 1}
 
 
 def weave_views(dst, src):
@@ -40,10 +43,18 @@ def tile_attend_ghsort_sig_kernel(tc, wo, dyT, W, h, offs, out):
     nc = tc.nc
     with ExitStack() as ctx:
         keep = ctx.enter_context(tc.tile_pool(name="keep", bufs=1))
+        work = ctx.enter_context(tc.tile_pool(name="work", bufs=1))
         psum = ctx.enter_context(tc.psum_pool(name="psum", bufs=1))
+        starts = {}
+        filled = [0]
 
-        def sbuf(shape, dtype, name, reuse=None):
-            return keep.tile(shape, dtype, name=name, tag=reuse or name, align_bytes=64)
+        def sbuf(shape, dtype, name, phase=0, reuse=None):
+            if reuse is None:
+                start = -(-filled[0] // BURST) * BURST
+                filled[0] = start + BURST + math.prod(shape[1:]) * BYTES_OF[dtype]
+                starts[name] = start
+            align = BURST if phase == 0 else 64
+            return work.tile(shape, dtype, name=name, align_bytes=align, offset=starts[reuse or name] + phase)
 
         def quantise(codes, scales, woven, fmt):
             nc.vector.quantize_mx(out=codes.bitcast(fmt), scales=scales, in_=woven)
@@ -66,14 +77,14 @@ def tile_attend_ghsort_sig_kernel(tc, wo, dyT, W, h, offs, out):
         for n in range(2):
             nc.sync.dma_start(out=wo_raw[n][:], in_=rows(wo)[:, 2 * n : 2 * n + 2, :])
 
-        factor_start = S - OVERLAP
-        arena = sbuf([P, (PACK + 3) * S], F32, "arena")
+        factor_start = BURST // 8
+        arena = sbuf([P, factor_start + PACK * S], F32, "arena")
         factor = as_planes(arena[:, factor_start : factor_start + PACK * S])
-        dy_raw = (sbuf([P, PACK, HALF], F32, "dy_raw0")[:], as_planes(arena[:, (PACK + 1) * S :]))
+        dy_raw = [sbuf([P, PACK, HALF], F32, "dy_raw%d" % n)[:] for n in range(2)]
         for n in range(2):
             nc.sync.dma_start(out=dy_raw[n], in_=rows(dyT)[:, :, HALF * n : HALF * (n + 1)])
-        h_first = factor_start + 3 * S - OVERLAP
-        h_rest = keep.tile([P, 3, S], F32, name="h_rest")
+        h_first = 3 * S - OVERLAP
+        h_rest = sbuf([P, 3, S], F32, "h_rest")
         h_plane = (arena[:, h_first : h_first + S], h_rest[:, 0, :], h_rest[:, 1, :], h_rest[:, 2, :])
         offsets = keep.tile([P, S // LIST_ROWS], U16, name="offsets")
         for t in range(PACK):
@@ -91,9 +102,9 @@ def tile_attend_ghsort_sig_kernel(tc, wo, dyT, W, h, offs, out):
         def make_one_minus_h(dst, part):
             nc.vector.tensor_scalar(out=dst, in0=part, scalar1=-1.0, scalar2=1.0, op0=ALU.mult, op1=ALU.add)
 
-        wo_codes = [sbuf([P, HALF], U32, "wo_codes0"), sbuf([P, HALF], U32, "wo_codes1", "wo_raw1")]
-        wo_scales = [sbuf([P, HALF], U8, "wo_scales%d" % pair) for pair in range(2)]
-        first_woven = sbuf([P, 2 * S], BF16, "woven0")
+        wo_codes = [sbuf([P, HALF], U32, "wo_codes0", 128), sbuf([P, HALF], U32, "wo_codes1", 192, "wo_raw1")]
+        wo_scales = [sbuf([P, HALF], U8, "wo_scales%d" % pair, 128 + 64 * pair) for pair in range(2)]
+        first_woven = sbuf([P, 2 * S], BF16, "woven0", 192)
         woven = (first_woven[:], arena[:, factor_start + HALF : factor_start + HALF + S].bitcast(BF16))
 
         def weave_wo(copy, pair, n):
@@ -105,7 +116,7 @@ def tile_attend_ghsort_sig_kernel(tc, wo, dyT, W, h, offs, out):
             quantise(wo_codes[pair][:], wo_scales[pair][:], woven[pair], E4M3)
 
         dy_codes = [sbuf([P, HALF], U32, "dy_codes%d" % n) for n in range(2)]
-        dy_scales = [sbuf([P, HALF], U8, "dy_scales%d" % n) for n in range(2)]
+        dy_scales = [sbuf([P, HALF], U8, "dy_scales%d" % n, 64) for n in range(2)]
 
         def weave_dy(copy, n, first, end):
             dy_bf = woven[n].rearrange("p (c j) -> p c j", j=PACK)
@@ -117,7 +128,7 @@ def tile_attend_ghsort_sig_kernel(tc, wo, dyT, W, h, offs, out):
             )
 
         u_acc = [psum.tile([P, S], F32, name="u_acc%d" % t) for t in range(PACK)]
-        u = [sbuf([P, S], F32, "u%d" % t) for t in range(PACK)]
+        u = [sbuf([P, S], F32, "u%d" % t, 128 + 64 * (t // 2)) for t in range(PACK)]
 
         def make_u(n):
             cols = slice(HALF * n, HALF * (n + 1))
@@ -148,7 +159,7 @@ def tile_attend_ghsort_sig_kernel(tc, wo, dyT, W, h, offs, out):
         make_one_minus_h(factor[:, 2, 0:P], h_plane[2][:, 0:P])
         make_one_minus_h(factor[:, 3, :], h_plane[3])
 
-        w_bf = sbuf([P, S, PACK], BF16, "w_bf", "wo_raw1")
+        w_bf = sbuf([P, S, PACK], BF16, "w_bf", 128, "wo_raw1")
         w_codes = sbuf([P, S], U32, "w_codes")
         w_scales = sbuf([P, S], U8, "w_scales")
 
@@ -167,8 +178,8 @@ def tile_attend_ghsort_sig_kernel(tc, wo, dyT, W, h, offs, out):
             MIDDLE: w_raw[:, 1, 0:HALF].bitcast(BF16),
             LAST: w_raw[:, 2, 0:HALF].bitcast(BF16),
         }
-        dz_codes = {first: sbuf([P, end - first], U32, "dz_codes%d" % first) for first, end in RUNS}
-        dz_scales = {first: sbuf([P, end - first], U8, "dz_scales%d" % first) for first, end in RUNS}
+        dz_codes = {first: sbuf([P, end - first], U32, "dz_codes%d" % first, 128 if first else 64) for first, end in RUNS}
+        dz_scales = {first: sbuf([P, end - first], U8, "dz_scales%d" % first, 128 if first == LAST else 192) for first, end in RUNS}
 
         def gather_on_scalar(first, end, planes):
             for t in planes:
@@ -202,7 +213,7 @@ def tile_attend_ghsort_sig_kernel(tc, wo, dyT, W, h, offs, out):
             if first == MIDDLE:
                 result = as_planes(w_stage[:, w_start + 3 * S + HALF : w_start + 4 * S + HALF])
             else:
-                result = keep.tile([P, len(quarters), end - first], F32, name="result%d_%d" % (first, quarters[0]))[:]
+                result = sbuf([P, len(quarters), end - first], F32, "result%d_%d" % (first, quarters[0]))[:]
             per_bank = len(quarters) // len(banks)
             for b, bank in enumerate(banks):
                 acc = psum.tile([P, per_bank, end - first], F32, name="acc%d_%d_%d" % (first, quarters[0], b), tag=bank)

@@ -25,7 +25,7 @@ LAST = HALF + P
 RUNS = ((0, MIDDLE), (MIDDLE, LAST), (LAST, S))
 PLANE_ORDER = (3, 2, 0, 1)
 DY_ON_VECTOR = 168
-W_ON_VECTOR = 416
+W_ON_VECTOR = 256
 OVERLAP = 64
 BURST = 256
 BYTES_OF = {F32: 4, U32: 4, BF16: 2, U8: 1}
@@ -209,21 +209,24 @@ def tile_attend_ghsort_sig_kernel(tc, wo, dyT, W, h, offs, out):
         def quantise_dz(first):
             quantise(dz_codes[first][:], dz_scales[first][:], dz_bf[first], E5M2)
 
-        def close(first, end, quarters, banks, copies):
-            if first == MIDDLE:
-                result = as_planes(w_stage[:, w_start + 3 * S + HALF : w_start + 4 * S + HALF])
-            else:
-                result = sbuf([P, len(quarters), end - first], F32, "result%d_%d" % (first, quarters[0]))[:]
-            per_bank = len(quarters) // len(banks)
-            for b, bank in enumerate(banks):
-                acc = psum.tile([P, per_bank, end - first], F32, name="acc%d_%d_%d" % (first, quarters[0], b), tag=bank)
-                for k in range(per_bank):
-                    q = quarters[b * per_bank + k]
-                    cols = slice(P * q, P * (q + 1))
-                    multiply(acc[:, k, :], w_codes[:, cols], w_scales[:, cols], dz_codes[first][:], dz_scales[first][:])
-                copies[b](result[:, b * per_bank : (b + 1) * per_bank, :], acc[:])
+        results = {
+            0: sbuf([P, PACK, MIDDLE], F32, "result_first")[:],
+            MIDDLE: as_planes(w_stage[:, w_start + 3 * S + HALF : w_start + 4 * S + HALF]),
+            LAST: sbuf([P, PACK, P], F32, "result_last")[:],
+        }
+
+        def close(first, end, quarters, bank, copy):
+            acc = psum.tile([P, len(quarters), end - first], F32, name="acc%d_%d" % (first, quarters[0]), tag=bank)
+            for k, q in enumerate(quarters):
+                cols = slice(P * q, P * (q + 1))
+                multiply(acc[:, k, :], w_codes[:, cols], w_scales[:, cols], dz_codes[first][:], dz_scales[first][:])
+            copy(results[first][:, quarters[0] : quarters[-1] + 1, :], acc[:])
+
+        def store(first, end, quarters):
             block = out[P * quarters[0] : P * (quarters[-1] + 1), first:end]
-            nc.sync.dma_start(out=block.rearrange("(q p) c -> p q c", p=P), in_=result)
+            nc.sync.dma_start(
+                out=block.rearrange("(q p) c -> p q c", p=P), in_=results[first][:, quarters[0] : quarters[-1] + 1, :]
+            )
 
         gather_on_vector(0, LAST, 3)
         gather_on_vector(0, P, 2)
@@ -238,14 +241,24 @@ def tile_attend_ghsort_sig_kernel(tc, wo, dyT, W, h, offs, out):
         weave_dz(0, MIDDLE)
         quantise_w(0)
         quantise_dz(0)
-        close(0, MIDDLE, (0, 1), ("out0",), (nc.scalar.copy,))
+        close(0, MIDDLE, (0,), "out0", nc.scalar.copy)
         weave_dz(MIDDLE, LAST)
         quantise_w(1)
-        close(0, MIDDLE, (2,), ("out1",), (nc.scalar.copy,))
-        close(0, MIDDLE, (3,), ("u_acc2",), (nc.scalar.copy,))
         quantise_dz(MIDDLE)
+        close(0, MIDDLE, (1,), "out1", nc.vector.tensor_copy)
+        store(0, MIDDLE, (0, 1))
+        close(0, MIDDLE, (2,), "u_acc2", nc.scalar.copy)
+        store(0, MIDDLE, (2,))
+        close(0, MIDDLE, (3,), "u_acc3", nc.scalar.copy)
+        store(0, MIDDLE, (3,))
         weave_dz(LAST, S)
         quantise_dz(LAST)
-        close(MIDDLE, LAST, (0, 1, 2, 3), ("out2", "out3"), (nc.vector.tensor_copy, nc.scalar.copy))
-        close(LAST, S, (0, 1), ("u_acc0", "u_acc1"), (nc.scalar.copy, nc.vector.tensor_copy))
-        close(LAST, S, (2, 3), ("u_acc3", "out0"), (nc.scalar.copy, nc.vector.tensor_copy))
+        close(MIDDLE, LAST, (0, 1), "out2", nc.vector.tensor_copy)
+        close(MIDDLE, LAST, (2, 3), "out3", nc.scalar.copy)
+        store(MIDDLE, LAST, (0, 1, 2, 3))
+        close(LAST, S, (0,), "u_acc0", nc.scalar.copy)
+        close(LAST, S, (1,), "u_acc1", nc.vector.tensor_copy)
+        store(LAST, S, (0, 1))
+        close(LAST, S, (2,), "out0", nc.scalar.copy)
+        close(LAST, S, (3,), "out1", nc.vector.tensor_copy)
+        store(LAST, S, (2, 3))

@@ -241,13 +241,12 @@ def tile_attend_ghsort_sig_kernel(tc, wo, dyT, W, h, offs, out):
         weave_dz(0, MIDDLE)
         quantise_w(0)
         quantise_dz(0)
-        close(0, MIDDLE, (0,), "out0", nc.scalar.copy)
+        close(0, MIDDLE, (0, 1), "out0", nc.scalar.copy)
+        store(0, MIDDLE, (0, 1))
         weave_dz(MIDDLE, LAST)
         quantise_w(1)
         quantise_dz(MIDDLE)
-        close(0, MIDDLE, (1,), "out1", nc.vector.tensor_copy)
-        store(0, MIDDLE, (0, 1))
-        close(0, MIDDLE, (2,), "u_acc2", nc.scalar.copy)
+        close(0, MIDDLE, (2,), "out1", nc.scalar.copy)
         store(0, MIDDLE, (2,))
         close(0, MIDDLE, (3,), "u_acc3", nc.scalar.copy)
         store(0, MIDDLE, (3,))

@@ -25,7 +25,6 @@ LAST = HALF + P
 RUNS = ((0, MIDDLE), (MIDDLE, LAST), (LAST, S))
 PLANE_ORDER = (3, 2, 0, 1)
 DY_ON_VECTOR = 168
-W_ON_VECTOR = 256
 OVERLAP = 64
 BURST = 256
 BYTES_OF = {F32: 4, U32: 4, BF16: 2, U8: 1}
@@ -73,9 +72,8 @@ def tile_attend_ghsort_sig_kernel(tc, wo, dyT, W, h, offs, out):
         def rows(matrix):
             return matrix.rearrange("(p j) c -> p j c", j=PACK)
 
-        wo_raw = [sbuf([P, 2, S], F32, "wo_raw%d" % n) for n in range(2)]
-        for n in range(2):
-            nc.sync.dma_start(out=wo_raw[n][:], in_=rows(wo)[:, 2 * n : 2 * n + 2, :])
+        wo_raw = sbuf([P, PACK, S], F32, "wo_raw")
+        nc.sync.dma_start(out=wo_raw[:], in_=rows(wo))
 
         factor_start = BURST // 8
         arena = sbuf([P, factor_start + PACK * S], F32, "arena")
@@ -92,9 +90,11 @@ def tile_attend_ghsort_sig_kernel(tc, wo, dyT, W, h, offs, out):
         nc.sync.dma_start(offsets[:], offs)
 
         w_start = S - OVERLAP
-        w_stage = sbuf([P, w_start + (PACK + 1) * S], F32, "w_stage")
-        w_raw = as_planes(w_stage[:, w_start : w_start + PACK * S])
-        nc.sync.dma_start(out=w_raw, in_=rows(W))
+        first_stage = sbuf([P, w_start + PACK * HALF], F32, "first_stage")
+        second_stage = sbuf([P, (PACK + 1) * HALF + P], F32, "second_stage")
+        w_raw = (as_planes(first_stage[:, w_start:]), as_planes(second_stage[:, 0 : PACK * HALF]))
+        for n in range(2):
+            nc.sync.dma_start(out=w_raw[n], in_=rows(W)[:, :, HALF * n : HALF * (n + 1)])
 
         def make_neg_slope(dst, part):
             nc.vector.scalar_tensor_tensor(out=dst, in0=part, scalar=1.0, in1=part, op0=ALU.subtract, op1=ALU.mult)
@@ -102,15 +102,14 @@ def tile_attend_ghsort_sig_kernel(tc, wo, dyT, W, h, offs, out):
         def make_one_minus_h(dst, part):
             nc.vector.tensor_scalar(out=dst, in0=part, scalar1=-1.0, scalar2=1.0, op0=ALU.mult, op1=ALU.add)
 
-        wo_codes = [sbuf([P, HALF], U32, "wo_codes0", 128), sbuf([P, HALF], U32, "wo_codes1", 192, "wo_raw1")]
+        wo_codes = [sbuf([P, HALF], U32, "wo_codes0", 128), sbuf([P, HALF], U32, "wo_codes1", 192, "wo_raw")]
         wo_scales = [sbuf([P, HALF], U8, "wo_scales%d" % pair, 128 + 64 * pair) for pair in range(2)]
         first_woven = sbuf([P, 2 * S], BF16, "woven0", 192)
         woven = (first_woven[:], arena[:, factor_start + HALF : factor_start + HALF + S].bitcast(BF16))
 
-        def weave_wo(copy, pair, n):
+        def weave_wo(copy, pair):
             dst = woven[pair].rearrange("p (t m j) -> p m j t", t=2, j=PACK)
-            src = wo_raw[n][:].rearrange("p j (m t) -> p m j t", t=PACK)
-            copy(dst[:, :, 2 * n : 2 * n + 2, :], src[:, :, :, 2 * pair : 2 * pair + 2])
+            copy(dst, wo_raw[:].rearrange("p j (m t) -> p m j t", t=PACK)[:, :, :, 2 * pair : 2 * pair + 2])
 
         def quantise_wo(pair):
             quantise(wo_codes[pair][:], wo_scales[pair][:], woven[pair], E4M3)
@@ -138,9 +137,8 @@ def tile_attend_ghsort_sig_kernel(tc, wo, dyT, W, h, offs, out):
                 multiply(u_acc[t][:, cols], codes, scales, dy_codes[n][:], dy_scales[n][:])
                 nc.scalar.copy(out=u[t][:, cols], in_=u_acc[t][:, cols])
 
-        for n in range(2):
-            weave_wo(nc.vector.tensor_copy, 0, n)
-            weave_wo(nc.scalar.copy, 1, n)
+        weave_wo(nc.vector.tensor_copy, 0)
+        weave_wo(nc.scalar.copy, 1)
         quantise_wo(0)
         weave_dy(nc.vector.tensor_copy, 0, 0, DY_ON_VECTOR)
         weave_dy(nc.scalar.copy, 0, DY_ON_VECTOR, HALF)
@@ -159,7 +157,7 @@ def tile_attend_ghsort_sig_kernel(tc, wo, dyT, W, h, offs, out):
         make_one_minus_h(factor[:, 2, 0:P], h_plane[2][:, 0:P])
         make_one_minus_h(factor[:, 3, :], h_plane[3])
 
-        w_bf = sbuf([P, S, PACK], BF16, "w_bf", 128, "wo_raw1")
+        w_bf = sbuf([P, S, PACK], BF16, "w_bf", 128, "wo_raw")
         w_codes = sbuf([P, S], U32, "w_codes")
         w_scales = sbuf([P, S], U8, "w_scales")
 
@@ -168,15 +166,15 @@ def tile_attend_ghsort_sig_kernel(tc, wo, dyT, W, h, offs, out):
             quantise(w_codes[:, cols], w_scales[:, cols], w_bf[:, cols, :].rearrange("p c j -> p (c j)"), E4M3)
 
         first_runs = sbuf([P, PACK, LAST], F32, "first_runs")
-        last_run = as_planes(w_stage[:, w_start + S :])
+        last_run = as_planes(second_stage[:, HALF : HALF + PACK * HALF])[:, :, P:HALF]
 
         def picked(planes, first, end):
-            return last_run[:, planes, first:end] if first >= LAST else first_runs[:, planes, first:end]
+            return last_run[:, planes, first - LAST : end - LAST] if first >= LAST else first_runs[:, planes, first:end]
 
         dz_bf = {
-            0: w_stage[:, 0:S].bitcast(BF16),
-            MIDDLE: w_raw[:, 1, 0:HALF].bitcast(BF16),
-            LAST: w_raw[:, 2, 0:HALF].bitcast(BF16),
+            0: first_stage[:, 0:S].bitcast(BF16),
+            MIDDLE: w_raw[0][:, 1, :].bitcast(BF16),
+            LAST: w_raw[0][:, 2, :].bitcast(BF16),
         }
         dz_codes = {first: sbuf([P, end - first], U32, "dz_codes%d" % first, 128 if first else 64) for first, end in RUNS}
         dz_scales = {first: sbuf([P, end - first], U8, "dz_scales%d" % first, 128 if first == LAST else 192) for first, end in RUNS}
@@ -211,7 +209,7 @@ def tile_attend_ghsort_sig_kernel(tc, wo, dyT, W, h, offs, out):
 
         results = {
             0: sbuf([P, PACK, MIDDLE], F32, "result_first")[:],
-            MIDDLE: as_planes(w_stage[:, w_start + 3 * S + HALF : w_start + 4 * S + HALF]),
+            MIDDLE: as_planes(second_stage[:, 3 * HALF + P :]),
             LAST: sbuf([P, PACK, P], F32, "result_last")[:],
         }
 
@@ -234,8 +232,9 @@ def tile_attend_ghsort_sig_kernel(tc, wo, dyT, W, h, offs, out):
         gather_on_scalar(P, MIDDLE, (2,))
         gather_on_scalar(0, MIDDLE, (1, 0))
         gather_on_scalar(MIDDLE, LAST, (2, 1, 0))
-        nc.vector.tensor_copy(*weave_views(w_bf[:, 0:W_ON_VECTOR, :], w_raw[:, :, 0:W_ON_VECTOR]))
-        nc.scalar.copy(*weave_views(w_bf[:, W_ON_VECTOR:S, :], w_raw[:, :, W_ON_VECTOR:S]))
+        for first, end in ((0, P), (P, HALF)):
+            nc.vector.tensor_copy(*weave_views(w_bf[:, first:end, :], w_raw[0][:, :, first:end]))
+        nc.scalar.copy(*weave_views(w_bf[:, HALF:S, :], w_raw[1]))
         gather_on_scalar(LAST, S, (2, 1, 0))
 
         weave_dz(0, MIDDLE)

@@ -153,8 +153,8 @@ def tile_attend_ghsort_sig_kernel(tc, wo, dyT, W, h, offs, out):
         make_u(1)
         make_neg_slope(factor[:, 0, :], h_plane[0])
         make_neg_slope(factor[:, 1, :], h_plane[1])
-        make_neg_slope(factor[:, 2, P:S], h_plane[2][:, P:S])
-        make_one_minus_h(factor[:, 2, 0:P], h_plane[2][:, 0:P])
+        make_neg_slope(factor[:, 2, MIDDLE:S], h_plane[2][:, MIDDLE:S])
+        make_one_minus_h(factor[:, 2, 0:MIDDLE], h_plane[2][:, 0:MIDDLE])
         make_one_minus_h(factor[:, 3, :], h_plane[3])
 
         w_bf = sbuf([P, S, PACK], BF16, "w_bf", 128, "wo_raw")
@@ -227,20 +227,21 @@ def tile_attend_ghsort_sig_kernel(tc, wo, dyT, W, h, offs, out):
             )
 
         gather_on_vector(0, LAST, 3)
-        gather_on_vector(0, P, 2)
+        gather_on_vector(0, MIDDLE, 2)
         gather_on_vector(LAST, S, 3)
-        gather_on_scalar(P, MIDDLE, (2,))
         gather_on_scalar(0, MIDDLE, (1, 0))
         gather_on_scalar(MIDDLE, LAST, (2, 1, 0))
         for first, end in ((0, P), (P, HALF)):
             nc.vector.tensor_copy(*weave_views(w_bf[:, first:end, :], w_raw[0][:, :, first:end]))
-        nc.scalar.copy(*weave_views(w_bf[:, HALF:S, :], w_raw[1]))
+        for first, end in ((P, HALF), (0, P)):
+            nc.scalar.copy(*weave_views(w_bf[:, HALF + first : HALF + end, :], w_raw[1][:, :, first:end]))
         gather_on_scalar(LAST, S, (2, 1, 0))
 
         weave_dz(0, MIDDLE)
         quantise_w(0)
         quantise_dz(0)
-        close(0, MIDDLE, (0, 1), "out0", nc.scalar.copy)
+        close(0, MIDDLE, (0,), "out0", nc.scalar.copy)
+        close(0, MIDDLE, (1,), "u_acc2", nc.scalar.copy)
         store(0, MIDDLE, (0, 1))
         weave_dz(MIDDLE, LAST)
         quantise_w(1)

@@ -153,8 +153,8 @@ def tile_attend_ghsort_sig_kernel(tc, wo, dyT, W, h, offs, out):
         make_u(1)
         make_neg_slope(factor[:, 0, :], h_plane[0])
         make_neg_slope(factor[:, 1, :], h_plane[1])
-        make_neg_slope(factor[:, 2, MIDDLE:S], h_plane[2][:, MIDDLE:S])
-        make_one_minus_h(factor[:, 2, 0:MIDDLE], h_plane[2][:, 0:MIDDLE])
+        make_neg_slope(factor[:, 2, P:S], h_plane[2][:, P:S])
+        make_one_minus_h(factor[:, 2, 0:P], h_plane[2][:, 0:P])
         make_one_minus_h(factor[:, 3, :], h_plane[3])
 
         w_bf = sbuf([P, S, PACK], BF16, "w_bf", 128, "wo_raw")
@@ -227,8 +227,9 @@ def tile_attend_ghsort_sig_kernel(tc, wo, dyT, W, h, offs, out):
             )
 
         gather_on_vector(0, LAST, 3)
-        gather_on_vector(0, MIDDLE, 2)
+        gather_on_vector(0, P, 2)
         gather_on_vector(LAST, S, 3)
+        gather_on_scalar(P, MIDDLE, (2,))
         gather_on_scalar(0, MIDDLE, (1, 0))
         gather_on_scalar(MIDDLE, LAST, (2, 1, 0))
         for first, end in ((0, P), (P, HALF)):

@@ -91,8 +91,10 @@ def tile_attend_ghsort_sig_kernel(tc, wo, dyT, W, h, offs, out):
 
         w_start = S - OVERLAP
         first_stage = sbuf([P, w_start + PACK * HALF], F32, "first_stage")
-        second_stage = sbuf([P, (PACK + 1) * HALF + P], F32, "second_stage")
-        w_raw = (as_planes(first_stage[:, w_start:]), as_planes(second_stage[:, 0 : PACK * HALF]))
+        row = HALF + OVERLAP
+        second_stage = sbuf([P, PACK * row - P + S], F32, "second_stage")
+        second_rows = as_planes(second_stage[:, 0 : PACK * row])
+        w_raw = (as_planes(first_stage[:, w_start:]), second_rows[:, :, 0:HALF])
         for n in range(2):
             nc.sync.dma_start(out=w_raw[n], in_=rows(W)[:, :, HALF * n : HALF * (n + 1)])
 
@@ -153,9 +155,9 @@ def tile_attend_ghsort_sig_kernel(tc, wo, dyT, W, h, offs, out):
         make_u(1)
         make_neg_slope(factor[:, 0, :], h_plane[0])
         make_neg_slope(factor[:, 1, :], h_plane[1])
-        make_neg_slope(factor[:, 2, P:S], h_plane[2][:, P:S])
-        make_one_minus_h(factor[:, 2, 0:P], h_plane[2][:, 0:P])
-        make_one_minus_h(factor[:, 3, :], h_plane[3])
+        for t in (2, 3):
+            make_neg_slope(factor[:, t, MIDDLE:S], h_plane[t][:, MIDDLE:S])
+            make_one_minus_h(factor[:, t, 0:MIDDLE], h_plane[t][:, 0:MIDDLE])
 
         w_bf = sbuf([P, S, PACK], BF16, "w_bf", 128, "wo_raw")
         w_codes = sbuf([P, S], U32, "w_codes")
@@ -166,7 +168,7 @@ def tile_attend_ghsort_sig_kernel(tc, wo, dyT, W, h, offs, out):
             quantise(w_codes[:, cols], w_scales[:, cols], w_bf[:, cols, :].rearrange("p c j -> p (c j)"), E4M3)
 
         first_runs = sbuf([P, PACK, LAST], F32, "first_runs")
-        last_run = as_planes(second_stage[:, HALF : HALF + PACK * HALF])[:, :, P:HALF]
+        last_run = second_rows[:, :, row - P : row]
 
         def picked(planes, first, end):
             return last_run[:, planes, first - LAST : end - LAST] if first >= LAST else first_runs[:, planes, first:end]
@@ -209,7 +211,7 @@ def tile_attend_ghsort_sig_kernel(tc, wo, dyT, W, h, offs, out):
 
         results = {
             0: sbuf([P, PACK, MIDDLE], F32, "result_first")[:],
-            MIDDLE: as_planes(second_stage[:, 3 * HALF + P :]),
+            MIDDLE: as_planes(second_stage[:, PACK * row - P :]),
             LAST: sbuf([P, PACK, P], F32, "result_last")[:],
         }
 
@@ -226,21 +228,20 @@ def tile_attend_ghsort_sig_kernel(tc, wo, dyT, W, h, offs, out):
                 out=block.rearrange("(q p) c -> p q c", p=P), in_=results[first][:, quarters[0] : quarters[-1] + 1, :]
             )
 
-        gather_on_vector(0, LAST, 3)
-        gather_on_vector(0, P, 2)
-        gather_on_vector(LAST, S, 3)
-        gather_on_scalar(P, MIDDLE, (2,))
-        gather_on_scalar(0, MIDDLE, (1, 0))
-        gather_on_scalar(MIDDLE, LAST, (2, 1, 0))
+        gather_on_vector(0, MIDDLE, 3)
+        gather_on_vector(0, MIDDLE, 2)
+        gather_on_scalar(0, MIDDLE, (0, 1))
+        gather_on_scalar(MIDDLE, LAST, (3, 2, 1, 0))
         for first, end in ((0, P), (P, HALF)):
             nc.vector.tensor_copy(*weave_views(w_bf[:, first:end, :], w_raw[0][:, :, first:end]))
-        for first, end in ((P, HALF), (0, P)):
+        for first, end in ((HALF - OVERLAP, HALF), (P, HALF - OVERLAP)):
             nc.scalar.copy(*weave_views(w_bf[:, HALF + first : HALF + end, :], w_raw[1][:, :, first:end]))
-        gather_on_scalar(LAST, S, (2, 1, 0))
+        gather_on_scalar(LAST, S, (3, 2, 1, 0))
 
         weave_dz(0, MIDDLE)
         quantise_w(0)
         quantise_dz(0)
+        nc.vector.tensor_copy(*weave_views(w_bf[:, HALF:LAST, :], w_raw[1][:, :, 0:P]))
         close(0, MIDDLE, (0,), "out0", nc.scalar.copy)
         close(0, MIDDLE, (1,), "u_acc2", nc.scalar.copy)
         store(0, MIDDLE, (0, 1))

import math
from contextlib import ExitStack

import concourse.mybir as mybir

S = 512
P = 128
PACK = 4
LIST_ROWS = 16
HALF = S // 2
FLOPS = 2 * 2 * S * S * S

F32 = mybir.dt.float32
BF16 = mybir.dt.bfloat16
U32 = mybir.dt.uint32
U16 = mybir.dt.uint16
U8 = mybir.dt.uint8
E4M3 = mybir.dt.float8_e4m3fn_x4
E5M2 = mybir.dt.float8_e5m2_x4
ALU = mybir.AluOpType
COPY = mybir.ActivationFunctionType.Copy

MIDDLE = HALF
LAST = HALF + P
RUNS = ((0, MIDDLE), (MIDDLE, LAST), (LAST, S))
PLANE_ORDER = (3, 2, 0, 1)
DY_ON_VECTOR = 168
OVERLAP = 64
BURST = 256
BYTES_OF = {F32: 4, U32: 4, BF16: 2, U8: 1}


def weave_views(dst, src):
    return dst.rearrange("p (c n) j -> p c j n", n=4), src.rearrange("p j (c n) -> p c j n", n=4)


def as_planes(flat):
    return flat.rearrange("p (j c) -> p j c", j=PACK)


def tile_attend_ghsort_sig_kernel(tc, wo, dyT, W, h, offs, out):
    nc = tc.nc
    with ExitStack() as ctx:
        keep = ctx.enter_context(tc.tile_pool(name="keep", bufs=1))
        work = ctx.enter_context(tc.tile_pool(name="work", bufs=1))
        psum = ctx.enter_context(tc.psum_pool(name="psum", bufs=1))
        starts = {}
        filled = [0]

        def sbuf(shape, dtype, name, phase=0, reuse=None):
            if reuse is None:
                start = -(-filled[0] // BURST) * BURST
                filled[0] = start + BURST + math.prod(shape[1:]) * BYTES_OF[dtype]
                starts[name] = start
            align = BURST if phase == 0 else 64
            return work.tile(shape, dtype, name=name, align_bytes=align, offset=starts[reuse or name] + phase)

        def quantise(codes, scales, woven, fmt):
            nc.vector.quantize_mx(out=codes.bitcast(fmt), scales=scales, in_=woven)

        def multiply(acc, e4m3_codes, e4m3_scales, e5m2_codes, e5m2_scales):
            nc.tensor.matmul_mx(
                out=acc,
                lhsT=e4m3_codes.bitcast(E4M3),
                lhsT_scale=e4m3_scales,
                rhs=e5m2_codes.bitcast(E5M2),
                rhs_scale=e5m2_scales,
                start=True,
                stop=True,
            )

        def rows(matrix):
            return matrix.rearrange("(p j) c -> p j c", j=PACK)

        wo_raw = sbuf([P, PACK, S], F32, "wo_raw")
        nc.sync.dma_start(out=wo_raw[:], in_=rows(wo))

        factor_start = BURST // 8
        arena = sbuf([P, factor_start + PACK * S], F32, "arena")
        factor = as_planes(arena[:, factor_start : factor_start + PACK * S])
        dy_raw = [sbuf([P, PACK, HALF], F32, "dy_raw%d" % n)[:] for n in range(2)]
        for n in range(2):
            nc.sync.dma_start(out=dy_raw[n], in_=rows(dyT)[:, :, HALF * n : HALF * (n + 1)])
        h_first = 3 * S - OVERLAP
        h_rest = sbuf([P, 3, S], F32, "h_rest")
        h_plane = (arena[:, h_first : h_first + S], h_rest[:, 0, :], h_rest[:, 1, :], h_rest[:, 2, :])
        offsets = keep.tile([P, S // LIST_ROWS], U16, name="offsets")
        for t in range(PACK):
            nc.sync.dma_start(out=h_plane[t], in_=rows(h)[:, t, :])
        nc.sync.dma_start(offsets[:], offs)

        w_start = S - OVERLAP
        first_stage = sbuf([P, w_start + PACK * HALF], F32, "first_stage")
        row = HALF + OVERLAP
        second_stage = sbuf([P, PACK * row - P + S], F32, "second_stage")
        second_rows = as_planes(second_stage[:, 0 : PACK * row])
        w_raw = (as_planes(first_stage[:, w_start:]), second_rows[:, :, 0:HALF])
        for n in range(2):
            nc.sync.dma_start(out=w_raw[n], in_=rows(W)[:, :, HALF * n : HALF * (n + 1)])

        def make_neg_slope(dst, part):
            nc.vector.scalar_tensor_tensor(out=dst, in0=part, scalar=1.0, in1=part, op0=ALU.subtract, op1=ALU.mult)

        def make_one_minus_h(dst, part):
            nc.vector.tensor_scalar(out=dst, in0=part, scalar1=-1.0, scalar2=1.0, op0=ALU.mult, op1=ALU.add)

        wo_codes = [sbuf([P, HALF], U32, "wo_codes0", 128), sbuf([P, HALF], U32, "wo_codes1", 192, "wo_raw")]
        wo_scales = [sbuf([P, HALF], U8, "wo_scales%d" % pair, 128 + 64 * pair) for pair in range(2)]
        first_woven = sbuf([P, 2 * S], BF16, "woven0", 192)
        woven = (first_woven[:], arena[:, factor_start + HALF : factor_start + HALF + S].bitcast(BF16))

        def weave_wo(copy, pair):
            dst = woven[pair].rearrange("p (t m j) -> p m j t", t=2, j=PACK)
            copy(dst, wo_raw[:].rearrange("p j (m t) -> p m j t", t=PACK)[:, :, :, 2 * pair : 2 * pair + 2])

        def quantise_wo(pair):
            quantise(wo_codes[pair][:], wo_scales[pair][:], woven[pair], E4M3)

        dy_codes = [sbuf([P, HALF], U32, "dy_codes%d" % n) for n in range(2)]
        dy_scales = [sbuf([P, HALF], U8, "dy_scales%d" % n, 64) for n in range(2)]

        def weave_dy(copy, n, first, end):
            dy_bf = woven[n].rearrange("p (c j) -> p c j", j=PACK)
            copy(*weave_views(dy_bf[:, first:end, :], dy_raw[n][:, :, first:end]))

        def quantise_dy(n, first, end):
            quantise(
                dy_codes[n][:, first:end], dy_scales[n][:, first:end], woven[n][:, PACK * first : PACK * end], E5M2
            )

        u_acc = [psum.tile([P, S], F32, name="u_acc%d" % t) for t in range(PACK)]
        u = [sbuf([P, S], F32, "u%d" % t, 128 + 64 * (t // 2)) for t in range(PACK)]

        def make_u(n):
            cols = slice(HALF * n, HALF * (n + 1))
            for t in PLANE_ORDER:
                words = slice(P * (t % 2), P * (t % 2 + 1))
                codes, scales = wo_codes[t // 2][:, words], wo_scales[t // 2][:, words]
                multiply(u_acc[t][:, cols], codes, scales, dy_codes[n][:], dy_scales[n][:])
                nc.scalar.copy(out=u[t][:, cols], in_=u_acc[t][:, cols])

        weave_wo(nc.vector.tensor_copy, 0)
        weave_wo(nc.scalar.copy, 1)
        quantise_wo(0)
        weave_dy(nc.vector.tensor_copy, 0, 0, DY_ON_VECTOR)
        weave_dy(nc.scalar.copy, 0, DY_ON_VECTOR, HALF)
        quantise_wo(1)
        quantise_dy(0, 0, HALF)
        weave_dy(nc.vector.tensor_copy, 1, 0, P)
        weave_dy(nc.vector.tensor_copy, 1, P, DY_ON_VECTOR)
        weave_dy(nc.scalar.copy, 1, DY_ON_VECTOR, HALF)
        make_u(0)
        quantise_dy(1, 0, P)
        quantise_dy(1, P, HALF)
        make_u(1)
        make_neg_slope(factor[:, 0, :], h_plane[0])
        make_neg_slope(factor[:, 1, :], h_plane[1])
        for t in (2, 3):
            make_neg_slope(factor[:, t, MIDDLE:S], h_plane[t][:, MIDDLE:S])
            make_one_minus_h(factor[:, t, 0:MIDDLE], h_plane[t][:, 0:MIDDLE])

        w_bf = sbuf([P, S, PACK], BF16, "w_bf", 128, "wo_raw")
        w_codes = sbuf([P, S], U32, "w_codes")
        w_scales = sbuf([P, S], U8, "w_scales")

        def quantise_w(n):
            cols = slice(HALF * n, HALF * (n + 1))
            quantise(w_codes[:, cols], w_scales[:, cols], w_bf[:, cols, :].rearrange("p c j -> p (c j)"), E4M3)

        first_runs = sbuf([P, PACK, LAST], F32, "first_runs")
        last_run = second_rows[:, :, row - P : row]

        def picked(planes, first, end):
            return last_run[:, planes, first - LAST : end - LAST] if first >= LAST else first_runs[:, planes, first:end]

        dz_bf = {
            0: first_stage[:, 0:S].bitcast(BF16),
            MIDDLE: w_raw[0][:, 1, :].bitcast(BF16),
            LAST: w_raw[0][:, 2, :].bitcast(BF16),
        }
        dz_codes = {first: sbuf([P, end - first], U32, "dz_codes%d" % first, 128 if first else 64) for first, end in RUNS}
        dz_scales = {first: sbuf([P, end - first], U8, "dz_scales%d" % first, 128 if first == LAST else 192) for first, end in RUNS}

        def gather_on_scalar(first, end, planes):
            for t in planes:
                nc.scalar.activation(
                    out=picked(t, first, end),
                    in_=u[t][:].indirect(offsets[:, first // LIST_ROWS : end // LIST_ROWS]),
                    func=COPY,
                    scale=-1.0,
                )

        def gather_on_vector(first, end, t):
            nc.vector.tensor_tensor(
                out=picked(t, first, end),
                in0=u[t][:].indirect(offsets[:, first // LIST_ROWS : end // LIST_ROWS]),
                in1=h_plane[t][:, first:end],
                op=ALU.mult,
            )

        def weave_dz(first, end):
            nc.vector.tensor_tensor(
                out=dz_bf[first].rearrange("p (c n j) -> p c j n", n=2, j=PACK),
                in0=picked(slice(0, PACK), first, end).rearrange("p j (c n) -> p c j n", n=2),
                in1=factor[:, :, first:end].rearrange("p j (c n) -> p c j n", n=2),
                op=ALU.mult,
            )

        def quantise_dz(first):
            quantise(dz_codes[first][:], dz_scales[first][:], dz_bf[first], E5M2)

        results = {
            0: sbuf([P, PACK, MIDDLE], F32, "result_first")[:],
            MIDDLE: as_planes(second_stage[:, PACK * row - P :]),
            LAST: sbuf([P, PACK, P], F32, "result_last")[:],
        }

        def close(first, end, quarters, bank, copy):
            acc = psum.tile([P, len(quarters), end - first], F32, name="acc%d_%d" % (first, quarters[0]), tag=bank)
            for k, q in enumerate(quarters):
                cols = slice(P * q, P * (q + 1))
                multiply(acc[:, k, :], w_codes[:, cols], w_scales[:, cols], dz_codes[first][:], dz_scales[first][:])
            copy(results[first][:, quarters[0] : quarters[-1] + 1, :], acc[:])

        def store(first, end, quarters):
            block = out[P * quarters[0] : P * (quarters[-1] + 1), first:end]
            nc.sync.dma_start(
                out=block.rearrange("(q p) c -> p q c", p=P), in_=results[first][:, quarters[0] : quarters[-1] + 1, :]
            )

        gather_on_vector(0, MIDDLE, 3)
        gather_on_vector(0, MIDDLE, 2)
        gather_on_scalar(0, MIDDLE, (0, 1))
        gather_on_scalar(MIDDLE, LAST, (3, 2, 1, 0))
        for first, end in ((0, P), (P, HALF)):
            nc.vector.tensor_copy(*weave_views(w_bf[:, first:end, :], w_raw[0][:, :, first:end]))
        for first, end in ((HALF - OVERLAP, HALF), (P, HALF - OVERLAP)):
            nc.scalar.copy(*weave_views(w_bf[:, HALF + first : HALF + end, :], w_raw[1][:, :, first:end]))
        gather_on_scalar(LAST, S, (3, 2, 1, 0))

        weave_dz(0, MIDDLE)
        quantise_w(0)
        quantise_dz(0)
        nc.vector.tensor_copy(*weave_views(w_bf[:, HALF:LAST, :], w_raw[1][:, :, 0:P]))
        close(0, MIDDLE, (0,), "out0", nc.scalar.copy)
        close(0, MIDDLE, (1,), "u_acc2", nc.scalar.copy)
        store(0, MIDDLE, (0, 1))
        weave_dz(MIDDLE, LAST)
        quantise_w(1)
        quantise_dz(MIDDLE)
        close(0, MIDDLE, (2,), "out1", nc.scalar.copy)
        store(0, MIDDLE, (2,))
        close(0, MIDDLE, (3,), "u_acc3", nc.scalar.copy)
        store(0, MIDDLE, (3,))
        weave_dz(LAST, S)
        quantise_dz(LAST)
        close(MIDDLE, LAST, (0, 1), "out2", nc.vector.tensor_copy)
        close(MIDDLE, LAST, (2, 3), "out3", nc.scalar.copy)
        store(MIDDLE, LAST, (0, 1, 2, 3))
        close(LAST, S, (0,), "u_acc0", nc.scalar.copy)
        close(LAST, S, (1,), "u_acc1", nc.vector.tensor_copy)
        store(LAST, S, (0, 1))
        close(LAST, S, (2,), "out0", nc.scalar.copy)
        close(LAST, S, (3,), "out1", nc.vector.tensor_copy)
        store(LAST, S, (2, 3))
